import numpy as np, ml_dtypes
CORES = [16,18,20,22]
N = 4
BF = ml_dtypes.bfloat16
W, V, Q, S, RO = 4096, 256, 2, 1, 4
RK = np.arange(N)[:, None, None]; GR = np.arange(8)[None, :, None]; VE = np.arange(V)[None, None, :]
def unfold(a, m):
    return np.ascontiguousarray(a.reshape(N, 8, 16, m).transpose(0, 1, 3, 2))
def fold(a):
    return np.ascontiguousarray(a.transpose(0, 1, 3, 2)).reshape(N, 128, -1)
def pack(T, U, P, x):
    return {"tx": fold(T).astype(np.float32).astype(BF), "pu": fold(U).astype(np.int32), "p0": fold(P).astype(np.int32), "x0": fold(x).astype(np.float32).astype(BF)}
def pair(rng, P):
    m = rng.integers(0, 17, (N, 8, V // 2, 1))
    P[:, :, 1::2] = np.where(np.arange(16) < m, P[:, :, 0::2], P[:, :, 1::2])
    return P
def parts(rng):
    T = rng.integers(0, 128, (N, 8, W, 16)); U = rng.integers(0, W, (N, 8, W, 16))
    U = np.where(rng.random((N, 8, W, 1)) < 0.25, U[..., :1], U)
    P = rng.integers(0, W, (N, 8, V, 16))
    for k in range(1, 16):
        nxt = U[RK, GR, P[..., k - 1], rng.integers(0, 16, (N, 8, V))]
        P[..., k] = np.where(rng.random((N, 8, V)) < 0.5, nxt, P[..., k])
    P = pair(rng, P)
    near = np.clip(T[RK, GR, P[..., 15]] + rng.integers(-20, 21, (N, 8, V, 16)), 0, 127)
    x = np.where(rng.random((N, 8, V, 1)) < 0.5, near, rng.integers(0, 128, (N, 8, V, 16)))
    return T, U, P, x
def setup_inputs(rng):
    return pack(*parts(rng))
def setup_inputs_ties(rng):
    T, U, P, x = parts(rng)
    few = rng.integers(0, 128, (N, 8, 6, 16)); few[:, :, 0] = 0; few[:, :, 1] = 127
    T = few[RK, GR, rng.integers(0, 6, (N, 8, W))]; x = few[RK, GR, rng.integers(0, 6, (N, 8, V))]
    return pack(T, U, P, x)
def setup_inputs_cuts(rng):
    T, U, P, x = parts(rng); h = W // 2; s = V // 4
    for g in range(8):
        o = rng.permutation(W); P[:, g] = o[h + P[:, g] % h]
        for j in range(s):
            m = (1, Q - 1, Q, N)[j if j < 4 else int(rng.integers(0, 4))]
            nm = o[s + np.arange(N)]; nm[rng.permutation(N)[:m]] = o[j]
            P[:, g, 2 * j + 1] = P[:, g, 2 * j]; P[:, g, 2 * j:2 * j + 2, 15] = nm[:, None]
    return pack(T, U, P, x)
def setup_inputs_crowd(rng):
    T, U, P, x = parts(rng); h = V // 2; r = np.arange(N)[:, None]; j = np.arange(h)[None, :]
    for g in (0, 1, 2, 3, 4, 5, 7):
        o = rng.permutation(W); nm = np.repeat(o[1:N + 1, None], V, axis=1); n = N + 1
        if g in (0, 7):
            if g == 7: o = np.concatenate([np.array([W - 1]), rng.permutation(W - 1)])
            nm = np.stack([rng.permutation(o[i * V:(i + 1) * V]) for i in np.minimum(rng.permutation(N) // Q, N // Q - 1)]); n = (N // Q) * V
        elif g in (1, 4):
            o = 1 + rng.permutation(W - 1); n = ((N - 1) // (Q - 1) + 1) * h
            nm = o[(rng.permutation(N) // (Q - 1))[:, None] * h + np.arange(V)[None, :] // 2]
        elif g == 2: nm[rng.permutation(N)[:Q]] = o[0]
        elif g == 5:
            s = int(rng.integers(0, N - Q + 1)); nm[s:s + Q - 1, :192] = o[0]; nm = nm[:, rng.permutation(V)]
        else: o = np.arange(W)[::-1]; n = 512
        a, b = o[:n], o[n:]
        T[:, g] = T[:, g] >> 2; x[:, g] = x[:, g] >> 2; T[:, g, a] = T[:, g, a] + 96
        P[:, g] = b[P[:, g] % len(b)]; U[:, g] = b[U[:, g] % len(b)]; P[:, g, 1::2] = np.array(P[:, g, 0::2])
        if g == 3:
            m = rng.integers(1, 15, (N, h)); c = W - 512 + 4 * rng.integers(0, 128, (N, h))
            P[r, g, 2 * j, m] = c; P[r, g, 2 * j + 1, m] = c + 1
        else: P[:, g, :, 15] = nm
        if g in (0, 7): P[:, g, :, 14] = np.array(P[:1, g, :, 14]); U[:, g] = np.array(U[:1, g, :, :1])
    return pack(T, U, P, x)
def setup_inputs_few(rng):
    T, U, P, x = parts(rng)
    for g in (0, 2, 4, 6):
        a = np.concatenate([np.array([0, W - 1]), rng.integers(0, W, 10)]); P[:, g] = a[P[:, g] % 12]
        if g in (0, 4): U[:, g] = a[U[:, g] % 12]
    P[:, 2] = np.array(P[:, 2, :, :1]); U[:, 4, ::2] = rng.integers(0, W, (N, W // 2, 16)); U[:, 6] = np.arange(W)[:, None]
    return pack(T, U, P, x)
def setup_inputs_spread(rng):
    T = np.minimum((np.exp2(7 * rng.random((N, 8, W, 1))) * rng.random((N, 8, W, 16))).astype(np.int64), 127)
    x = np.minimum((np.exp2(7 * rng.random((N, 8, V, 1))) * rng.random((N, 8, V, 16))).astype(np.int64), 127)
    U = np.minimum((W * rng.random((N, 8, W, 16)) ** 2).astype(np.int64), W - 1)
    P = np.minimum((W * rng.random((N, 8, V, 16)) ** 3).astype(np.int64), W - 1)
    return pack(T, U, pair(rng, P), x)
def check_inputs(d):
    bad = []
    for k, hi in (("tx", 127), ("pu", W - 1), ("p0", W - 1), ("x0", 127)):
        a = np.asarray(d[k]).astype(np.float64)
        if not (np.all(a >= 0) and np.all(a <= hi)): bad.append("range of " + k)
        elif np.any(np.floor(a) != a): bad.append("whole numbers of " + k)
    return bad
def reference(tx, pu, p0, x0):
    T = unfold(tx.astype(np.float32).astype(np.int32), W); U = unfold(pu.astype(np.int64), W)
    P = unfold(p0.astype(np.int64), V); x = unfold(x0.astype(np.float32).astype(np.int32), V)
    row = np.arange(16); cut = np.zeros((8, W), bool); R4 = RK[..., None]; G4 = GR[..., None]
    for rnd in range(RO):
        d = np.add.reduce(np.abs(T[R4, G4, P] - x[:, :, :, None, :]), axis=4)
        differ = P != P[:, :, np.arange(V) ^ 1]
        q = np.where(np.any(differ, axis=3), np.argmax(differ, axis=3), 15)
        f = np.argmax(np.where(row >= np.maximum(q, 1)[..., None], d, -1), axis=3)
        old = cut[G4, P] & (row >= 1)
        k = np.where(np.any(old, axis=3), np.argmax(old, axis=3), f)
        charged = np.zeros((N, 8, W), bool); charged[RK, GR, P[RK, GR, VE, f]] = True
        cut = cut | (np.add.reduce(charged.astype(np.int64), axis=0) >= Q)
        T[:, cut] = 256
        pup = U[RK, GR, P[RK, GR, VE, k - 1]]
        e = np.add.reduce(np.abs(T[R4, G4, pup] - x[:, :, :, None, :]), axis=4)
        b = np.argmin(e, axis=3); best = pup[RK, GR, VE, b]
        take = e[RK, GR, VE, b] < d[RK, GR, VE, k]
        P[RK, GR, VE, k] = np.where(take, best, P[RK, GR, VE, k])
        x = np.where(take[..., None], (x + T[RK, GR, best]) >> 1, x)
        if rnd + 1 < RO: P = np.roll(P, S, axis=0); x = np.roll(x, S, axis=0)
    return {"yp": fold(P).astype(np.float32), "yx": fold(x).astype(np.float32).astype(BF), "yc": np.repeat(cut[None], N, axis=0).astype(np.float32)}

@@ -1,0 +1,435 @@
+from concourse.bass import DstId, RemoteDMATransfer
+from concourse.mybir import AluOpType, ActivationFunctionType
+
+R = 4
+BIG = 16384.0
+TOP = 8388608
+
+SCRATCH = {}
+SHAPES = {
+    "bfloat16": "TX 4096 X0 256 D 4112 AB 4096 OA 2048 OX 1024 OB 4096 LS 2048 LX 2048 IDM 128 IDN 128 IDB 128 IDT 128 GR 768 IOM 128 IM 128 "
+                "IOB 256 CKC 256 CKE 256 NEG 256 ONE 8 NE 128 TCH 256 FB 32 XN 256 GX 256 YX 256",
+    "int32": "PUW 4096 P0 256 I1 16 I2 16 I3 16 I5 16 PERMI 16 REPI 16 VS 16 GI 16 HI 16 FI 32 FM 32 KS 16 TH 16 EI 32 EM 32 ET 16 LT 16 "
+             "JJ 16 PO 16 TO 16 TF 16 OLD 16",
+    "uint16": "PERM 16 PERM2 32 REP 16 TL 32 CU 256 POU 16",
+    "float32": "MKI 512 MK 512 CL 256 COLS 16 COLP 16 COLH 16 SW 512 SWT 512 AA 256 RA 256 RB 256 SK 256 KT 256 OH 256 PR 128 "
+               "CF 256 CB 256 N1 16 BN 16 DL 16 DT 16 UP 256 YP 256 YC 256",
+}
+for _d, _l in SHAPES.items():
+    _w = _l.split()
+    for _n, _c in zip(_w[::2], _w[1::2]):
+        SCRATCH[_n] = ("sbuf", [128, int(_c)], _d)
+for _n in ("pcr", "pcnt", "pchg", "pcut", "pd0", "pd1", "pd2", "pd3"):
+    SCRATCH[_n] = ("psum", [128, 512], "float32")
+for _r in range(R):
+    SCRATCH["TR%d" % _r] = ("sbuf", [128, 256], "bfloat16")
+    SCRATCH["TS%d" % _r] = ("sbuf", [128, 256], "bfloat16")
+    SCRATCH["XR%d" % _r] = ("sbuf", [128, 1024], "bfloat16")
+    SCRATCH["PU%d" % _r] = ("sbuf", [128, 256], "uint16")
+    SCRATCH["M%d" % _r] = ("sbuf", [128, 1008], "float32")
+    SCRATCH["XS%d" % _r] = ("sbuf", [128, 256], "bfloat16")
+    SCRATCH["PS%d" % _r] = ("sbuf", [128, 256], "uint16")
+    SCRATCH["MS%d" % _r] = ("sbuf", [128, 1008], "float32")
+SCRATCH["FS"] = ("sbuf", [128, 256 * R], "bfloat16")
+SCRATCH["FR"] = ("sbuf", [128, 768 * R], "bfloat16")
+SCRATCH["T0"] = ("sbuf", [128, 256 * R + 256], "bfloat16")
+
+SEMAPHORES = ["qv", "qs", "qt", "qg", "ls", "dx0", "dp0", "dtx", "dpu", "dt0", "dyp", "dyx", "dyc"]
+SEMAPHORES += ["%s%d" % (a, r) for a in ("a1", "a2", "a3", "fl", "dc") for r in range(R)]
+
+
+def rank_program(g, core, T, topo):
+    rank = T.rank_of(core)
+    if rank is None:
+        return
+    OP = AluOpType
+    AF = ActivationFunctionType
+    eng = {"v": g.vector, "s": g.scalar, "t": g.tensor, "g": g, "y": g.sync}
+    cnt = {"v": 0, "s": 0, "t": 0, "g": 0}
+    known = {e: {} for e in eng}
+    acc = {}
+
+    def B(name, lo=0, hi=None, step=1):
+        if hi is None:
+            hi = SCRATCH[name][1][1]
+        ap = T[name][:, lo:hi] if step == 1 else T[name][:, lo:hi:step]
+        return (name, lo, hi, ap)
+
+    def psum(name):
+        return SCRATCH[name][0] == "psum"
+
+    def need(e, reads, writes):
+        deps = {}
+        for w, specs in ((False, reads), (True, writes)):
+            for name, lo, hi, _ in specs:
+                for plo, phi, pw, pe, tok in acc.get(name, ()):
+                    if pe == e:
+                        hit = e != "t" and pw != w and lo < phi and plo < hi
+                    elif psum(name):
+                        hit = True
+                    else:
+                        hit = (pw or w) and lo < phi and plo < hi
+                    if hit and deps.get(tok[0], 0) < tok[1]:
+                        deps[tok[0]] = tok[1]
+        for sem in sorted(deps):
+            if known[e].get(sem, 0) < deps[sem]:
+                eng[e].wait_ge(T.sem[sem], deps[sem])
+                known[e][sem] = deps[sem]
+
+    def mark(pe, tok, reads, writes):
+        for name, lo, hi, _ in writes:
+            old = [a for a in acc.get(name, ()) if not (lo <= a[0] and a[1] <= hi)]
+            acc[name] = old + [(lo, hi, True, pe, tok)]
+        for name, lo, hi, _ in reads:
+            old = [a for a in acc.get(name, ()) if not (a[3] == pe and not a[2] and lo <= a[0] and a[1] <= hi)]
+            acc[name] = old + [(lo, hi, False, pe, tok)]
+
+    def op(e, reads, writes, fn):
+        need(e, reads, writes)
+        fn().then_inc(T.sem["q" + e], 1)
+        cnt[e] += 1
+        mark(e, ("q" + e, cnt[e]), reads, writes)
+
+    def dma(e, sem, out, in_, reads, writes):
+        need(e, reads, writes)
+        eng[e].dma_start(out, in_).then_inc(T.sem[sem], 16)
+        mark("d" + sem, (sem, 16), reads, writes)
+
+    def tt(out, a, b, o):
+        op("v", [a, b], [out], lambda: g.vector.tensor_tensor(out[3], a[3], b[3], o))
+
+    def ts(out, a, s1, o1, s2=None, o2=None):
+        reads = [a] + [s for s in (s1,) if isinstance(s, tuple)]
+        x = s1[3] if isinstance(s1, tuple) else s1
+        if o2 is None:
+            op("v", reads, [out], lambda: g.vector.tensor_scalar(out[3], a[3], x, None, o1))
+        else:
+            op("v", reads, [out], lambda: g.vector.tensor_scalar(out[3], a[3], x, s2, o1, o2))
+
+    def cp(out, a):
+        op("v", [a], [out], lambda: g.vector.tensor_copy(out[3], a[3]))
+
+    def gat(out, win, lst, b, o):
+        if b is None:
+            op("v", [win, lst], [out], lambda: g.vector.tensor_copy(out[3], win[3].indirect(lst[3])))
+        else:
+            op("v", [win, lst, b], [out], lambda: g.vector.tensor_tensor(out[3], win[3].indirect(lst[3]), b[3], o))
+
+    def fill(out, value):
+        op("v", [], [out], lambda: g.vector.memset(out[3], value))
+
+    def act(out, a, f, scale=1.0, bias=0.0):
+        col = isinstance(bias, tuple)
+        x = bias[3] if col else bias
+        op("s", [a, bias] if col else [a], [out], lambda: g.scalar.activation(out[3], a[3], f, bias=x, scale=scale))
+
+    def sgat(out, win, lst):
+        op("s", [win, lst], [out], lambda: g.scalar.activation(out[3], win[3].indirect(lst[3]), AF.Copy))
+
+    def mm(out, lhsT, rhs, start, stop):
+        op("t", [lhsT, rhs], [out], lambda: g.tensor.matmul(out[3], lhsT[3], rhs[3], start, stop))
+
+    def iota(name, pattern, base, cm):
+        out = B(name)
+        if SCRATCH[name][2] == "int32":
+            op("g", [], [out], lambda: g.iota(out[3], pattern, base, cm))
+        else:
+            op("g", [], [out], lambda: g.iota(out[3], pattern, base, cm, allow_small_or_imprecise_dtypes=True))
+
+    def tree(out, a, b, o):
+        tt(B("KT", 0, 128), a, b, o)
+        tt(B("KT", 128, 192), B("KT", 0, 64), B("KT", 64, 128), o)
+        tt(B("KT", 192, 224), B("KT", 128, 160), B("KT", 160, 192), o)
+        tt(out, B("KT", 192, 208), B("KT", 208, 224), o)
+
+    def swap_in(win, lst):
+        gat(B("SW"), win, lst, B("MK"), OP.mult)
+        op("v", [B("SW")], [B("SWT")], lambda: g.vector.transpose(T.SWT[:, :], T.SW[:, :]))
+
+    def swap_out(name):
+        for t in range(16):
+            tt(B(name, 16 * t, 16 * t + 16), B("SWT", t, 512, 32), B("SWT", 16 + t, 512, 32), OP.add)
+
+    def high(src, ta):
+        act(ta, src, AF.Identity, scale=1.0 / 256.0, bias=159.502)
+
+    def minus257(ta):
+        act(B("pcr", 256, 512), ta, AF.Identity, scale=-257.0, bias=257.0 * 160.0)
+
+    def prep(m, ta):
+        tt(B("NE"), B(m, 0, 256, 2), B(m, 1, 256, 2), OP.not_equal)
+        high(B(m, 0, 256), B(ta))
+        minus257(B(ta))
+        act(B("pcr", 0, 240), B(m, 0, 240), AF.Copy, scale=4096.0)
+        for k in range(16):
+            mm(B("pcut", 8 * k, 128), B("IDT"), B("NE", 0, 128 - 8 * k), k == 0, False)
+        mm(B("pcut", 120, 128), B("IDT"), B("ONE"), False, True)
+
+    def prep2(m):
+        tt(B(m, 512, 768), B(m, 0, 256), B("pcr", 256, 512), OP.add)
+        for p in (0, 1):
+            tt(B(m, 256 + p, 512, 2), B("pcut", 0, 128), B("CL", p, 256, 2), OP.min)
+        tt(B(m, 768, 1008), B("pcr", 0, 240), B(m, 16, 256), OP.add)
+
+    def distances(lst, xr, ck, ta, raw, chunks, later, keep):
+        sgat(B("GR"), B("TX"), B(lst, 16 * raw, 16 * raw + 48))
+        two, one = B("pcnt", 0, 512), B("pchg", 0, 256)
+        mm(two, B("IDM"), B("GR", 0, 512), True, False)
+        mm(B("pcnt", 0, 256), B("IDN"), B(xr, 0, 256), False, False)
+        mm(B("pcnt", 256, 512), B("IDN"), B(xr, 0, 256), False, True)
+        mm(one, B("IDM"), B("GR", 512, 768), True, False)
+        mm(one, B("IDN"), B(xr, 0, 256), False, True)
+        wait = []
+        for q, calls in enumerate(chunks):
+            for ka, kb in calls:
+                gat(B("D", 16 + 256 * ka, 16 + 256 * kb), B("TX"), B(lst, 16 * ka, 16 * kb), B(xr, 0, 256 * (kb - ka)), OP.subtract)
+            ka, kb = calls[0][0], calls[-1][1]
+            for ja, jb in ([(ka, kb)] if q < 3 else [(ka, kb - 1), (kb - 1, kb)]):
+                act(B("AB", 256 * ja, 256 * jb), B("D", 16 + 256 * ja, 16 + 256 * jb), AF.Abs)
+            if q == 0:
+                act(B("AB", 256 * raw, 256 * raw + 512), two, AF.Abs)
+                act(B("AB", 256 * raw + 512, 256 * raw + 768), one, AF.Abs)
+                ka = raw
+            if q == 1:
+                later()
+            ps = B("pd%d" % q, 0, 16 * (kb - ka))
+            mm(ps, B("IDM"), B(ck, 16 * ka, 16 * kb), True, False)
+            for s in range(16):
+                mm(ps, B("LS", 128 * s, 128 * s + 128), B("AB", 256 * ka + s, 256 * kb, 16), False, False)
+            wait.append((ps, B(ta, 16 * ka, 16 * kb)))
+            while q > 0 and wait:
+                ps, dig = wait.pop(0)
+                mm(ps, B("IDM"), dig, False, True)
+        if keep:
+            act(B("D", 16 + 256 * raw, 16 + 256 * raw + 512), two, AF.Copy)
+            act(B("D", 16 + 256 * raw + 512, 16 + 256 * raw + 768), one, AF.Copy)
+
+    dma("y", "dp0", T.P0[:, :], T.p0[:, :], [], [B("P0")])
+    dma("y", "dx0", T.X0[:, :], T.x0[:, :], [], [B("X0")])
+    dma("y", "dtx", T.TX[:, :], T.tx[:, :], [], [B("TX")])
+    dma("y", "dt0", T.T0[:, 0:256], T.tx[0:128:16, :], [], [B("T0", 0, 256)])
+    g.sync.wait_ge(T.sem.dtx, 16)
+    dma("y", "dpu", T.PUW[:, :], T.pu[:, :], [], [B("PUW")])
+
+    iota("I1", [[1, 16]], 0, 16)
+    iota("I2", [[0, 16]], 0, 1)
+    iota("MKI", [[0, 16], [1, 2], [0, 16]], 0, 0)
+    iota("IOM", [[1, 128]], 0, 0)
+    iota("I5", [[1, 16]], 0, 0)
+    iota("I3", [[16, 16]], 16, 0)
+    iota("CL", [[-256, 16], [0, 16]], TOP + 4096 + 255, 0)
+    iota("CKC", [[-256, 16], [0, 16]], 4096 - 160, 0)
+    iota("IOB", [[1, 256]], 0, 0)
+    iota("CKE", [[256, 16], [0, 16]], -160, 0)
+    fill(B("ONE"), 1.0)
+    fill(B("NEG"), -1.0)
+    fill(B("D", 0, 16), 0.0)
+    fill(B("AA", 0, 16), 0.0)
+    fill(B("PR", 0, 16), 0.0)
+    fill(B("SK", 0, 16), 0.0)
+    ts(B("PERMI"), B("I1"), 255, OP.bitwise_and)
+    ts(B("HI"), B("I2"), 16, OP.bitwise_and, 4, OP.logical_shift_right)
+    ts(B("REPI"), B("I2"), 15, OP.bitwise_and)
+    ts(B("GI"), B("I2"), 112, OP.bitwise_and)
+    cp(B("PERM"), B("PERMI"))
+    cp(B("PERM2", 0, 32, 2), B("PERMI"))
+    cp(B("PERM2", 1, 32, 2), B("PERMI"))
+    cp(B("COLH"), B("HI"))
+    cp(B("COLP"), B("I2"))
+    cp(B("REP"), B("REPI"))
+    ts(B("MK"), B("MKI"), B("COLH", 0, 1), OP.is_equal)
+    tt(B("COLS"), B("GI"), B("I5"), OP.add)
+    tt(B("VS"), B("REPI"), B("I3"), OP.add)
+    ts(B("IDM"), B("IOM"), B("COLP", 0, 1), OP.is_equal)
+    ts(B("IDN"), B("IOM"), B("COLP", 0, 1), OP.is_equal, -1.0, OP.mult)
+    for s in range(16):
+        act(B("LX", 128 * s, 128 * s + 128), B("IOM"), AF.Abs, scale=-1.0, bias=B("COLS", s, s + 1))
+    act(B("LS"), B("LX"), AF.Relu, scale=-4096.0, bias=4096.0)
+    swap_in(B("P0"), B("PERM2"))
+    swap_out("M0")
+    cp(B("PU0"), B("M0", 0, 256))
+    gat(B("XR0", 0, 256), B("X0"), B("PERM"), None, None)
+    ts(B("IDT"), B("IOM"), B("COLP", 0, 1), OP.is_equal, 16777216.0, OP.mult)
+    ts(B("IDB"), B("IOM"), B("COLP", 0, 1), OP.is_equal, BIG, OP.mult)
+    ts(B("IM"), B("IOM"), B("COLS", 0, 1), OP.subtract)
+    fill(B("CL", 0, 16), 0.0)
+
+    others = [q for q in range(R) if q != rank]
+    nxt, prv = T.cores[(rank + 1) % R], T.cores[(rank - 1) % R]
+    rows = [(1, 5), (5, 9), (9, 13), (13, 16)]
+    singles = [[(k, k + 1) for k in range(max(a, 4), b)] for a, b in rows]
+    sent = 0
+    for r in range(R):
+        xr, pu, m, last = "XR%d" % r, "PU%d" % r, "M%d" % r, r == R - 1
+        told, tnew = B("T0", 256 * r, 256 * r + 256), B("T0", 256 * r + 256, 256 * r + 512)
+        fs = B("FS", 256 * r, 256 * r + 256)
+
+        def chain_arrays():
+            if r == 0:
+                prep(m, "TR0")
+
+        distances(pu, xr, "CKC", "TR%d" % r, 1, singles, chain_arrays, False)
+        act(B(xr, 256, 512), B(xr, 0, 256), AF.Copy)
+        act(B(xr, 512, 1024), B(xr, 0, 512), AF.Copy)
+        if r == 0:
+            prep2(m)
+        act(B("pcr", 0, 240), B(m, 768, 1008), AF.Copy)
+
+        def key_a(q):
+            ka, kb = 16 * rows[q][0], 16 * rows[q][1]
+            tt(B("AA", ka, kb), B("pd%d" % q, 0, kb - ka), B(m, 256 + ka, 256 + kb), OP.min)
+
+        def key_b(q):
+            ka, kb = 16 * rows[q][0], 16 * rows[q][1]
+            tt(B("RB", 0, 64) if q == 0 else B("pcut", 64 * q, 64 * q + kb - ka), B("AA", ka, kb), B(m, 512 + ka, 512 + kb), OP.add)
+
+        key_a(0)
+        key_a(1)
+        key_b(0)
+        tt(B("pcut", 256, 320), B("AA", 16, 80), B("AA", 80, 144), OP.max)
+        key_a(2)
+        key_b(1)
+        tt(B("RA", 64, 128), B("pcut", 256, 320), B("AA", 144, 208), OP.max)
+        tt(B("RB", 128, 192), B("RB", 0, 64), B("pcut", 64, 128), OP.max)
+        key_b(2)
+        key_a(3)
+        tt(B("RB", 64, 128), B("RB", 128, 192), B("pcut", 128, 192), OP.max)
+        key_b(3)
+        tt(B("RA", 64, 112), B("RA", 64, 112), B("AA", 208, 256), OP.max)
+        tt(B("RB", 64, 112), B("RB", 64, 112), B("pcut", 192, 240), OP.max)
+        for run in ("RA", "RB"):
+            tt(B(run, 192, 224), B(run, 64, 96), B(run, 96, 128), OP.max)
+        for j, run in enumerate(("RA", "RB")):
+            tt(B("FI", 16 * j, 16 * j + 16), B(run, 192, 208), B(run, 208, 224), OP.max)
+        ts(B("FM"), B("FI"), 255, OP.bitwise_and)
+        cp(B("FB"), B("FM"))
+        for c in range(16):
+            if c < 8:
+                ts(B("OA", 128 * c, 128 * c + 128), B("IM"), B("FB", c, c + 1), OP.is_equal)
+            else:
+                j = c - 8
+                act(B("OX", 128 * j, 128 * j + 128), B("IM"), AF.Abs, scale=-1.0, bias=B("FB", c, c + 1))
+                if c % 4 == 3:
+                    act(B("OA", 128 * c - 384, 128 * c + 128), B("OX", 128 * j - 384, 128 * j + 128), AF.Relu, scale=-1.0, bias=1.0)
+            ts(B("OB", 256 * c, 256 * c + 256), B("IOB"), B("FB", 16 + c, 17 + c), OP.is_equal)
+        for c in range(16):
+            mm(B("pchg", 0, 256), B("OA", 128 * c, 128 * c + 128), B("OB", 256 * c, 256 * c + 256), c == 0, c == 15)
+        mm(B("pcut", 0, 256), B("IDM"), told, True, False)
+        mm(B("pcut", 0, 256), B("IDB"), B("NEG"), False, False)
+        if r > 0:
+            for q, (ka, kb) in enumerate(rows):
+                act(B("pcnt", 16 * ka, 16 * kb), B("pd%d" % q, 0, 16 * (kb - ka)), AF.Relu, bias=-16777216.0)
+        act(fs, B("pchg", 0, 256), AF.Sign)
+        mm(B("pcut", 0, 256), B("IDB"), fs, False, False)
+        need("g", [fs], [])
+        dsts, ids = [], []
+        for q in others:
+            j = 3 * r + (rank - q - 1) % R
+            rid, pid = topo.addr(T.cores[q])[:2]
+            ids.append(DstId(rid=rid, pnc=pid))
+            dsts.append(T.FR[:, 256 * j:256 * j + 256])
+        g.remote_dma_fused([RemoteDMATransfer(dst_ids=ids, dma_engine_mask=topo.mask(core, T.cores[others[0]]), remote_sem=T.sem["fl%d" % r],
+                                              srcs=[fs[3]], dsts=dsts)], local_sem=T.sem.ls)
+        sent += len(topo.engines(core, T.cores[others[0]]))
+        mark("rem", ("fl%d" % r, sum(len(topo.engines(T.cores[q], core)) for q in others)), [], [B("FR", 768 * r, 768 * r + 768)])
+        for j in range(3 * r, 3 * r + 3):
+            mm(B("pcut", 0, 256), B("IDB"), B("FR", 256 * j, 256 * j + 256), False, j == 3 * r + 2)
+        ks, sk = ("FI", "AA")
+        if r > 0:
+            ks, sk = ("KS", "SK")
+            tt(B("pcnt", 272, 512), B("pcnt", 16, 256), B("CL", 16, 256), OP.min)
+            tt(B("SK", 16, 256), B("pcnt", 272, 512), B("AA", 16, 256), OP.max)
+            tree(B("KS", 0, 16), B("SK", 0, 128), B("SK", 128, 256), OP.max)
+        gat(B("OH"), B(ks, 0, 16), B("REP"), B(sk), OP.is_equal)
+        tt(B("PR", 16, 128), B("OH", 16, 128), B("pcr", 0, 112), OP.mult)
+        tt(B("pchg", 0, 128), B("OH", 128, 256), B("pcr", 112, 240), OP.mult)
+        tree(B("TO"), B("PR"), B("pchg", 0, 128), OP.add)
+        ts(B("TF"), B("TO"), 12, OP.logical_shift_right)
+        cp(B("TL", 0, 32, 2), B("TF"))
+        cp(B("TL", 1, 32, 2), B("TF"))
+        swap_in(B("PUW"), B("TL"))
+        tt(tnew, B("pcut", 0, 256), told, OP.max)
+        dma("y", "dc%d" % r, T.TX[0:128:16, 0:4096], tnew[3], [tnew], [B("TX")])
+        swap_out("CF")
+        cp(B("CU"), B("CF"))
+        high(B("CF"), B("TCH"))
+        minus257(B("TCH"))
+        if last:
+            ts(B("YC"), tnew, 1000.0, OP.is_ge)
+            dma("y", "dyc", T.yc[:, :], T.YC[:, :], [B("YC")], [])
+        distances("CU", xr, "CKE", "TCH", 0, [[(3, 4)], [(4, 8)], [(8, 12)], [(12, 15), (15, 16)]], lambda: None, True)
+        tt(B("CB"), B("CF"), B("pcr", 256, 512), OP.add)
+        ts(B("TH"), B(ks, 0, 16), 0xFFF000, OP.bitwise_and)
+        ts(B("OLD"), B("TO"), 4095, OP.bitwise_and)
+        act(B("pcr", 0, 256), B(m, 0, 256), AF.Copy)
+        mm(B("pcnt", 0, 256), B("IDM"), B(xr, 0, 256), True, False)
+        mm(B("pcnt", 0, 256), B("IDM"), B(xr, 0, 256), False, False)
+        for q in range(4):
+            low = B("RB", 0, 64) if q == 0 else B("pcut", 64 * q, 64 * q + 64)
+            tt(low, B("pd%d" % q, 0, 64), B("CB", 64 * q, 64 * q + 64), OP.add)
+            if q == 0:
+                cp(B("RA", 0, 64), B("pd0", 0, 64))
+            else:
+                o = 64 * (q - 1)
+                tt(B("RA", o + 64, o + 128), B("RA", o, o + 64), B("pd%d" % q, 0, 64), OP.min)
+                tt(B("RB", o + 64, o + 128), B("RB", o, o + 64), low, OP.min)
+        for run in ("RA", "RB"):
+            tt(B(run, 0, 32), B(run, 192, 224), B(run, 224, 256), OP.min)
+        for j, run in enumerate(("RA", "RB")):
+            tt(B("EI", 16 * j, 16 * j + 16), B(run, 0, 16), B(run, 16, 32), OP.min)
+        tt(B("LT"), B("EI", 0, 16), B("TH"), OP.is_lt)
+        ts(B("ET"), B("EI", 0, 16), 3840, OP.bitwise_and)
+        ts(B("EM"), B("EI"), 255, OP.bitwise_and)
+        tt(B("JJ"), B("ET"), B("VS"), OP.add)
+        ts(B("N1"), B("EM", 0, 16), 256.0, OP.mult)
+        tt(B("PO"), B("JJ"), B("LT"), OP.mult)
+        tt(B("BN"), B("N1"), B("EM", 16, 32), OP.add)
+        cp(B("POU"), B("PO"))
+        tt(B("DL"), B("BN"), B("OLD"), OP.subtract)
+        sgat(B("GX"), B("D", 0, 4112), B("POU"))
+        mm(B("pcnt", 0, 256), B("IDM"), B("GX"), False, True)
+        act(B("XN"), B("pcnt", 0, 256), AF.Identity, bias=255.75)
+        tt(B("DT"), B("DL"), B("LT"), OP.mult)
+        act(B("XS%d" % r), B("XN"), AF.Identity, scale=0.5, bias=-128.0)
+        gat(B("UP"), B("DT"), B("REP"), B("OH"), OP.mult)
+        ms = "MS%d" % r
+        tt(B(ms, 0, 256), B("UP"), B("pcr", 0, 256), OP.add)
+        if last:
+            sgat(B("YX"), B("XS%d" % r), B("PERM"))
+            dma("y", "dyx", T.yx[:, :], T.YX[:, :], [B("YX")], [])
+            swap_in(B(ms, 0, 256), B("PERM2"))
+            swap_out("YP")
+            dma("y", "dyp", T.yp[:, :], T.YP[:, :], [B("YP")], [])
+            break
+        cp(B("PS%d" % r), B(ms, 0, 256))
+        need("g", [B("XS%d" % r), B("PS%d" % r)], [])
+        rid, pid = topo.addr(nxt)[:2]
+        eg = topo.engines(core, nxt)
+        half = len(eg) // 2
+        masks = [sum(1 << e for e in eg[:half]), sum(1 << e for e in eg[half:])]
+        dst = [DstId(rid=rid, pnc=pid)]
+        a1, a2, a3 = "a1%d" % (r + 1), "a2%d" % (r + 1), "a3%d" % (r + 1)
+        g.remote_dma_fused([
+            RemoteDMATransfer(dst_ids=dst, dma_engine_mask=masks[0], remote_sem=T.sem[a1], src=T["XS%d" % r][:, :],
+                              dst=T["XR%d" % (r + 1)][:, 0:256]),
+            RemoteDMATransfer(dst_ids=dst, dma_engine_mask=masks[1], remote_sem=T.sem[a1], src=T["PS%d" % r][:, :],
+                              dst=T["PU%d" % (r + 1)][:, :])], local_sem=T.sem.ls)
+        sent += len(eg)
+        n = len(topo.engines(prv, core))
+        mark("rem", (a1, n), [], [B("XR%d" % (r + 1), 0, 256), B("PU%d" % (r + 1))])
+        ta = "TS%d" % r
+        prep(ms, ta)
+        need("g", [B(ta)], [])
+        g.remote_dma(T["TR%d" % (r + 1)][:, :], T[ta][:, :], T.sem[a3], T.sem.ls, pid, rid, topo.mask(core, nxt))
+        sent += len(eg)
+        mark("rem", (a3, n), [], [B("TR%d" % (r + 1))])
+        prep2(ms)
+        need("g", [B(ms)], [])
+        g.remote_dma(T["M%d" % (r + 1)][:, :], T[ms][:, :], T.sem[a2], T.sem.ls, pid, rid, topo.mask(core, nxt))
+        sent += len(eg)
+        mark("rem", (a2, n), [], [B("M%d" % (r + 1))])
+    g.wait_ge(T.sem.ls, sent)
+    for e in "vstg":
+        g.wait_ge(T.sem["q" + e], cnt[e])
+    for s in ("dx0", "dp0", "dtx", "dpu", "dt0", "dyp", "dyx", "dyc") + tuple("dc%d" % r for r in range(R)):
+        g.wait_ge(T.sem[s], 16)

@@ -3,39 +3,40 @@ from concourse.mybir import AluOpType, ActivationFunctionType
 
 R = 4
 BIG = 16384.0
-TOP = 8388608
+TOP = 2040 * 4096
+CYCLE, GATHER, HOP, DMA, REMOTE, MIB = 0.85, 1.2, 200.0, 1100.0, 1200.0, 3500.0
+LEAD, PE, CALL = 4000.0, 0.55, 40.0
 
 SCRATCH = {}
-SHAPES = {
-    "bfloat16": "TX 4096 X0 256 D 4112 AB 4096 OA 2048 OX 1024 OB 4096 LS 2048 LX 2048 IDM 128 IDN 128 IDB 128 IDT 128 GR 768 IOM 128 IM 128 "
-                "IOB 256 CKC 256 CKE 256 NEG 256 ONE 8 NE 128 TCH 256 FB 32 XN 256 GX 256 YX 256",
-    "int32": "PUW 4096 P0 256 I1 16 I2 16 I3 16 I5 16 PERMI 16 REPI 16 VS 16 GI 16 HI 16 FI 32 FM 32 KS 16 TH 16 EI 32 EM 32 ET 16 LT 16 "
-             "JJ 16 PO 16 TO 16 TF 16 OLD 16",
-    "uint16": "PERM 16 PERM2 32 REP 16 TL 32 CU 256 POU 16",
-    "float32": "MKI 512 MK 512 CL 256 COLS 16 COLP 16 COLH 16 SW 512 SWT 512 AA 256 RA 256 RB 256 SK 256 KT 256 OH 256 PR 128 "
-               "CF 256 CB 256 N1 16 BN 16 DL 16 DT 16 UP 256 YP 256 YC 256",
+SHARED = {
+    "bfloat16": "X0 256 LW 144 LV 144 IDM 128 IDB 128 IDC 128 IDP 128 IDQ 128 MVB 512 IOM 144 IM 128 CKC 128 CKE 128 CK1 128 NEG 256 C160 128 "
+                "LAST 128 YX 256 FS 1024 FR 3072 IE 128 SPR 256 SELI 256 SEL 2048 XIN 1024 XS 1024",
+    "int32": "PUW 4096 P0 256 I1 8 I2 8 I4 16 I5 16 I6 8 I7 8 I8 8 J3 8 J4 8 J5 8",
+    "uint16": "RO 16 FIN 16 END 8 REP 8 REP5 8 PIN 1024 PS 1024",
+    "float32": "ID32 128 PD32 128 MVF 512 CL 128 JM 8 COL 24 P0F 256 SW 256 YP 256 YCF 256 GOON 384 ANEW 256 STEP 40",
 }
-for _d, _l in SHAPES.items():
-    _w = _l.split()
-    for _n, _c in zip(_w[::2], _w[1::2]):
-        SCRATCH[_n] = ("sbuf", [128, int(_c)], _d)
-for _n in ("pcr", "pcnt", "pchg", "pcut", "pd0", "pd1", "pd2", "pd3"):
+OWN = {
+    "bfloat16": "TX 4224 T0 1280 XT 128 D 2048 AB 2048 OA 1024 OB 1024 TA 128 FB 16 CFL 128",
+    "uint16": "TL 16 CU 128 XL 8",
+    "float32": "NE 128 EL 128 BND 128 LO 128 X 384 Y 384 C 128 KS 128 OH 128 PR 256 TO 256 G 256 GT 256 CF 128 ST 24 Z 128 SQ 40 NM 40 TK 8 "
+               "OT 128 UP 128 YC 256 MN 128 MS 128",
+}
+SIDE = {}
+for _t, _k in ((SHARED, 1), (OWN, 2)):
+    for _d, _l in _t.items():
+        _w = _l.split()
+        for _n, _c in zip(_w[::2], _w[1::2]):
+            SCRATCH[_n] = ("sbuf", [128, _k * int(_c)], _d)
+            if _k == 2:
+                SIDE[_n + "a"], SIDE[_n + "b"] = (_n, 0, int(_c)), (_n, int(_c), int(_c))
+for _n in ("pa", "pb", "ma", "mb", "wa0", "wa1", "wb0", "wb1"):
     SCRATCH[_n] = ("psum", [128, 512], "float32")
-for _r in range(R):
-    SCRATCH["TR%d" % _r] = ("sbuf", [128, 256], "bfloat16")
-    SCRATCH["TS%d" % _r] = ("sbuf", [128, 256], "bfloat16")
-    SCRATCH["XR%d" % _r] = ("sbuf", [128, 1024], "bfloat16")
-    SCRATCH["PU%d" % _r] = ("sbuf", [128, 256], "uint16")
-    SCRATCH["M%d" % _r] = ("sbuf", [128, 1008], "float32")
-    SCRATCH["XS%d" % _r] = ("sbuf", [128, 256], "bfloat16")
-    SCRATCH["PS%d" % _r] = ("sbuf", [128, 256], "uint16")
-    SCRATCH["MS%d" % _r] = ("sbuf", [128, 1008], "float32")
-SCRATCH["FS"] = ("sbuf", [128, 256 * R], "bfloat16")
-SCRATCH["FR"] = ("sbuf", [128, 768 * R], "bfloat16")
-SCRATCH["T0"] = ("sbuf", [128, 256 * R + 256], "bfloat16")
 
-SEMAPHORES = ["qv", "qs", "qt", "qg", "ls", "dx0", "dp0", "dtx", "dpu", "dt0", "dyp", "dyx", "dyc"]
-SEMAPHORES += ["%s%d" % (a, r) for a in ("a1", "a2", "a3", "fl", "dc") for r in range(R)]
+SEMAPHORES = ["qv", "qs", "qt", "qg", "ls", "dx0", "dp0", "dpu", "dyp", "dyx", "dyc"]
+SEMAPHORES += [a + e for a in ("dtx", "dt0") for e in "ab"]
+SEMAPHORES += ["%s%s%d" % (a, e, r) for a in ("a1", "a2", "fl", "dc") for e in "ab" for r in range(R)]
+
+WHO = "svss"
 
 
 def rank_program(g, core, T, topo):
@@ -48,27 +49,38 @@ def rank_program(g, core, T, topo):
     cnt = {"v": 0, "s": 0, "t": 0, "g": 0}
     known = {e: {} for e in eng}
     acc = {}
+    total = {}
 
     def B(name, lo=0, hi=None, step=1):
+        if name in SIDE:
+            name, at, n = SIDE[name]
+            lo, hi = at + lo, at + (n if hi is None else hi)
         if hi is None:
             hi = SCRATCH[name][1][1]
         ap = T[name][:, lo:hi] if step == 1 else T[name][:, lo:hi:step]
-        return (name, lo, hi, ap)
+        return (name, lo, hi, ap, (hi - lo + step - 1) // step, step)
 
     def psum(name):
         return SCRATCH[name][0] == "psum"
 
+    def short(*specs):
+        return all(SCRATCH[b[0]][2] in ("bfloat16", "uint16") for b in specs)
+
+    def meet(a, b):
+        return a[1] < b[2] and b[1] < a[2] and not (a[5] == b[5] and (a[1] - b[1]) % a[5])
+
+    def covers(a, b):
+        return a[1] <= b[1] and b[2] <= a[2] and (a[5] == 1 or (a[5] == b[5] and (a[1] - b[1]) % a[5] == 0))
+
     def need(e, reads, writes):
         deps = {}
         for w, specs in ((False, reads), (True, writes)):
-            for name, lo, hi, _ in specs:
-                for plo, phi, pw, pe, tok in acc.get(name, ()):
-                    if pe == e:
-                        hit = e != "t" and pw != w and lo < phi and plo < hi
-                    elif psum(name):
-                        hit = True
+            for b in specs:
+                for a, pw, pe, tok in acc.get(b[0], ()):
+                    if pe == e == "t":
+                        hit = False
                     else:
-                        hit = (pw or w) and lo < phi and plo < hi
+                        hit = (pe != e and psum(b[0])) or ((pw or w) and meet(a, b))
                     if hit and deps.get(tok[0], 0) < tok[1]:
                         deps[tok[0]] = tok[1]
         for sem in sorted(deps):
@@ -77,359 +89,385 @@ def rank_program(g, core, T, topo):
                 known[e][sem] = deps[sem]
 
     def mark(pe, tok, reads, writes):
-        for name, lo, hi, _ in writes:
-            old = [a for a in acc.get(name, ()) if not (lo <= a[0] and a[1] <= hi)]
-            acc[name] = old + [(lo, hi, True, pe, tok)]
-        for name, lo, hi, _ in reads:
-            old = [a for a in acc.get(name, ()) if not (a[3] == pe and not a[2] and lo <= a[0] and a[1] <= hi)]
-            acc[name] = old + [(lo, hi, False, pe, tok)]
+        for b in writes:
+            old = [a for a in acc.get(b[0], ()) if not (covers(b, a[0]) and (a[2] == pe or not psum(b[0])))]
+            acc[b[0]] = old + [(b, True, pe, tok)]
+        for b in reads:
+            old = [a for a in acc.get(b[0], ()) if not (a[2] == pe and not a[1] and covers(b, a[0]))]
+            acc[b[0]] = old + [(b, False, pe, tok)]
 
-    def op(e, reads, writes, fn):
-        need(e, reads, writes)
-        fn().then_inc(T.sem["q" + e], 1)
-        cnt[e] += 1
-        mark(e, ("q" + e, cnt[e]), reads, writes)
+    calls = []
+    second = [0]
 
-    def dma(e, sem, out, in_, reads, writes):
-        need(e, reads, writes)
-        eng[e].dma_start(out, in_).then_inc(T.sem[sem], 16)
-        mark("d" + sem, (sem, 16), reads, writes)
+    def op(e, reads, writes, fn, each=1.0, least=64, fixed=0):
+        def issue():
+            need(e, reads, writes)
+            fn().then_inc(T.sem["q" + e], 1)
+            cnt[e] += 1
+            mark(e, ("q" + e, cnt[e]), reads, writes)
+        t = CYCLE * (fixed + max(least, each * writes[0][4])) + (CALL if e == "v" and least else 0.0)
+        calls.append((e, reads, writes, issue, t, t + HOP))
+
+    def dmas(sem, moves, reads, writes, lands=DMA):
+        def issue():
+            for e, out, in_ in moves:
+                need(e, reads, writes)
+                eng[e].dma_start(out, in_).then_inc(T.sem[sem], 16)
+            total[sem] = 16 * len(moves)
+            mark("d" + sem, (sem, total[sem]), reads, writes)
+        calls.append((moves[0][0], reads, writes, issue, 60.0, lands))
+
+    def remote(transfers, srcs, arrivals, writes):
+        def issue():
+            need("g", srcs, [])
+            g.remote_dma_fused(transfers, local_sem=T.sem.ls)
+            for sem, n, bufs in arrivals:
+                mark("rem", (sem, n), [], bufs)
+                total[sem] = n
+        calls.append(("g", srcs, [b for a in arrivals for b in a[2]], issue, 300.0, REMOTE + 250.0 * (writes - 1)))
+
+    def issue_all():
+        seen, turn_of, after = {}, {}, [{} for _ in calls]
+        for i, (e, reads, writes, _, _, _) in enumerate(calls):
+            for w, specs in ((False, reads), (True, writes)):
+                for b in specs:
+                    for j, a, pw in seen.get(b[0], ()):
+                        same = calls[j][0] == e
+                        if j != i and (((w or pw) and meet(a, b)) or (psum(b[0]) and (not same or e == "t"))):
+                            after[j][i] = calls[j][4 if same and e == "t" else 5]
+            for w, specs in ((True, writes), (False, reads)):
+                for b in specs:
+                    name = b[0]
+                    old = seen.get(name, [])
+                    if psum(name):
+                        if turn_of.get(name, (e,))[0] != e:
+                            old = old[turn_of[name][1]:]
+                            turn_of[name] = (e, len(old))
+                        turn_of.setdefault(name, (e, 0))
+                    elif w:
+                        old = [a for a in old if not covers(b, a[1])]
+                    seen[name] = old + [(i, b, w)]
+        way = [0.0] * len(calls)
+        for i in range(len(calls) - 1, -1, -1):
+            way[i] = max([t + way[j] for j, t in after[i].items()] + [calls[i][5]])
+        for i in range(second[0]):
+            way[i] += LEAD
+        there = [0.0] * len(calls)
+        busy = {e: [] for e in eng}
+        for i in sorted(range(len(calls)), key=lambda i: (-way[i], i)):
+            t, slots, k = there[i], busy[calls[i][0]], 0
+            while k < len(slots) and slots[k][0] < t + calls[i][4]:
+                t = max(t, slots[k][1])
+                k += 1
+            slots.insert(k, (t, t + calls[i][4]))
+            there[i] = t
+            for j, gap in after[i].items():
+                there[j] = max(there[j], t + gap)
+        for i in sorted(range(len(calls)), key=lambda i: (there[i], i)):
+            calls[i][3]()
 
     def tt(out, a, b, o):
-        op("v", [a, b], [out], lambda: g.vector.tensor_tensor(out[3], a[3], b[3], o))
+        op("v", [a, b], [out], lambda: g.vector.tensor_tensor(out[3], a[3], b[3], o), 1.0 if psum(a[0]) or psum(b[0]) else 2.0)
 
     def ts(out, a, s1, o1, s2=None, o2=None):
         reads = [a] + [s for s in (s1,) if isinstance(s, tuple)]
         x = s1[3] if isinstance(s1, tuple) else s1
+        each = 0.5 if short(out, a) else 1.0
         if o2 is None:
-            op("v", reads, [out], lambda: g.vector.tensor_scalar(out[3], a[3], x, None, o1))
+            op("v", reads, [out], lambda: g.vector.tensor_scalar(out[3], a[3], x, None, o1), each)
         else:
-            op("v", reads, [out], lambda: g.vector.tensor_scalar(out[3], a[3], x, s2, o1, o2))
+            op("v", reads, [out], lambda: g.vector.tensor_scalar(out[3], a[3], x, s2, o1, o2), each)
 
     def cp(out, a):
         op("v", [a], [out], lambda: g.vector.tensor_copy(out[3], a[3]))
 
-    def gat(out, win, lst, b, o):
+    def scan(out, a, b, o1, o2):
+        op("v", [a, b], [out], lambda: g.vector.tensor_tensor_scan(out[3], a[3], b[3], 0.0, o1, o2))
+
+    def gat(out, win, lst, b=None, o=None):
         if b is None:
-            op("v", [win, lst], [out], lambda: g.vector.tensor_copy(out[3], win[3].indirect(lst[3])))
+            op("v", [win, lst], [out], lambda: g.vector.tensor_copy(out[3], win[3].indirect(lst[3])), GATHER, 0, 60)
         else:
-            op("v", [win, lst, b], [out], lambda: g.vector.tensor_tensor(out[3], win[3].indirect(lst[3]), b[3], o))
+            op("v", [win, lst, b], [out], lambda: g.vector.tensor_tensor(out[3], win[3].indirect(lst[3]), b[3], o), GATHER, 0, 60)
+
+    def turn(out, a):
+        op("v", [a], [out], lambda: g.vector.transpose(out[3], a[3]))
 
     def fill(out, value):
         op("v", [], [out], lambda: g.vector.memset(out[3], value))
 
     def act(out, a, f, scale=1.0, bias=0.0):
-        col = isinstance(bias, tuple)
-        x = bias[3] if col else bias
-        op("s", [a, bias] if col else [a], [out], lambda: g.scalar.activation(out[3], a[3], f, bias=x, scale=scale))
+        op("s", [a], [out], lambda: g.scalar.activation(out[3], a[3], f, bias=bias, scale=scale), 1.0, 0, 50)
 
     def sgat(out, win, lst):
-        op("s", [win, lst], [out], lambda: g.scalar.activation(out[3], win[3].indirect(lst[3]), AF.Copy))
+        op("s", [win, lst], [out], lambda: g.scalar.activation(out[3], win[3].indirect(lst[3]), AF.Copy), GATHER, 0, 80)
 
     def mm(out, lhsT, rhs, start, stop):
-        op("t", [lhsT, rhs], [out], lambda: g.tensor.matmul(out[3], lhsT[3], rhs[3], start, stop))
+        k = PE if short(rhs) else 4.0 * PE
+        op("t", [lhsT, rhs], [out], lambda: g.tensor.matmul(out[3], lhsT[3], rhs[3], start, stop), k, 64 * k, 12)
 
     def iota(name, pattern, base, cm):
         out = B(name)
         if SCRATCH[name][2] == "int32":
-            op("g", [], [out], lambda: g.iota(out[3], pattern, base, cm))
+            op("g", [], [out], lambda: g.iota(out[3], pattern, base, cm), 2.0, 0, 160)
         else:
-            op("g", [], [out], lambda: g.iota(out[3], pattern, base, cm, allow_small_or_imprecise_dtypes=True))
+            op("g", [], [out], lambda: g.iota(out[3], pattern, base, cm, allow_small_or_imprecise_dtypes=True), 2.0, 0, 160)
 
-    def tree(out, a, b, o):
-        tt(B("KT", 0, 128), a, b, o)
-        tt(B("KT", 128, 192), B("KT", 0, 64), B("KT", 64, 128), o)
-        tt(B("KT", 192, 224), B("KT", 128, 160), B("KT", 160, 192), o)
-        tt(out, B("KT", 192, 208), B("KT", 208, 224), o)
+    def MV(kind, u, w):
+        return B(kind, 128 * (2 * u + w), 128 * (2 * u + w) + 128)
 
-    def swap_in(win, lst):
-        gat(B("SW"), win, lst, B("MK"), OP.mult)
-        op("v", [B("SW")], [B("SWT")], lambda: g.vector.transpose(T.SWT[:, :], T.SW[:, :]))
+    dmas("dp0", [("y", T.P0[:, :], T.p0[:, :])], [], [B("P0")])
+    dmas("dx0", [("s", T.X0[:, :], T.x0[:, :])], [], [B("X0")])
+    for par, e in enumerate("ab"):
+        dmas("dtx" + e, [("ys"[h], T.TX[32 * a + 16 * h:32 * a + 16 * h + 16, 4224 * par:4224 * par + 4096],
+                          T.tx[32 * a + 16 * par:32 * a + 16 * par + 16, :]) for a in range(4) for h in range(2)],
+             [], [B("TX" + e, 0, 4096)], DMA + MIB * (par + 1))
+    dmas("dpu", [("y", T.PUW[:, :], T.pu[:, :])], [], [B("PUW")], DMA + MIB * 4)
+    for i, c in enumerate(calls):
+        c[3]()
+        calls[i] = c[:3] + (lambda: None,) + c[4:]
+    for par, e in enumerate("ab"):
+        dmas("dt0" + e, [("y", B("T0" + e, 0, 256)[3], T.TX[0:128:16, 4224 * par:4224 * par + 4096])], [B("TX" + e, 0, 4096)],
+             [B("T0" + e, 0, 256)], DMA + MIB * 2)
 
-    def swap_out(name):
-        for t in range(16):
-            tt(B(name, 16 * t, 16 * t + 16), B("SWT", t, 512, 32), B("SWT", 16 + t, 512, 32), OP.add)
+    iota("I1", [[0, 8]], 0, 1)
+    iota("IOM", [[1, 144]], 0, 0)
+    iota("I4", [[16, 2], [32, 8]], 0, 0)
+    iota("SELI", [[0, 16], [1, 16]], 0, 0)
+    iota("CKC", [[0, 8], [-128, 16]], 2048, 0)
+    iota("CL", [[0, 8], [-128, 16]], TOP + 2048, 0)
+    iota("CKE", [[0, 8], [128, 16]], 128, 0)
+    iota("I2", [[16, 8]], 0, 0)
+    iota("I5", [[16, 8], [128, 2]], 0, 0)
+    iota("I6", [[16, 8]], 15, 0)
+    iota("I7", [[1, 8]], 0, 0)
+    iota("I8", [[5, 8]], 4, 0)
+    iota("IE", [[32, 4], [0, 2], [2, 16]], 0, 0)
 
-    def high(src, ta):
-        act(ta, src, AF.Identity, scale=1.0 / 256.0, bias=159.502)
+    def col(j):
+        return B("COL", j, j + 1)
 
-    def minus257(ta):
-        act(B("pcr", 256, 512), ta, AF.Identity, scale=-257.0, bias=257.0 * 160.0)
+    def ident(out, c, value=None):
+        if value is None:
+            ts(out, B("IOM", 0, 128), c, OP.is_equal)
+        else:
+            ts(out, B("IOM", 0, 128), c, OP.is_equal, value, OP.mult)
 
-    def prep(m, ta):
-        tt(B("NE"), B(m, 0, 256, 2), B(m, 1, 256, 2), OP.not_equal)
-        high(B(m, 0, 256), B(ta))
-        minus257(B(ta))
-        act(B("pcr", 0, 240), B(m, 0, 240), AF.Copy, scale=4096.0)
-        for k in range(16):
-            mm(B("pcut", 8 * k, 128), B("IDT"), B("NE", 0, 128 - 8 * k), k == 0, False)
-        mm(B("pcut", 120, 128), B("IDT"), B("ONE"), False, True)
-
-    def prep2(m):
-        tt(B(m, 512, 768), B(m, 0, 256), B("pcr", 256, 512), OP.add)
-        for p in (0, 1):
-            tt(B(m, 256 + p, 512, 2), B("pcut", 0, 128), B("CL", p, 256, 2), OP.min)
-        tt(B(m, 768, 1008), B("pcr", 0, 240), B(m, 16, 256), OP.add)
-
-    def distances(lst, xr, ck, ta, raw, chunks, later, keep):
-        sgat(B("GR"), B("TX"), B(lst, 16 * raw, 16 * raw + 48))
-        two, one = B("pcnt", 0, 512), B("pchg", 0, 256)
-        mm(two, B("IDM"), B("GR", 0, 512), True, False)
-        mm(B("pcnt", 0, 256), B("IDN"), B(xr, 0, 256), False, False)
-        mm(B("pcnt", 256, 512), B("IDN"), B(xr, 0, 256), False, True)
-        mm(one, B("IDM"), B("GR", 512, 768), True, False)
-        mm(one, B("IDN"), B(xr, 0, 256), False, True)
-        wait = []
-        for q, calls in enumerate(chunks):
-            for ka, kb in calls:
-                gat(B("D", 16 + 256 * ka, 16 + 256 * kb), B("TX"), B(lst, 16 * ka, 16 * kb), B(xr, 0, 256 * (kb - ka)), OP.subtract)
-            ka, kb = calls[0][0], calls[-1][1]
-            for ja, jb in ([(ka, kb)] if q < 3 else [(ka, kb - 1), (kb - 1, kb)]):
-                act(B("AB", 256 * ja, 256 * jb), B("D", 16 + 256 * ja, 16 + 256 * jb), AF.Abs)
-            if q == 0:
-                act(B("AB", 256 * raw, 256 * raw + 512), two, AF.Abs)
-                act(B("AB", 256 * raw + 512, 256 * raw + 768), one, AF.Abs)
-                ka = raw
-            if q == 1:
-                later()
-            ps = B("pd%d" % q, 0, 16 * (kb - ka))
-            mm(ps, B("IDM"), B(ck, 16 * ka, 16 * kb), True, False)
-            for s in range(16):
-                mm(ps, B("LS", 128 * s, 128 * s + 128), B("AB", 256 * ka + s, 256 * kb, 16), False, False)
-            wait.append((ps, B(ta, 16 * ka, 16 * kb)))
-            while q > 0 and wait:
-                ps, dig = wait.pop(0)
-                mm(ps, B("IDM"), dig, False, True)
-        if keep:
-            act(B("D", 16 + 256 * raw, 16 + 256 * raw + 512), two, AF.Copy)
-            act(B("D", 16 + 256 * raw + 512, 16 + 256 * raw + 768), one, AF.Copy)
-
-    dma("y", "dp0", T.P0[:, :], T.p0[:, :], [], [B("P0")])
-    dma("y", "dx0", T.X0[:, :], T.x0[:, :], [], [B("X0")])
-    dma("y", "dtx", T.TX[:, :], T.tx[:, :], [], [B("TX")])
-    dma("y", "dt0", T.T0[:, 0:256], T.tx[0:128:16, :], [], [B("T0", 0, 256)])
-    g.sync.wait_ge(T.sem.dtx, 16)
-    dma("y", "dpu", T.PUW[:, :], T.pu[:, :], [], [B("PUW")])
-
-    iota("I1", [[1, 16]], 0, 16)
-    iota("I2", [[0, 16]], 0, 1)
-    iota("MKI", [[0, 16], [1, 2], [0, 16]], 0, 0)
-    iota("IOM", [[1, 128]], 0, 0)
-    iota("I5", [[1, 16]], 0, 0)
-    iota("I3", [[16, 16]], 16, 0)
-    iota("CL", [[-256, 16], [0, 16]], TOP + 4096 + 255, 0)
-    iota("CKC", [[-256, 16], [0, 16]], 4096 - 160, 0)
-    iota("IOB", [[1, 256]], 0, 0)
-    iota("CKE", [[256, 16], [0, 16]], -160, 0)
-    fill(B("ONE"), 1.0)
+    ts(B("J3"), B("I1"), 16, OP.bitwise_and)
+    ts(B("J4"), B("I1"), 15, OP.bitwise_and)
+    ts(B("J5"), B("I1"), 1, OP.bitwise_and)
+    cp(col(0), B("I1", 0, 1))
+    cp(col(1), B("J4", 0, 1))
+    ts(B("RO"), B("I4"), col(1), OP.add)
+    ts(B("FIN"), B("I5"), col(1), OP.add)
+    for name, src in (("END", "I6"), ("REP", "I7"), ("REP5", "I8")):
+        cp(B(name), B(src))
+    for u in range(2):
+        ts(col(3 + u), B("J3", 0, 1), 16.0 * u, OP.not_equal, 1000.0, OP.mult)
+        ts(col(16 + u), B("J3", 0, 1), 16.0 * u, OP.is_equal)
+        for w in range(2):
+            ts(col(5 + 2 * u + w), col(3 + u), col(0), OP.add, 16.0 * (w - u), OP.add)
+            ident(MV("MVB", u, w), col(5 + 2 * u + w))
+            ident(MV("MVF", u, w), col(5 + 2 * u + w))
+    tt(col(9), col(0), B("J4", 0, 1), OP.subtract)
+    ts(col(10), B("J5", 0, 1), -2.0, OP.mult, 1.0, OP.add)
+    ts(col(11), col(9), 15.0, OP.add)
+    tt(col(12), col(10), col(0), OP.add)
+    tt(col(13), col(9), B("J3", 0, 1), OP.subtract)
+    ts(col(14), col(13), -160.0, OP.add)
+    ts(col(15), col(0), -1.0, OP.add)
+    for c in range(8):
+        ts(B("SEL", 256 * c, 256 * c + 256), B("SELI"), col(0), OP.subtract, -16.0 * c, OP.is_equal)
+    ts(B("LW"), B("IOM"), col(11), OP.is_equal, 4096.0, OP.mult)
+    ts(B("LV"), B("IOM"), col(11), OP.is_equal, 8192.0, OP.mult)
+    ts(B("IM"), B("IOM", 0, 128), col(14), OP.subtract)
+    for name, value in (("IDM", None), ("ID32", None), ("IDB", BIG), ("IDC", float(TOP)), ("IDP", 128.0), ("IDQ", -128.0)):
+        ident(B(name), col(0), value)
+    ident(B("PD32"), col(12))
+    tt(B("PD32"), B("ID32"), B("PD32"), OP.subtract)
+    for j in range(2):
+        ts(B("SPR", 128 * j, 128 * j + 128), B("IE"), col(15 * j), OP.is_equal, BIG, OP.mult)
+    tt(B("JM"), B("I2"), B("J4"), OP.add)
+    for name, value, at, step, there in (("LAST", 0.0, 15, 16, 8192.0), ("GOON", 1.0, 0, 16, 0.0), ("ANEW", 0.0, 0, 16, 33554432.0)):
+        fill(B(name), value)
+        fill(B(name, at, None, step), there)
+    for j, value in enumerate((0.0, -1.0, -128.0, -1.0, 1.0)):
+        fill(B("STEP", j, None, 5), value)
+    fill(B("CL", 0, None, 16), 0.0)
+    cp(B("CK1"), B("CKC"))
+    fill(B("CK1", 0, None, 16), -2.0 * TOP)
     fill(B("NEG"), -1.0)
-    fill(B("D", 0, 16), 0.0)
-    fill(B("AA", 0, 16), 0.0)
-    fill(B("PR", 0, 16), 0.0)
-    fill(B("SK", 0, 16), 0.0)
-    ts(B("PERMI"), B("I1"), 255, OP.bitwise_and)
-    ts(B("HI"), B("I2"), 16, OP.bitwise_and, 4, OP.logical_shift_right)
-    ts(B("REPI"), B("I2"), 15, OP.bitwise_and)
-    ts(B("GI"), B("I2"), 112, OP.bitwise_and)
-    cp(B("PERM"), B("PERMI"))
-    cp(B("PERM2", 0, 32, 2), B("PERMI"))
-    cp(B("PERM2", 1, 32, 2), B("PERMI"))
-    cp(B("COLH"), B("HI"))
-    cp(B("COLP"), B("I2"))
-    cp(B("REP"), B("REPI"))
-    ts(B("MK"), B("MKI"), B("COLH", 0, 1), OP.is_equal)
-    tt(B("COLS"), B("GI"), B("I5"), OP.add)
-    tt(B("VS"), B("REPI"), B("I3"), OP.add)
-    ts(B("IDM"), B("IOM"), B("COLP", 0, 1), OP.is_equal)
-    ts(B("IDN"), B("IOM"), B("COLP", 0, 1), OP.is_equal, -1.0, OP.mult)
-    for s in range(16):
-        act(B("LX", 128 * s, 128 * s + 128), B("IOM"), AF.Abs, scale=-1.0, bias=B("COLS", s, s + 1))
-    act(B("LS"), B("LX"), AF.Relu, scale=-4096.0, bias=4096.0)
-    swap_in(B("P0"), B("PERM2"))
-    swap_out("M0")
-    cp(B("PU0"), B("M0", 0, 256))
-    gat(B("XR0", 0, 256), B("X0"), B("PERM"), None, None)
-    ts(B("IDT"), B("IOM"), B("COLP", 0, 1), OP.is_equal, 16777216.0, OP.mult)
-    ts(B("IDB"), B("IOM"), B("COLP", 0, 1), OP.is_equal, BIG, OP.mult)
-    ts(B("IM"), B("IOM"), B("COLS", 0, 1), OP.subtract)
-    fill(B("CL", 0, 16), 0.0)
+    fill(B("C160"), 160.0)
+    cp(B("P0F"), B("P0"))
+    turn(B("SW"), B("P0F"))
+    for par, e in enumerate("ab"):
+        fill(B("PR" + e, 0, 8), 0.0)
+        gat(B("MN" + e), B("SW"), B("RO", 8 * par, 8 * par + 8))
+        gat(B("PIN", 128 * par, 128 * par + 128), B("SW"), B("RO", 8 * par, 8 * par + 8))
+        for c in range(8):
+            for h in range(2):
+                mm(B("w%s0" % e, 16 * c, 16 * c + 16), MV("MVB", par, h), B("X0", 32 * c + 16 * h, 32 * c + 16 * h + 16), c + h == 0, c + h == 8)
+        act(B("XIN", 128 * par, 128 * par + 128), B("w%s0" % e, 0, 128), AF.Identity, scale=2.0, bias=256.0)
 
     others = [q for q in range(R) if q != rank]
     nxt, prv = T.cores[(rank + 1) % R], T.cores[(rank - 1) % R]
-    rows = [(1, 5), (5, 9), (9, 13), (13, 16)]
-    singles = [[(k, k + 1) for k in range(max(a, 4), b)] for a, b in rows]
-    sent = 0
-    for r in range(R):
-        xr, pu, m, last = "XR%d" % r, "PU%d" % r, "M%d" % r, r == R - 1
-        told, tnew = B("T0", 256 * r, 256 * r + 256), B("T0", 256 * r + 256, 256 * r + 512)
-        fs = B("FS", 256 * r, 256 * r + 256)
+    sent = [0]
 
-        def chain_arrays():
-            if r == 0:
-                prep(m, "TR0")
+    def stream(par, r):
+        e = "ab"[par]
+        o = 128 * (2 * r + par)
+        p, m, w = "p" + e, "m" + e, "w%s0" % e
+        told, tnew = B("T0" + e, 256 * r, 256 * r + 256), B("T0" + e, 256 * r + 256, 256 * r + 512)
+        fs, xin, xs = B("FS", o, o + 128), B("XIN", o, o + 128), B("XS", o, o + 128)
+        tx, pd = B("TX" + e, 0, 4096), B(p, 0, 128)
 
-        distances(pu, xr, "CKC", "TR%d" % r, 1, singles, chain_arrays, False)
-        act(B(xr, 256, 512), B(xr, 0, 256), AF.Copy)
-        act(B(xr, 512, 1024), B(xr, 0, 512), AF.Copy)
-        if r == 0:
-            prep2(m)
-        act(B("pcr", 0, 240), B(m, 768, 1008), AF.Copy)
+        def S(name, a=0, b=None, step=1):
+            return B(name + e, a, b, step)
 
-        def key_a(q):
-            ka, kb = 16 * rows[q][0], 16 * rows[q][1]
-            tt(B("AA", ka, kb), B("pd%d" % q, 0, kb - ka), B(m, 256 + ka, 256 + kb), OP.min)
+        def ends(name, j):
+            return S(name, 128 * j + 15, 128 * j + 128, 16)
 
-        def key_b(q):
-            ka, kb = 16 * rows[q][0], 16 * rows[q][1]
-            tt(B("RB", 0, 64) if q == 0 else B("pcut", 64 * q, 64 * q + kb - ka), B("AA", ka, kb), B(m, 512 + ka, 512 + kb), OP.add)
+        def digits(src):
+            act(S("TA"), src, AF.Identity, scale=1.0 / 128.0, bias=159.502)
+            mm(B(m, 256, 384), B("ID32"), src, True, False)
+            mm(B(m, 256, 384), B("IDP"), B("C160"), False, False)
+            mm(B(m, 256, 384), B("IDQ"), S("TA"), False, True)
 
-        key_a(0)
-        key_a(1)
-        key_b(0)
-        tt(B("pcut", 256, 320), B("AA", 16, 80), B("AA", 80, 144), OP.max)
-        key_a(2)
-        key_b(1)
-        tt(B("RA", 64, 128), B("pcut", 256, 320), B("AA", 144, 208), OP.max)
-        tt(B("RB", 128, 192), B("RB", 0, 64), B("pcut", 64, 128), OP.max)
-        key_b(2)
-        key_a(3)
-        tt(B("RB", 64, 128), B("RB", 128, 192), B("pcut", 128, 192), OP.max)
-        key_b(3)
-        tt(B("RA", 64, 112), B("RA", 64, 112), B("AA", 208, 256), OP.max)
-        tt(B("RB", 64, 112), B("RB", 64, 112), B("pcut", 192, 240), OP.max)
-        for run in ("RA", "RB"):
-            tt(B(run, 192, 224), B(run, 64, 96), B(run, 96, 128), OP.max)
-        for j, run in enumerate(("RA", "RB")):
-            tt(B("FI", 16 * j, 16 * j + 16), B(run, 192, 208), B(run, 208, 224), OP.max)
-        ts(B("FM"), B("FI"), 255, OP.bitwise_and)
-        cp(B("FB"), B("FM"))
-        for c in range(16):
-            if c < 8:
-                ts(B("OA", 128 * c, 128 * c + 128), B("IM"), B("FB", c, c + 1), OP.is_equal)
-            else:
-                j = c - 8
-                act(B("OX", 128 * j, 128 * j + 128), B("IM"), AF.Abs, scale=-1.0, bias=B("FB", c, c + 1))
-                if c % 4 == 3:
-                    act(B("OA", 128 * c - 384, 128 * c + 128), B("OX", 128 * j - 384, 128 * j + 128), AF.Relu, scale=-1.0, bias=1.0)
-            ts(B("OB", 256 * c, 256 * c + 256), B("IOB"), B("FB", 16 + c, 17 + c), OP.is_equal)
-        for c in range(16):
-            mm(B("pchg", 0, 256), B("OA", 128 * c, 128 * c + 128), B("OB", 256 * c, 256 * c + 256), c == 0, c == 15)
-        mm(B("pcut", 0, 256), B("IDM"), told, True, False)
-        mm(B("pcut", 0, 256), B("IDB"), B("NEG"), False, False)
+        def distances(lst, l0, lw, code):
+            for q, who in enumerate(WHO):
+                d, bank = S("D", 512 * q, 512 * q + 512), "w%s%d" % (e, q % 2)
+                (sgat if who == "s" else gat)(d, tx, B(lst, l0 + 32 * q, l0 + 32 * q + 32))
+                for j in range(2):
+                    mm(B(bank, 256 * j, 256 * j + 256), S("XT"), B("SEL", 512 * q + 256 * j, 512 * q + 256 * j + 256), j == 0, False)
+                mm(B(bank), B("IDM"), d, False, True)
+                act(S("AB", 512 * q, 512 * q + 512), B(bank), AF.Abs)
+            mm(pd, B("IDM"), B(code), True, False)
+            for half in range(2):
+                for s in range(16):
+                    mm(B(p, 64 * half, 64 * half + 64), B(lw, 15 - s, 143 - s), S("AB", 1024 * half + s, 1024 * half + 1024, 16), False,
+                       half + s == 16)
+
+        mm(B(m, 384, 512), xin, B("IDM"), True, True)
+        act(S("XT"), B(m, 384, 512), AF.Identity, scale=-0.5, bias=128.0)
         if r > 0:
-            for q, (ka, kb) in enumerate(rows):
-                act(B("pcnt", 16 * ka, 16 * kb), B("pd%d" % q, 0, 16 * (kb - ka)), AF.Relu, bias=-16777216.0)
-        act(fs, B("pchg", 0, 256), AF.Sign)
-        mm(B("pcut", 0, 256), B("IDB"), fs, False, False)
-        need("g", [fs], [])
+            cp(S("MN"), B("PIN", o, o + 128))
+        mm(B(m, 0, 128), B("PD32"), S("MN"), True, False)
+        mm(B(m, 0, 128), B("IDM"), B("LAST"), False, True)
+        act(S("NE"), B(m, 0, 128), AF.Abs, scale=16777216.0)
+        digits(S("MN"))
+        mm(B(m, 128, 256), B("IDM"), S("TA"), True, True)
+        scan(S("EL"), B("GOON", 0, 128), S("NE"), OP.mult, OP.max)
+        tt(S("BND"), S("EL"), B("CL"), OP.min)
+        distances("PIN", o, "LW", "CKC")
+        tt(S("X", 0, 128), pd, S("BND"), OP.min)
+        if r > 0:
+            act(S("CFL"), pd, AF.Sign, bias=-16777216.0)
+        for j in (1, 2):
+            tt(S("X", 128 * j, 128 * j + 128), S("X", 0, 128), B(m, 128 * j, 128 * j + 128), OP.add)
+        scan(S("Y"), B("GOON"), S("X"), OP.mult, OP.max)
+        for j in (1, 2):
+            tt(S("FB", 8 * j - 8, 8 * j), ends("Y", j), ends("Y", 0), OP.subtract)
+        for c in range(8):
+            ts(S("OA", 128 * c, 128 * c + 128), B("IM"), S("FB", c, c + 1), OP.is_equal)
+            ts(S("OB", 128 * c, 128 * c + 128), B("IOM", 0, 128), S("FB", 8 + c, 9 + c), OP.is_equal)
+        for c in range(8):
+            mm(B(w, 0, 128), S("OA", 128 * c, 128 * c + 128), S("OB", 128 * c, 128 * c + 128), c == 0, c == 7)
+        act(fs, B(w, 0, 128), AF.Sign)
         dsts, ids = [], []
         for q in others:
-            j = 3 * r + (rank - q - 1) % R
+            j = 3 * o + 128 * ((rank - q - 1) % R)
             rid, pid = topo.addr(T.cores[q])[:2]
             ids.append(DstId(rid=rid, pnc=pid))
-            dsts.append(T.FR[:, 256 * j:256 * j + 256])
-        g.remote_dma_fused([RemoteDMATransfer(dst_ids=ids, dma_engine_mask=topo.mask(core, T.cores[others[0]]), remote_sem=T.sem["fl%d" % r],
-                                              srcs=[fs[3]], dsts=dsts)], local_sem=T.sem.ls)
-        sent += len(topo.engines(core, T.cores[others[0]]))
-        mark("rem", ("fl%d" % r, sum(len(topo.engines(T.cores[q], core)) for q in others)), [], [B("FR", 768 * r, 768 * r + 768)])
-        for j in range(3 * r, 3 * r + 3):
-            mm(B("pcut", 0, 256), B("IDB"), B("FR", 256 * j, 256 * j + 256), False, j == 3 * r + 2)
-        ks, sk = ("FI", "AA")
+            dsts.append(T.FR[:, j:j + 128])
+        fl = "fl%s%d" % (e, r)
+        remote([RemoteDMATransfer(dst_ids=ids, dma_engine_mask=topo.mask(core, T.cores[others[0]]), remote_sem=T.sem[fl], srcs=[fs[3]],
+                                  dsts=dsts)], [fs],
+               [(fl, sum(len(topo.engines(T.cores[q], core)) for q in others), [B("FR", 3 * o, 3 * o + 384)])], 3)
+        sent[0] += len(topo.engines(core, T.cores[others[0]]))
+        mm(B(w, 128, 384), B("IDB"), B("NEG"), True, False)
+        for i, mp in enumerate([fs] + [B("FR", 3 * o + 128 * j, 3 * o + 128 * j + 128) for j in range(3)]):
+            for j in range(2):
+                mm(B(w, 128 + 128 * j, 256 + 128 * j), B("SPR", 128 * j, 128 * j + 128), mp, False, i + j == 4)
+        tt(tnew, B(w, 128, 384), told, OP.max)
+        dmas("dc%s%d" % (e, r), [("y", T.TX[0:128:16, 4224 * par:4224 * par + 4096], tnew[3])], [tnew], [tx])
+        keys, top = S("X", 0, 128), S("Y", 0, 128)
         if r > 0:
-            ks, sk = ("KS", "SK")
-            tt(B("pcnt", 272, 512), B("pcnt", 16, 256), B("CL", 16, 256), OP.min)
-            tt(B("SK", 16, 256), B("pcnt", 272, 512), B("AA", 16, 256), OP.max)
-            tree(B("KS", 0, 16), B("SK", 0, 128), B("SK", 128, 256), OP.max)
-        gat(B("OH"), B(ks, 0, 16), B("REP"), B(sk), OP.is_equal)
-        tt(B("PR", 16, 128), B("OH", 16, 128), B("pcr", 0, 112), OP.mult)
-        tt(B("pchg", 0, 128), B("OH", 128, 256), B("pcr", 112, 240), OP.mult)
-        tree(B("TO"), B("PR"), B("pchg", 0, 128), OP.add)
-        ts(B("TF"), B("TO"), 12, OP.logical_shift_right)
-        cp(B("TL", 0, 32, 2), B("TF"))
-        cp(B("TL", 1, 32, 2), B("TF"))
-        swap_in(B("PUW"), B("TL"))
-        tt(tnew, B("pcut", 0, 256), told, OP.max)
-        dma("y", "dc%d" % r, T.TX[0:128:16, 0:4096], tnew[3], [tnew], [B("TX")])
-        swap_out("CF")
-        cp(B("CU"), B("CF"))
-        high(B("CF"), B("TCH"))
-        minus257(B("TCH"))
-        if last:
-            ts(B("YC"), tnew, 1000.0, OP.is_ge)
-            dma("y", "dyc", T.yc[:, :], T.YC[:, :], [B("YC")], [])
-        distances("CU", xr, "CKE", "TCH", 0, [[(3, 4)], [(4, 8)], [(8, 12)], [(12, 15), (15, 16)]], lambda: None, True)
-        tt(B("CB"), B("CF"), B("pcr", 256, 512), OP.add)
-        ts(B("TH"), B(ks, 0, 16), 0xFFF000, OP.bitwise_and)
-        ts(B("OLD"), B("TO"), 4095, OP.bitwise_and)
-        act(B("pcr", 0, 256), B(m, 0, 256), AF.Copy)
-        mm(B("pcnt", 0, 256), B("IDM"), B(xr, 0, 256), True, False)
-        mm(B("pcnt", 0, 256), B("IDM"), B(xr, 0, 256), False, False)
-        for q in range(4):
-            low = B("RB", 0, 64) if q == 0 else B("pcut", 64 * q, 64 * q + 64)
-            tt(low, B("pd%d" % q, 0, 64), B("CB", 64 * q, 64 * q + 64), OP.add)
-            if q == 0:
-                cp(B("RA", 0, 64), B("pd0", 0, 64))
-            else:
-                o = 64 * (q - 1)
-                tt(B("RA", o + 64, o + 128), B("RA", o, o + 64), B("pd%d" % q, 0, 64), OP.min)
-                tt(B("RB", o + 64, o + 128), B("RB", o, o + 64), low, OP.min)
-        for run in ("RA", "RB"):
-            tt(B(run, 0, 32), B(run, 192, 224), B(run, 224, 256), OP.min)
-        for j, run in enumerate(("RA", "RB")):
-            tt(B("EI", 16 * j, 16 * j + 16), B(run, 0, 16), B(run, 16, 32), OP.min)
-        tt(B("LT"), B("EI", 0, 16), B("TH"), OP.is_lt)
-        ts(B("ET"), B("EI", 0, 16), 3840, OP.bitwise_and)
-        ts(B("EM"), B("EI"), 255, OP.bitwise_and)
-        tt(B("JJ"), B("ET"), B("VS"), OP.add)
-        ts(B("N1"), B("EM", 0, 16), 256.0, OP.mult)
-        tt(B("PO"), B("JJ"), B("LT"), OP.mult)
-        tt(B("BN"), B("N1"), B("EM", 16, 32), OP.add)
-        cp(B("POU"), B("PO"))
-        tt(B("DL"), B("BN"), B("OLD"), OP.subtract)
-        sgat(B("GX"), B("D", 0, 4112), B("POU"))
-        mm(B("pcnt", 0, 256), B("IDM"), B("GX"), False, True)
-        act(B("XN"), B("pcnt", 0, 256), AF.Identity, bias=255.75)
-        tt(B("DT"), B("DL"), B("LT"), OP.mult)
-        act(B("XS%d" % r), B("XN"), AF.Identity, scale=0.5, bias=-128.0)
-        gat(B("UP"), B("DT"), B("REP"), B("OH"), OP.mult)
-        ms = "MS%d" % r
-        tt(B(ms, 0, 256), B("UP"), B("pcr", 0, 256), OP.add)
-        if last:
-            sgat(B("YX"), B("XS%d" % r), B("PERM"))
-            dma("y", "dyx", T.yx[:, :], T.YX[:, :], [B("YX")], [])
-            swap_in(B(ms, 0, 256), B("PERM2"))
-            swap_out("YP")
-            dma("y", "dyp", T.yp[:, :], T.YP[:, :], [B("YP")], [])
-            break
-        cp(B("PS%d" % r), B(ms, 0, 256))
-        need("g", [B("XS%d" % r), B("PS%d" % r)], [])
+            mm(B(p, 128, 256), B("IDC"), S("CFL"), True, False)
+            mm(B(p, 128, 256), B("IDM"), B("CK1"), False, True)
+            tt(S("C"), B(p, 128, 256), keys, OP.max)
+            scan(S("KS"), B("GOON", 0, 128), S("C"), OP.mult, OP.max)
+            keys, top = S("C"), S("KS")
+        mm(B(p, 384, 512), B("ID32"), S("MN"), True, True)
+        gat(S("OH"), top, B("END"), keys, OP.is_equal)
+        tt(S("PR", 1, 128), S("OH", 1, 128), B(p, 384, 511), OP.mult)
+        tt(S("PR", 128, 256), S("OH"), B(p, 384, 512), OP.mult)
+        scan(S("TO"), B("GOON", 0, 256), S("PR"), OP.mult, OP.add)
+        for h in range(2):
+            mm(B(p, 256 + 8 * h, 264 + 8 * h), MV("MVF", h, par), ends("TO", 0), h == 0, h == 1)
+        for h in range(2):
+            cp(S("TL", h, 16, 2), B(p, 256 + 8 * h, 264 + 8 * h))
+        gat(S("G"), B("PUW"), S("TL"))
+        turn(S("GT"), S("G"))
+        gat(S("CU"), S("GT"), B("RO", 8 * par, 8 * par + 8))
+        sgat(S("CF"), S("GT"), B("RO", 8 * par, 8 * par + 8))
+        digits(S("CF"))
+        act(S("LO"), B(m, 256, 384), AF.Copy)
+        dk = ends("KS" if r > 0 else "Y", 0)
+        ts(S("ST", 0, 8), dk, 2.0, OP.mult, -4096.0, OP.add)
+        ts(S("ST", 8, 16), dk, 2.0, OP.mult, 192.0 - 4096.0, OP.add)
+        tt(S("ST", 16, 24), S("ST", 0, 8), B("JM"), OP.add)
+        ts(S("SQ", 4, 40, 5), ends("TO", 1), -1.0, OP.mult, -20480.0, OP.add)
+        act(S("Z"), xin, AF.Identity, scale=0.5, bias=127.75)
+        act(S("TX", 4096, 4224), xin, AF.Identity, scale=0.5, bias=-128.0)
+        distances("CU" + e, 0, "LV", "CKE")
+        tt(S("X", 128, 256), pd, S("TA"), OP.add)
+        tt(S("X", 256, 384), pd, S("LO"), OP.add)
+        scan(S("Y", 0, 128), B("ANEW", 0, 128), pd, OP.max, OP.min)
+        scan(S("Y", 128, 384), B("ANEW"), S("X", 128, 384), OP.max, OP.min)
+        tt(S("TK"), ends("Y", 0), S("ST", 0, 8), OP.is_lt)
+        for at, j in ((0, 0), (2, 0), (1, 1), (3, 2)):
+            tt(S("SQ", at, 40, 5), ends("Y", j), S("ST", 8 * j, 8 * j + 8), OP.min)
+        gat(S("OT"), S("TK"), B("REP"), S("OH"), OP.mult)
+        scan(S("NM"), B("STEP"), S("SQ"), OP.mult, OP.add)
+        gat(S("UP"), S("NM"), B("REP5"), S("OT"), OP.mult)
+        ts(S("XL"), S("NM", 3, 40, 5), -20480.0, OP.add)
+        tt(S("MS"), S("UP"), B(p, 384, 512), OP.add)
+        gat(xs, S("TX"), S("XL"), S("Z"), OP.add)
+        if r == R - 1:
+            ts(S("YC"), tnew, 1000.0, OP.is_ge)
+            ts(S("YC"), S("YC"), col(16 + par), OP.mult)
+            return
+        ps = B("PS", o, o + 128)
+        cp(ps, S("MS"))
         rid, pid = topo.addr(nxt)[:2]
-        eg = topo.engines(core, nxt)
-        half = len(eg) // 2
-        masks = [sum(1 << e for e in eg[:half]), sum(1 << e for e in eg[half:])]
-        dst = [DstId(rid=rid, pnc=pid)]
-        a1, a2, a3 = "a1%d" % (r + 1), "a2%d" % (r + 1), "a3%d" % (r + 1)
-        g.remote_dma_fused([
-            RemoteDMATransfer(dst_ids=dst, dma_engine_mask=masks[0], remote_sem=T.sem[a1], src=T["XS%d" % r][:, :],
-                              dst=T["XR%d" % (r + 1)][:, 0:256]),
-            RemoteDMATransfer(dst_ids=dst, dma_engine_mask=masks[1], remote_sem=T.sem[a1], src=T["PS%d" % r][:, :],
-                              dst=T["PU%d" % (r + 1)][:, :])], local_sem=T.sem.ls)
-        sent += len(eg)
-        n = len(topo.engines(prv, core))
-        mark("rem", (a1, n), [], [B("XR%d" % (r + 1), 0, 256), B("PU%d" % (r + 1))])
-        ta = "TS%d" % r
-        prep(ms, ta)
-        need("g", [B(ta)], [])
-        g.remote_dma(T["TR%d" % (r + 1)][:, :], T[ta][:, :], T.sem[a3], T.sem.ls, pid, rid, topo.mask(core, nxt))
-        sent += len(eg)
-        mark("rem", (a3, n), [], [B("TR%d" % (r + 1))])
-        prep2(ms)
-        need("g", [B(ms)], [])
-        g.remote_dma(T["M%d" % (r + 1)][:, :], T[ms][:, :], T.sem[a2], T.sem.ls, pid, rid, topo.mask(core, nxt))
-        sent += len(eg)
-        mark("rem", (a2, n), [], [B("M%d" % (r + 1))])
-    g.wait_ge(T.sem.ls, sent)
+        eg, got = topo.engines(core, nxt), len(topo.engines(prv, core)) // 2
+        n = len(eg) // 2
+        moves = [("a1%s%d" % (e, r + 1), xs, B("XIN", o + 256, o + 384)), ("a2%s%d" % (e, r + 1), ps, B("PIN", o + 256, o + 384))]
+        remote([RemoteDMATransfer(dst_ids=[DstId(rid=rid, pnc=pid)], dma_engine_mask=sum(1 << x for x in eg[n * j:n * j + n]),
+                                  remote_sem=T.sem[sem], src=src[3], dst=dst[3]) for j, (sem, src, dst) in enumerate(moves)],
+               [xs, ps], [(sem, got, [dst]) for sem, _, dst in moves], 2)
+        sent[0] += len(eg)
+
+    for par in range(2):
+        second[0] = len(calls)
+        for r in range(R):
+            stream(par, r)
+    for par in range(2):
+        o = 128 * (2 * (R - 1) + par)
+        for c in range(8):
+            for h in range(2):
+                mm(B("wa0", 32 * c + 16 * h, 32 * c + 16 * h + 16), MV("MVB", h, par), B("XS", o + 16 * c, o + 16 * c + 16),
+                   par + c + h == 0, par + c + h == 9)
+    act(B("YX"), B("wa0", 0, 256), AF.Identity, scale=0.5, bias=-128.0)
+    dmas("dyx", [("s", T.yx[:, :], T.YX[:, :])], [B("YX")], [])
+    tt(B("YCF"), B("YCa"), B("YCb"), OP.add)
+    dmas("dyc", [("y", T.yc[:, :], T.YCF[:, :])], [B("YCF")], [])
+    gat(B("SW"), B("MS"), B("FIN"))
+    turn(B("YP"), B("SW"))
+    dmas("dyp", [("y", T.yp[:, :], T.YP[:, :])], [B("YP")], [])
+    issue_all()
+    g.wait_ge(T.sem.ls, sent[0])
     for e in "vstg":
         g.wait_ge(T.sem["q" + e], cnt[e])
-    for s in ("dx0", "dp0", "dtx", "dpu", "dt0", "dyp", "dyx", "dyc") + tuple("dc%d" % r for r in range(R)):
-        g.wait_ge(T.sem[s], 16)
+    for s in sorted(total):
+        g.wait_ge(T.sem[s], total[s])

@@ -5,7 +5,7 @@ R = 4
 BIG = 16384.0
 TOP = 2040 * 4096
 CYCLE, GATHER, HOP, DMA, REMOTE, MIB = 0.85, 1.2, 200.0, 1100.0, 1200.0, 3500.0
-LEAD, PE, CALL = 4000.0, 0.55, 40.0
+PE, CALL, PASSES, LEADS = 0.55, 40.0, 3, (1500.0, 2000.0, 2500.0, 3000.0, 3500.0, 4000.0, 5000.0)
 
 SCRATCH = {}
 SHARED = {
@@ -13,7 +13,7 @@ SHARED = {
                 "LAST 128 YX 256 FS 1024 FR 3072 IE 128 SPR 256 SELI 256 SEL 2048 XIN 1024 XS 1024",
     "int32": "PUW 4096 P0 256 I1 8 I2 8 I4 16 I5 16 I6 8 I7 8 I8 8 J3 8 J4 8 J5 8",
     "uint16": "RO 16 FIN 16 END 8 REP 8 REP5 8 PIN 1024 PS 1024",
-    "float32": "ID32 128 PD32 128 MVF 512 CL 128 JM 8 COL 24 P0F 256 SW 256 YP 256 YCF 256 GOON 384 ANEW 256 STEP 40",
+    "float32": "ID32 128 PD32 128 MVF 512 CL 128 JM 8 COL 24 P0F 256 SW 256 YP 256 YCF 256 GOON 256 ANEW 256 STEP 40",
 }
 OWN = {
     "bfloat16": "TX 4224 T0 1280 XT 128 D 2048 AB 2048 OA 1024 OB 1024 TA 128 FB 16 CFL 128",
@@ -36,7 +36,8 @@ SEMAPHORES = ["qv", "qs", "qt", "qg", "ls", "dx0", "dp0", "dpu", "dyp", "dyx", "
 SEMAPHORES += [a + e for a in ("dtx", "dt0") for e in "ab"]
 SEMAPHORES += ["%s%s%d" % (a, e, r) for a in ("a1", "a2", "fl", "dc") for e in "ab" for r in range(R)]
 
-WHO = "svss"
+WHO = "svsv"
+HELP = 3
 
 
 def rank_program(g, core, T, topo):
@@ -150,20 +151,40 @@ def rank_program(g, core, T, topo):
         way = [0.0] * len(calls)
         for i in range(len(calls) - 1, -1, -1):
             way[i] = max([t + way[j] for j, t in after[i].items()] + [calls[i][5]])
-        for i in range(second[0]):
-            way[i] += LEAD
-        there = [0.0] * len(calls)
-        busy = {e: [] for e in eng}
-        for i in sorted(range(len(calls)), key=lambda i: (-way[i], i)):
-            t, slots, k = there[i], busy[calls[i][0]], 0
-            while k < len(slots) and slots[k][0] < t + calls[i][4]:
-                t = max(t, slots[k][1])
-                k += 1
-            slots.insert(k, (t, t + calls[i][4]))
-            there[i] = t
+        n = len(calls)
+        before = [{} for _ in calls]
+        for i in range(n):
             for j, gap in after[i].items():
-                there[j] = max(there[j], t + gap)
-        for i in sorted(range(len(calls)), key=lambda i: (there[i], i)):
+                before[j][i] = gap + calls[j][4] - calls[i][4]
+
+        def place(order, nexts, first):
+            there, busy = list(first), {e: ([], []) for e in eng}
+            for i in order:
+                t, (starts, stops) = there[i], busy[calls[i][0]]
+                k = len(stops)
+                while k and stops[k - 1] > t:
+                    k -= 1
+                while k < len(starts) and starts[k] < t + calls[i][4]:
+                    t = max(t, stops[k])
+                    k += 1
+                starts.insert(k, t)
+                stops.insert(k, t + calls[i][4])
+                there[i] = t
+                for j, gap in nexts[i].items():
+                    there[j] = max(there[j], t + gap)
+            return there
+
+        best = None
+        for lead in LEADS:
+            order = sorted(range(n), key=lambda i: (-way[i] - (lead if i < second[0] else 0.0), i))
+            for _ in range(PASSES):
+                there = place(order, after, [0.0] * n)
+                end = max(there[i] + calls[i][5] for i in range(n))
+                if best is None or end < best[0]:
+                    best = (end, there)
+                back = place(sorted(range(n), key=lambda i: (-there[i] - calls[i][4], -i)), before, [c[5] - c[4] for c in calls])
+                order = sorted(range(n), key=lambda i: (-back[i] - calls[i][4], i))
+        for i in sorted(range(n), key=lambda i: (best[1][i], i)):
             calls[i][3]()
 
     def tt(out, a, b, o):
@@ -197,7 +218,9 @@ def rank_program(g, core, T, topo):
         op("v", [], [out], lambda: g.vector.memset(out[3], value))
 
     def act(out, a, f, scale=1.0, bias=0.0):
-        op("s", [a], [out], lambda: g.scalar.activation(out[3], a[3], f, bias=bias, scale=scale), 1.0, 0, 50)
+        column = isinstance(bias, tuple)
+        x = bias[3] if column else bias
+        op("s", [a, bias] if column else [a], [out], lambda: g.scalar.activation(out[3], a[3], f, bias=x, scale=scale), 1.0, 0, 50)
 
     def sgat(out, win, lst):
         op("s", [win, lst], [out], lambda: g.scalar.activation(out[3], win[3].indirect(lst[3]), AF.Copy), GATHER, 0, 80)
@@ -268,7 +291,7 @@ def rank_program(g, core, T, topo):
         for w in range(2):
             ts(col(5 + 2 * u + w), col(3 + u), col(0), OP.add, 16.0 * (w - u), OP.add)
             ident(MV("MVB", u, w), col(5 + 2 * u + w))
-            ident(MV("MVF", u, w), col(5 + 2 * u + w))
+            act(MV("MVF", u, w), MV("MVB", u, w), AF.Copy)
     tt(col(9), col(0), B("J4", 0, 1), OP.subtract)
     ts(col(10), B("J5", 0, 1), -2.0, OP.mult, 1.0, OP.add)
     ts(col(11), col(9), 15.0, OP.add)
@@ -279,25 +302,26 @@ def rank_program(g, core, T, topo):
     for c in range(8):
         ts(B("SEL", 256 * c, 256 * c + 256), B("SELI"), col(0), OP.subtract, -16.0 * c, OP.is_equal)
     ts(B("LW"), B("IOM"), col(11), OP.is_equal, 4096.0, OP.mult)
-    ts(B("LV"), B("IOM"), col(11), OP.is_equal, 8192.0, OP.mult)
+    act(B("LV"), B("LW"), AF.Copy, scale=2.0)
     ts(B("IM"), B("IOM", 0, 128), col(14), OP.subtract)
-    for name, value in (("IDM", None), ("ID32", None), ("IDB", BIG), ("IDC", float(TOP)), ("IDP", 128.0), ("IDQ", -128.0)):
-        ident(B(name), col(0), value)
+    ident(B("IDM"), col(0))
+    for name, value in (("ID32", 1.0), ("IDB", BIG), ("IDC", float(TOP)), ("IDP", 128.0), ("IDQ", -128.0)):
+        act(B(name), B("IDM"), AF.Copy, scale=value)
     ident(B("PD32"), col(12))
-    tt(B("PD32"), B("ID32"), B("PD32"), OP.subtract)
+    tt(B("PD32"), B("IDM"), B("PD32"), OP.subtract)
     for j in range(2):
         ts(B("SPR", 128 * j, 128 * j + 128), B("IE"), col(15 * j), OP.is_equal, BIG, OP.mult)
     tt(B("JM"), B("I2"), B("J4"), OP.add)
-    for name, value, at, step, there in (("LAST", 0.0, 15, 16, 8192.0), ("GOON", 1.0, 0, 16, 0.0), ("ANEW", 0.0, 0, 16, 33554432.0)):
-        fill(B(name), value)
-        fill(B(name, at, None, step), there)
+    act(B("LAST"), B("SELI", 0, 128), AF.Relu, scale=8192.0, bias=-14.0 * 8192.0)
+    act(B("GOON"), B("SELI"), AF.Sign)
+    act(B("ANEW"), B("SELI"), AF.Relu, scale=-33554432.0, bias=33554432.0)
+    act(B("NEG"), B("SELI"), AF.Identity, scale=0.0, bias=-1.0)
+    act(B("C160"), B("SELI", 0, 128), AF.Identity, scale=0.0, bias=160.0)
     for j, value in enumerate((0.0, -1.0, -128.0, -1.0, 1.0)):
         fill(B("STEP", j, None, 5), value)
     fill(B("CL", 0, None, 16), 0.0)
-    cp(B("CK1"), B("CKC"))
+    act(B("CK1"), B("CKC"), AF.Copy)
     fill(B("CK1", 0, None, 16), -2.0 * TOP)
-    fill(B("NEG"), -1.0)
-    fill(B("C160"), 160.0)
     cp(B("P0F"), B("P0"))
     turn(B("SW"), B("P0F"))
     for par, e in enumerate("ab"):
@@ -316,7 +340,7 @@ def rank_program(g, core, T, topo):
     def stream(par, r):
         e = "ab"[par]
         o = 128 * (2 * r + par)
-        p, m, w = "p" + e, "m" + e, "w%s0" % e
+        p, m, w, w1 = "p" + e, "m" + e, "w%s0" % e, "w%s1" % e
         told, tnew = B("T0" + e, 256 * r, 256 * r + 256), B("T0" + e, 256 * r + 256, 256 * r + 512)
         fs, xin, xs = B("FS", o, o + 128), B("XIN", o, o + 128), B("XS", o, o + 128)
         tx, pd = B("TX" + e, 0, 4096), B(p, 0, 128)
@@ -329,13 +353,13 @@ def rank_program(g, core, T, topo):
 
         def digits(src):
             act(S("TA"), src, AF.Identity, scale=1.0 / 128.0, bias=159.502)
-            mm(B(m, 256, 384), B("ID32"), src, True, False)
-            mm(B(m, 256, 384), B("IDP"), B("C160"), False, False)
-            mm(B(m, 256, 384), B("IDQ"), S("TA"), False, True)
+            mm(B(p, 256, 384), B("ID32"), src, True, False)
+            mm(B(p, 256, 384), B("IDP"), B("C160"), False, False)
+            mm(B(p, 256, 384), B("IDQ"), S("TA"), False, True)
 
-        def distances(lst, l0, lw, code):
+        def distances(lst, l0, lw, code, banks):
             for q, who in enumerate(WHO):
-                d, bank = S("D", 512 * q, 512 * q + 512), "w%s%d" % (e, q % 2)
+                d, bank = S("D", 512 * q, 512 * q + 512), banks[q % 3]
                 (sgat if who == "s" else gat)(d, tx, B(lst, l0 + 32 * q, l0 + 32 * q + 32))
                 for j in range(2):
                     mm(B(bank, 256 * j, 256 * j + 256), S("XT"), B("SEL", 512 * q + 256 * j, 512 * q + 256 * j + 256), j == 0, False)
@@ -351,25 +375,31 @@ def rank_program(g, core, T, topo):
         act(S("XT"), B(m, 384, 512), AF.Identity, scale=-0.5, bias=128.0)
         if r > 0:
             cp(S("MN"), B("PIN", o, o + 128))
-        mm(B(m, 0, 128), B("PD32"), S("MN"), True, False)
-        mm(B(m, 0, 128), B("IDM"), B("LAST"), False, True)
-        act(S("NE"), B(m, 0, 128), AF.Abs, scale=16777216.0)
+        mm(pd, B("PD32"), S("MN"), True, False)
+        mm(pd, B("IDM"), B("LAST"), False, True)
+        act(S("NE"), pd, AF.Abs, scale=16777216.0)
         digits(S("MN"))
-        mm(B(m, 128, 256), B("IDM"), S("TA"), True, True)
+        mm(B(p, 128, 256), B("IDM"), S("TA"), True, True)
         scan(S("EL"), B("GOON", 0, 128), S("NE"), OP.mult, OP.max)
         tt(S("BND"), S("EL"), B("CL"), OP.min)
-        distances("PIN", o, "LW", "CKC")
+        distances("PIN", o, "LW", "CKC", (w, w1, m))
         tt(S("X", 0, 128), pd, S("BND"), OP.min)
+        for j in (1, 2):
+            tt(S("X", 128 * j, 128 * j + 128), S("X", 0, 128), B(p, 128 * j, 128 * j + 128), OP.add)
         if r > 0:
             act(S("CFL"), pd, AF.Sign, bias=-16777216.0)
-        for j in (1, 2):
-            tt(S("X", 128 * j, 128 * j + 128), S("X", 0, 128), B(m, 128 * j, 128 * j + 128), OP.add)
-        scan(S("Y"), B("GOON"), S("X"), OP.mult, OP.max)
+        scan(S("Y", 0, 128), B("GOON", 0, 128), S("X", 0, 128), OP.mult, OP.max)
+        scan(S("Y", 128, 384), B("GOON", 0, 256), S("X", 128, 384), OP.mult, OP.max)
         for j in (1, 2):
             tt(S("FB", 8 * j - 8, 8 * j), ends("Y", j), ends("Y", 0), OP.subtract)
         for c in range(8):
-            ts(S("OA", 128 * c, 128 * c + 128), B("IM"), S("FB", c, c + 1), OP.is_equal)
+            if c < 8 - HELP:
+                ts(S("OA", 128 * c, 128 * c + 128), B("IM"), S("FB", c, c + 1), OP.is_equal)
+            else:
+                act(S("D", 128 * c, 128 * c + 128), B("IM"), AF.Abs, scale=-1.0, bias=S("FB", c, c + 1))
             ts(S("OB", 128 * c, 128 * c + 128), B("IOM", 0, 128), S("FB", 8 + c, 9 + c), OP.is_equal)
+        if HELP:
+            act(S("OA", 1024 - 128 * HELP, 1024), S("D", 1024 - 128 * HELP, 1024), AF.Relu, scale=-1.0, bias=1.0)
         for c in range(8):
             mm(B(w, 0, 128), S("OA", 128 * c, 128 * c + 128), S("OB", 128 * c, 128 * c + 128), c == 0, c == 7)
         act(fs, B(w, 0, 128), AF.Sign)
@@ -392,9 +422,9 @@ def rank_program(g, core, T, topo):
         dmas("dc%s%d" % (e, r), [("y", T.TX[0:128:16, 4224 * par:4224 * par + 4096], tnew[3])], [tnew], [tx])
         keys, top = S("X", 0, 128), S("Y", 0, 128)
         if r > 0:
-            mm(B(p, 128, 256), B("IDC"), S("CFL"), True, False)
-            mm(B(p, 128, 256), B("IDM"), B("CK1"), False, True)
-            tt(S("C"), B(p, 128, 256), keys, OP.max)
+            mm(B(m, 128, 256), B("IDC"), S("CFL"), True, False)
+            mm(B(m, 128, 256), B("IDM"), B("CK1"), False, True)
+            tt(S("C"), B(m, 128, 256), keys, OP.max)
             scan(S("KS"), B("GOON", 0, 128), S("C"), OP.mult, OP.max)
             keys, top = S("C"), S("KS")
         mm(B(p, 384, 512), B("ID32"), S("MN"), True, True)
@@ -403,15 +433,15 @@ def rank_program(g, core, T, topo):
         tt(S("PR", 128, 256), S("OH"), B(p, 384, 512), OP.mult)
         scan(S("TO"), B("GOON", 0, 256), S("PR"), OP.mult, OP.add)
         for h in range(2):
-            mm(B(p, 256 + 8 * h, 264 + 8 * h), MV("MVF", h, par), ends("TO", 0), h == 0, h == 1)
+            mm(B(m, 256 + 8 * h, 264 + 8 * h), MV("MVF", h, par), ends("TO", 0), h == 0, h == 1)
         for h in range(2):
-            cp(S("TL", h, 16, 2), B(p, 256 + 8 * h, 264 + 8 * h))
+            cp(S("TL", h, 16, 2), B(m, 256 + 8 * h, 264 + 8 * h))
         gat(S("G"), B("PUW"), S("TL"))
         turn(S("GT"), S("G"))
         gat(S("CU"), S("GT"), B("RO", 8 * par, 8 * par + 8))
         sgat(S("CF"), S("GT"), B("RO", 8 * par, 8 * par + 8))
         digits(S("CF"))
-        act(S("LO"), B(m, 256, 384), AF.Copy)
+        act(S("LO"), B(p, 256, 384), AF.Copy)
         dk = ends("KS" if r > 0 else "Y", 0)
         ts(S("ST", 0, 8), dk, 2.0, OP.mult, -4096.0, OP.add)
         ts(S("ST", 8, 16), dk, 2.0, OP.mult, 192.0 - 4096.0, OP.add)
@@ -419,7 +449,7 @@ def rank_program(g, core, T, topo):
         ts(S("SQ", 4, 40, 5), ends("TO", 1), -1.0, OP.mult, -20480.0, OP.add)
         act(S("Z"), xin, AF.Identity, scale=0.5, bias=127.75)
         act(S("TX", 4096, 4224), xin, AF.Identity, scale=0.5, bias=-128.0)
-        distances("CU" + e, 0, "LV", "CKE")
+        distances("CU" + e, 0, "LV", "CKE", (w1, m, w))
         tt(S("X", 128, 256), pd, S("TA"), OP.add)
         tt(S("X", 256, 384), pd, S("LO"), OP.add)
         scan(S("Y", 0, 128), B("ANEW", 0, 128), pd, OP.max, OP.min)

@@ -4,22 +4,22 @@ from concourse.mybir import AluOpType, ActivationFunctionType
 R = 4
 BIG = 16384.0
 TOP = 2040 * 4096
-CYCLE, GATHER, HOP, DMA, REMOTE, MIB = 0.85, 1.2, 200.0, 1100.0, 1200.0, 3500.0
+CYCLE, GATHER, HOP, DMA, REMOTE, MIB = 0.85, 1.3, 220.0, 1100.0, 1200.0, 3500.0
 PE, CALL, PASSES, LEADS = 0.55, 40.0, 3, (1500.0, 2000.0, 2500.0, 3000.0, 3500.0, 4000.0, 5000.0)
 
 SCRATCH = {}
 SHARED = {
-    "bfloat16": "X0 256 LW 144 LV 144 IDM 128 IDB 128 IDC 128 IDP 128 IDQ 128 MVB 512 IOM 144 IM 128 CKC 128 CKE 128 CK1 128 NEG 256 C160 128 "
-                "LAST 128 YX 256 FS 1024 FR 3072 IE 128 SPR 256 SELI 256 SEL 2048 XIN 1024 XS 1024",
-    "int32": "PUW 4096 P0 256 I1 8 I2 8 I4 16 I5 16 I6 8 I7 8 I8 8 J3 8 J4 8 J5 8",
-    "uint16": "RO 16 FIN 16 END 8 REP 8 REP5 8 PIN 1024 PS 1024",
-    "float32": "ID32 128 PD32 128 MVF 512 CL 128 JM 8 COL 24 P0F 256 SW 256 YP 256 YCF 256 GOON 256 ANEW 256 STEP 40",
+    "bfloat16": "X0 256 LW 144 LV 144 IDM 128 IDB 128 IDC 128 PDH 128 PDL 128 MVB 512 IOM 144 IM 128 CKC 128 CKE 128 IDP 128 NEG 128 "
+                "CM 128 PRE 3072 PRS 3072 YX 256 FS 1024 FR 3072 SELI 256 SEL 2048 XIN 1024 XS 1024",
+    "int32": "PUW 4096 P0 256 I1 8 I2 8 I4 16 I5 16 I6 8 I7 8 I8 8 J3 8 J4 8 J5 8 J6 8 J7 8",
+    "uint16": "RO 16 FIN 16 END 8 REP 8 REP5 8 PICK 4 PIN 1024 PS 1024",
+    "float32": "MVF 512 CL 128 JM 8 COL 24 P0F 256 SW 256 YP 256 YCF 256 GOON 256 ANEW 256 STEP 64",
 }
 OWN = {
-    "bfloat16": "TX 4224 T0 1280 XT 128 D 2048 AB 2048 OA 1024 OB 1024 TA 128 FB 16 CFL 128",
+    "bfloat16": "TX 4224 T0 640 XT 128 D 2048 AB 2048 OA 1024 OB 1024 TA 128 FB 32 CFL 128 LO 128",
     "uint16": "TL 16 CU 128 XL 8",
-    "float32": "NE 128 EL 128 BND 128 LO 128 X 384 Y 384 C 128 KS 128 OH 128 PR 256 TO 256 G 256 GT 256 CF 128 ST 24 Z 128 SQ 40 NM 40 TK 8 "
-               "OT 128 UP 128 YC 256 MN 128 MS 128",
+    "float32": "NE 136 EL 128 X 384 Y 384 C 128 KS 8 OH 128 PR 256 TO 256 G 256 GT 256 CF 128 ST 64 Z 128 SQ 64 NM 64 TK 8 "
+               "OT 128 UP 128 YC 128 MS 128",
 }
 SIDE = {}
 for _t, _k in ((SHARED, 1), (OWN, 2)):
@@ -32,11 +32,11 @@ for _t, _k in ((SHARED, 1), (OWN, 2)):
 for _n in ("pa", "pb", "ma", "mb", "wa0", "wa1", "wb0", "wb1"):
     SCRATCH[_n] = ("psum", [128, 512], "float32")
 
-SEMAPHORES = ["qv", "qs", "qt", "qg", "ls", "dx0", "dp0", "dpu", "dyp", "dyx", "dyc"]
-SEMAPHORES += [a + e for a in ("dtx", "dt0") for e in "ab"]
-SEMAPHORES += ["%s%s%d" % (a, e, r) for a in ("a1", "a2", "fl", "dc") for e in "ab" for r in range(R)]
+SEMAPHORES = ["qv", "qs", "qt", "qg", "ls", "dx0", "dp0", "dpu", "dyp", "dyx"]
+SEMAPHORES += [a + e for a in ("dtx", "dt0", "dyc") for e in "ab"]
+SEMAPHORES += ["%s%s%d" % (a, e, r) for a in ("a1", "a2", "a3", "fl", "dc") for e in "ab" for r in range(R)]
 
-WHO = "svsv"
+WHO = ("svsv", "svsv")
 HELP = 3
 
 
@@ -191,13 +191,13 @@ def rank_program(g, core, T, topo):
         op("v", [a, b], [out], lambda: g.vector.tensor_tensor(out[3], a[3], b[3], o), 1.0 if psum(a[0]) or psum(b[0]) else 2.0)
 
     def ts(out, a, s1, o1, s2=None, o2=None):
-        reads = [a] + [s for s in (s1,) if isinstance(s, tuple)]
-        x = s1[3] if isinstance(s1, tuple) else s1
+        reads = [a] + [s for s in (s1, s2) if isinstance(s, tuple)]
+        x, y = (s[3] if isinstance(s, tuple) else s for s in (s1, s2))
         each = 0.5 if short(out, a) else 1.0
         if o2 is None:
             op("v", reads, [out], lambda: g.vector.tensor_scalar(out[3], a[3], x, None, o1), each)
         else:
-            op("v", reads, [out], lambda: g.vector.tensor_scalar(out[3], a[3], x, s2, o1, o2), each)
+            op("v", reads, [out], lambda: g.vector.tensor_scalar(out[3], a[3], x, y, o1, o2), each)
 
     def cp(out, a):
         op("v", [a], [out], lambda: g.vector.tensor_copy(out[3], a[3]))
@@ -245,13 +245,12 @@ def rank_program(g, core, T, topo):
         dmas("dtx" + e, [("ys"[h], T.TX[32 * a + 16 * h:32 * a + 16 * h + 16, 4224 * par:4224 * par + 4096],
                           T.tx[32 * a + 16 * par:32 * a + 16 * par + 16, :]) for a in range(4) for h in range(2)],
              [], [B("TX" + e, 0, 4096)], DMA + MIB * (par + 1))
+    for par, e in enumerate("ab"):
+        dmas("dt0" + e, [("s", B("T0" + e, 0, 128)[3], T.tx[16 * par:128:32, :])], [], [B("T0" + e, 0, 128)], DMA + MIB * 2)
     dmas("dpu", [("y", T.PUW[:, :], T.pu[:, :])], [], [B("PUW")], DMA + MIB * 4)
     for i, c in enumerate(calls):
         c[3]()
         calls[i] = c[:3] + (lambda: None,) + c[4:]
-    for par, e in enumerate("ab"):
-        dmas("dt0" + e, [("y", B("T0" + e, 0, 256)[3], T.TX[0:128:16, 4224 * par:4224 * par + 4096])], [B("TX" + e, 0, 4096)],
-             [B("T0" + e, 0, 256)], DMA + MIB * 2)
 
     iota("I1", [[0, 8]], 0, 1)
     iota("IOM", [[1, 144]], 0, 0)
@@ -264,8 +263,7 @@ def rank_program(g, core, T, topo):
     iota("I5", [[16, 8], [128, 2]], 0, 0)
     iota("I6", [[16, 8]], 15, 0)
     iota("I7", [[1, 8]], 0, 0)
-    iota("I8", [[5, 8]], 4, 0)
-    iota("IE", [[32, 4], [0, 2], [2, 16]], 0, 0)
+    iota("I8", [[8, 8]], 5, 0)
 
     def col(j):
         return B("COL", j, j + 1)
@@ -287,7 +285,6 @@ def rank_program(g, core, T, topo):
         cp(B(name), B(src))
     for u in range(2):
         ts(col(3 + u), B("J3", 0, 1), 16.0 * u, OP.not_equal, 1000.0, OP.mult)
-        ts(col(16 + u), B("J3", 0, 1), 16.0 * u, OP.is_equal)
         for w in range(2):
             ts(col(5 + 2 * u + w), col(3 + u), col(0), OP.add, 16.0 * (w - u), OP.add)
             ident(MV("MVB", u, w), col(5 + 2 * u + w))
@@ -298,35 +295,40 @@ def rank_program(g, core, T, topo):
     tt(col(12), col(10), col(0), OP.add)
     tt(col(13), col(9), B("J3", 0, 1), OP.subtract)
     ts(col(14), col(13), -160.0, OP.add)
-    ts(col(15), col(0), -1.0, OP.add)
     for c in range(8):
         ts(B("SEL", 256 * c, 256 * c + 256), B("SELI"), col(0), OP.subtract, -16.0 * c, OP.is_equal)
     ts(B("LW"), B("IOM"), col(11), OP.is_equal, 4096.0, OP.mult)
     act(B("LV"), B("LW"), AF.Copy, scale=2.0)
     ts(B("IM"), B("IOM", 0, 128), col(14), OP.subtract)
     ident(B("IDM"), col(0))
-    for name, value in (("ID32", 1.0), ("IDB", BIG), ("IDC", float(TOP)), ("IDP", 128.0), ("IDQ", -128.0)):
+    for name, value in (("IDB", BIG), ("IDC", float(TOP)), ("IDP", 128.0)):
         act(B(name), B("IDM"), AF.Copy, scale=value)
-    ident(B("PD32"), col(12))
-    tt(B("PD32"), B("IDM"), B("PD32"), OP.subtract)
-    for j in range(2):
-        ts(B("SPR", 128 * j, 128 * j + 128), B("IE"), col(15 * j), OP.is_equal, BIG, OP.mult)
+    ident(B("PDH"), col(12))
+    tt(B("PDL"), B("IDM"), B("PDH"), OP.subtract)
+    act(B("PDH"), B("PDL"), AF.Copy, scale=128.0)
     tt(B("JM"), B("I2"), B("J4"), OP.add)
-    act(B("LAST"), B("SELI", 0, 128), AF.Relu, scale=8192.0, bias=-14.0 * 8192.0)
+    act(B("CM"), B("SELI", 0, 128), AF.Identity, scale=0.0, bias=-20480.0)
     act(B("GOON"), B("SELI"), AF.Sign)
     act(B("ANEW"), B("SELI"), AF.Relu, scale=-33554432.0, bias=33554432.0)
-    act(B("NEG"), B("SELI"), AF.Identity, scale=0.0, bias=-1.0)
-    act(B("C160"), B("SELI", 0, 128), AF.Identity, scale=0.0, bias=160.0)
-    for j, value in enumerate((0.0, -1.0, -128.0, -1.0, 1.0)):
-        fill(B("STEP", j, None, 5), value)
-    fill(B("CL", 0, None, 16), 0.0)
-    act(B("CK1"), B("CKC"), AF.Copy)
-    fill(B("CK1", 0, None, 16), -2.0 * TOP)
+    act(B("NEG"), B("SELI", 0, 128), AF.Identity, scale=0.0, bias=-1.0)
+    for j, value in enumerate((0.0, -1.0, -128.0, 1.0, -1.0, -1.0, 0.0, 0.0)):
+        fill(B("STEP", j, None, 8), value)
+    fill(B("ST"), 0.0)
+    ts(B("J6"), B("I1"), 7, OP.bitwise_and)
+    ts(B("J7"), B("I1"), 8, OP.bitwise_and)
+    ts(col(18), B("J6", 0, 1), 0.0, OP.is_equal, 128.0, OP.mult)
+    ts(col(19), B("J6", 0, 1), 3.0, OP.is_equal, 256.0, OP.mult)
+    ts(col(20), B("J7", 0, 1), 2.0, OP.mult, 15.0, OP.add)
+    tt(col(21), col(18), col(19), OP.add)
+    tt(col(22), col(20), col(21), OP.add)
+    ts(B("PICK"), B("I4", 0, 4), col(22), OP.add)
+    fill(B("CKC", 0, None, 16), -1073741824.0)
     cp(B("P0F"), B("P0"))
     turn(B("SW"), B("P0F"))
     for par, e in enumerate("ab"):
         fill(B("PR" + e, 0, 8), 0.0)
-        gat(B("MN" + e), B("SW"), B("RO", 8 * par, 8 * par + 8))
+        fill(B("NE" + e, 0, 1), 0.0)
+        sgat(B("MS" + e), B("SW"), B("RO", 8 * par, 8 * par + 8))
         gat(B("PIN", 128 * par, 128 * par + 128), B("SW"), B("RO", 8 * par, 8 * par + 8))
         for c in range(8):
             for h in range(2):
@@ -341,7 +343,7 @@ def rank_program(g, core, T, topo):
         e = "ab"[par]
         o = 128 * (2 * r + par)
         p, m, w, w1 = "p" + e, "m" + e, "w%s0" % e, "w%s1" % e
-        told, tnew = B("T0" + e, 256 * r, 256 * r + 256), B("T0" + e, 256 * r + 256, 256 * r + 512)
+        told, tnew = B("T0" + e, 128 * r, 128 * r + 128), B("T0" + e, 128 * r + 128, 128 * r + 256)
         fs, xin, xs = B("FS", o, o + 128), B("XIN", o, o + 128), B("XS", o, o + 128)
         tx, pd = B("TX" + e, 0, 4096), B(p, 0, 128)
 
@@ -351,18 +353,24 @@ def rank_program(g, core, T, topo):
         def ends(name, j):
             return S(name, 128 * j + 15, 128 * j + 128, 16)
 
-        def digits(src):
-            act(S("TA"), src, AF.Identity, scale=1.0 / 128.0, bias=159.502)
-            mm(B(p, 256, 384), B("ID32"), src, True, False)
-            mm(B(p, 256, 384), B("IDP"), B("C160"), False, False)
-            mm(B(p, 256, 384), B("IDQ"), S("TA"), False, True)
+        def digits(src, high, low):
+            act(high, src, AF.Identity, scale=1.0 / 128.0, bias=159.502)
+            act(B(p, 256, 384), high, AF.Identity, scale=-128.0, bias=20480.0)
+            tt(low, B(p, 256, 384), src, OP.add)
 
-        def distances(lst, l0, lw, code, banks):
-            for q, who in enumerate(WHO):
+        def prepare(src, buf, at):
+            high, low = B(buf, at, at + 128), B(buf, at + 128, at + 256)
+            digits(src, high, low)
+            mm(B(p, 128, 256), B("PDH"), high, True, False)
+            mm(B(p, 128, 256), B("PDL"), low, False, True)
+            act(S("NE", 1, 129), B(p, 128, 256), AF.Abs)
+            scan(B(buf, at + 256, at + 384), S("NE", 0, 128), B("GOON", 0, 128), OP.max, OP.min)
+
+        def distances(lst, l0, lw, code, banks, whos):
+            for q, who in enumerate(whos):
                 d, bank = S("D", 512 * q, 512 * q + 512), banks[q % 3]
                 (sgat if who == "s" else gat)(d, tx, B(lst, l0 + 32 * q, l0 + 32 * q + 32))
-                for j in range(2):
-                    mm(B(bank, 256 * j, 256 * j + 256), S("XT"), B("SEL", 512 * q + 256 * j, 512 * q + 256 * j + 256), j == 0, False)
+                mm(B(bank), S("XT"), B("SEL", 512 * q, 512 * q + 512), True, False)
                 mm(B(bank), B("IDM"), d, False, True)
                 act(S("AB", 512 * q, 512 * q + 512), B(bank), AF.Abs)
             mm(pd, B("IDM"), B(code), True, False)
@@ -372,24 +380,18 @@ def rank_program(g, core, T, topo):
                        half + s == 16)
 
         mm(B(m, 384, 512), xin, B("IDM"), True, True)
-        act(S("XT"), B(m, 384, 512), AF.Identity, scale=-0.5, bias=128.0)
-        if r > 0:
-            cp(S("MN"), B("PIN", o, o + 128))
-        mm(pd, B("PD32"), S("MN"), True, False)
-        mm(pd, B("IDM"), B("LAST"), False, True)
-        act(S("NE"), pd, AF.Abs, scale=16777216.0)
-        digits(S("MN"))
-        mm(B(p, 128, 256), B("IDM"), S("TA"), True, True)
-        scan(S("EL"), B("GOON", 0, 128), S("NE"), OP.mult, OP.max)
-        tt(S("BND"), S("EL"), B("CL"), OP.min)
-        distances("PIN", o, "LW", "CKC", (w, w1, m))
-        tt(S("X", 0, 128), pd, S("BND"), OP.min)
-        for j in (1, 2):
-            tt(S("X", 128 * j, 128 * j + 128), S("X", 0, 128), B(p, 128 * j, 128 * j + 128), OP.add)
+        ts(S("XT"), B(m, 384, 512), -0.5, OP.mult, 128.0, OP.add)
+        if r == 0:
+            prepare(S("MS"), "PRE", 3 * o)
+        high, low, goon = (B("PRE", 3 * o + 128 * j, 3 * o + 128 * j + 128) for j in range(3))
+        distances("PIN", o, "LW", "CKC", (w, w1, m), WHO[0])
+        for j, digit in ((1, high), (2, low)):
+            tt(S("X", 128 * j, 128 * j + 128), pd, digit, OP.add)
+        for j in range(3):
+            scan(S("Y", 128 * j, 128 * j + 128), goon, S("X", 128 * j, 128 * j + 128) if j else pd, OP.mult, OP.max)
         if r > 0:
             act(S("CFL"), pd, AF.Sign, bias=-16777216.0)
-        scan(S("Y", 0, 128), B("GOON", 0, 128), S("X", 0, 128), OP.mult, OP.max)
-        scan(S("Y", 128, 384), B("GOON", 0, 256), S("X", 128, 384), OP.mult, OP.max)
+            ts(S("FB", 16, 24), ends("Y", 0), 16777216.0, OP.is_lt)
         for j in (1, 2):
             tt(S("FB", 8 * j - 8, 8 * j), ends("Y", j), ends("Y", 0), OP.subtract)
         for c in range(8):
@@ -397,7 +399,8 @@ def rank_program(g, core, T, topo):
                 ts(S("OA", 128 * c, 128 * c + 128), B("IM"), S("FB", c, c + 1), OP.is_equal)
             else:
                 act(S("D", 128 * c, 128 * c + 128), B("IM"), AF.Abs, scale=-1.0, bias=S("FB", c, c + 1))
-            ts(S("OB", 128 * c, 128 * c + 128), B("IOM", 0, 128), S("FB", 8 + c, 9 + c), OP.is_equal)
+            ts(S("OB", 128 * c, 128 * c + 128), B("IOM", 0, 128), S("FB", 8 + c, 9 + c), OP.is_equal,
+               S("FB", 16 + c, 17 + c) if r else 1.0, OP.mult)
         if HELP:
             act(S("OA", 1024 - 128 * HELP, 1024), S("D", 1024 - 128 * HELP, 1024), AF.Relu, scale=-1.0, bias=1.0)
         for c in range(8):
@@ -414,58 +417,57 @@ def rank_program(g, core, T, topo):
                                   dsts=dsts)], [fs],
                [(fl, sum(len(topo.engines(T.cores[q], core)) for q in others), [B("FR", 3 * o, 3 * o + 384)])], 3)
         sent[0] += len(topo.engines(core, T.cores[others[0]]))
-        mm(B(w, 128, 384), B("IDB"), B("NEG"), True, False)
-        for i, mp in enumerate([fs] + [B("FR", 3 * o + 128 * j, 3 * o + 128 * j + 128) for j in range(3)]):
-            for j in range(2):
-                mm(B(w, 128 + 128 * j, 256 + 128 * j), B("SPR", 128 * j, 128 * j + 128), mp, False, i + j == 4)
-        tt(tnew, B(w, 128, 384), told, OP.max)
-        dmas("dc%s%d" % (e, r), [("y", T.TX[0:128:16, 4224 * par:4224 * par + 4096], tnew[3])], [tnew], [tx])
-        keys, top = S("X", 0, 128), S("Y", 0, 128)
-        if r > 0:
+        for i, mp in enumerate([B("NEG"), fs] + [B("FR", 3 * o + 128 * j, 3 * o + 128 * j + 128) for j in range(3)]):
+            mm(B(w, 128, 256), B("IDB"), mp, i == 0, i == 4)
+        tt(tnew, B(w, 128, 256), told, OP.max)
+        dmas("dc%s%d" % (e, r), [("y", T.TX[16 * h:128:32, 4224 * par:4224 * par + 4096], tnew[3]) for h in range(2)], [tnew], [tx], DMA + 200.0)
+        for j, (lhs, rhs) in enumerate(((B("IDP"), high), (B("IDM"), low), (B("IDM"), B("CM")))):
+            mm(B(p, 384, 512), lhs, rhs, j == 0, j == 2)
+        if r == 0:
+            dk = ends("Y", 1)
+            gat(S("OH"), S("Y", 128, 256), B("END"), S("X", 128, 256), OP.is_equal)
+        else:
+            dk = S("KS")
             mm(B(m, 128, 256), B("IDC"), S("CFL"), True, False)
-            mm(B(m, 128, 256), B("IDM"), B("CK1"), False, True)
-            tt(S("C"), B(m, 128, 256), keys, OP.max)
-            scan(S("KS"), B("GOON", 0, 128), S("C"), OP.mult, OP.max)
-            keys, top = S("C"), S("KS")
-        mm(B(p, 384, 512), B("ID32"), S("MN"), True, True)
-        gat(S("OH"), top, B("END"), keys, OP.is_equal)
+            mm(B(m, 128, 256), B("IDM"), B("CKC"), False, True)
+            scan(S("EL"), B("GOON", 0, 128), B(m, 128, 256), OP.mult, OP.max)
+            tt(S("C"), S("X", 128, 256), B("CL"), OP.min)
+            ts(S("TK"), ends("Y", 1), float(TOP), OP.min)
+            tt(dk, ends("EL", 0), S("TK"), OP.max)
+            gat(S("OH"), dk, B("REP"), S("C"), OP.is_equal)
         tt(S("PR", 1, 128), S("OH", 1, 128), B(p, 384, 511), OP.mult)
         tt(S("PR", 128, 256), S("OH"), B(p, 384, 512), OP.mult)
         scan(S("TO"), B("GOON", 0, 256), S("PR"), OP.mult, OP.add)
         for h in range(2):
-            mm(B(m, 256 + 8 * h, 264 + 8 * h), MV("MVF", h, par), ends("TO", 0), h == 0, h == 1)
-        for h in range(2):
-            cp(S("TL", h, 16, 2), B(m, 256 + 8 * h, 264 + 8 * h))
+            mm(B(m, 256 + h, 272, 2), MV("MVF", h, par), ends("TO", 0), h == 0, h == 1)
+        cp(S("TL"), B(m, 256, 272))
         gat(S("G"), B("PUW"), S("TL"))
         turn(S("GT"), S("G"))
         gat(S("CU"), S("GT"), B("RO", 8 * par, 8 * par + 8))
         sgat(S("CF"), S("GT"), B("RO", 8 * par, 8 * par + 8))
-        digits(S("CF"))
-        act(S("LO"), B(p, 256, 384), AF.Copy)
-        dk = ends("KS" if r > 0 else "Y", 0)
-        ts(S("ST", 0, 8), dk, 2.0, OP.mult, -4096.0, OP.add)
-        ts(S("ST", 8, 16), dk, 2.0, OP.mult, 192.0 - 4096.0, OP.add)
-        tt(S("ST", 16, 24), S("ST", 0, 8), B("JM"), OP.add)
-        ts(S("SQ", 4, 40, 5), ends("TO", 1), -1.0, OP.mult, -20480.0, OP.add)
+        digits(S("CF"), S("TA"), S("LO"))
+        for at, more in ((0, 192.0), (1, 0.0), (4, 0.0)):
+            act(S("ST", at, 64, 8), dk, AF.Identity, scale=2.0, bias=more - 4352.0)
+        tt(S("ST", 3, 64, 8), S("ST", 1, 64, 8), B("JM"), OP.add)
+        act(S("ST", 5, 64, 8), ends("TO", 1), AF.Identity, scale=-1.0, bias=-20480.0)
         act(S("Z"), xin, AF.Identity, scale=0.5, bias=127.75)
         act(S("TX", 4096, 4224), xin, AF.Identity, scale=0.5, bias=-128.0)
-        distances("CU" + e, 0, "LV", "CKE", (w1, m, w))
+        distances("CU" + e, 0, "LV", "CKE", (w1, m, w), WHO[1])
         tt(S("X", 128, 256), pd, S("TA"), OP.add)
         tt(S("X", 256, 384), pd, S("LO"), OP.add)
         scan(S("Y", 0, 128), B("ANEW", 0, 128), pd, OP.max, OP.min)
         scan(S("Y", 128, 384), B("ANEW"), S("X", 128, 384), OP.max, OP.min)
-        tt(S("TK"), ends("Y", 0), S("ST", 0, 8), OP.is_lt)
-        for at, j in ((0, 0), (2, 0), (1, 1), (3, 2)):
-            tt(S("SQ", at, 40, 5), ends("Y", j), S("ST", 8 * j, 8 * j + 8), OP.min)
+        tt(S("TK"), ends("Y", 0), S("ST", 1, 64, 8), OP.is_lt)
+        gat(S("SQ"), S("Y"), B("PICK"), S("ST"), OP.min)
         gat(S("OT"), S("TK"), B("REP"), S("OH"), OP.mult)
         scan(S("NM"), B("STEP"), S("SQ"), OP.mult, OP.add)
         gat(S("UP"), S("NM"), B("REP5"), S("OT"), OP.mult)
-        ts(S("XL"), S("NM", 3, 40, 5), -20480.0, OP.add)
+        ts(S("XL"), S("NM", 4, 64, 8), -1.0, OP.mult, -20480.0, OP.add)
         tt(S("MS"), S("UP"), B(p, 384, 512), OP.add)
         gat(xs, S("TX"), S("XL"), S("Z"), OP.add)
         if r == R - 1:
             ts(S("YC"), tnew, 1000.0, OP.is_ge)
-            ts(S("YC"), S("YC"), col(16 + par), OP.mult)
+            dmas("dyc" + e, [("y", T.yc[par:8:2, :], S("YC")[3])], [S("YC")], [])
             return
         ps = B("PS", o, o + 128)
         cp(ps, S("MS"))
@@ -476,7 +478,11 @@ def rank_program(g, core, T, topo):
         remote([RemoteDMATransfer(dst_ids=[DstId(rid=rid, pnc=pid)], dma_engine_mask=sum(1 << x for x in eg[n * j:n * j + n]),
                                   remote_sem=T.sem[sem], src=src[3], dst=dst[3]) for j, (sem, src, dst) in enumerate(moves)],
                [xs, ps], [(sem, got, [dst]) for sem, _, dst in moves], 2)
-        sent[0] += len(eg)
+        prepare(S("MS"), "PRS", 3 * o)
+        out, land, a3 = B("PRS", 3 * o, 3 * o + 384), B("PRE", 3 * o + 768, 3 * o + 1152), "a3%s%d" % (e, r + 1)
+        remote([RemoteDMATransfer(dst_ids=[DstId(rid=rid, pnc=pid)], dma_engine_mask=topo.mask(core, nxt), remote_sem=T.sem[a3],
+                                  src=out[3], dst=land[3])], [out], [(a3, 2 * got, [land])], 1)
+        sent[0] += 2 * len(eg)
 
     for par in range(2):
         second[0] = len(calls)
@@ -490,8 +496,6 @@ def rank_program(g, core, T, topo):
                    par + c + h == 0, par + c + h == 9)
     act(B("YX"), B("wa0", 0, 256), AF.Identity, scale=0.5, bias=-128.0)
     dmas("dyx", [("s", T.yx[:, :], T.YX[:, :])], [B("YX")], [])
-    tt(B("YCF"), B("YCa"), B("YCb"), OP.add)
-    dmas("dyc", [("y", T.yc[:, :], T.YCF[:, :])], [B("YCF")], [])
     gat(B("SW"), B("MS"), B("FIN"))
     turn(B("YP"), B("SW"))
     dmas("dyp", [("y", T.yp[:, :], T.YP[:, :])], [B("YP")], [])

@@ -2,24 +2,32 @@ from concourse.bass import DstId, RemoteDMATransfer
 from concourse.mybir import AluOpType, ActivationFunctionType
 
 R = 4
-BIG = 16384.0
-TOP = 2040 * 4096
-CYCLE, GATHER, HOP, DMA, REMOTE, MIB = 0.85, 1.3, 220.0, 1100.0, 1200.0, 3500.0
-PE, CALL, PASSES, LEADS = 0.55, 40.0, 3, (1500.0, 2000.0, 2500.0, 3000.0, 3500.0, 4000.0, 5000.0)
+KAP = 4096.0
+BIG = 8192.0
+TOP = 2048 * 4096
+OFF = 20480.0
+DROP = float(2 ** 28)
+ROUND = 1.5 * 2 ** 31
+DMA, REMOTE, MIB = 1200.0, 1300.0, 3600.0
+TRIES, FRESH, PASSES, LEAD, NOISE, SHAKE = 200, 40, 2, 8000.0, 60.0, 2000.0
+TIMES = ((1.0, 1.56, 0.0, 0.42, 250.0, 150.0, 0.8), (1.25, 1.3, 0.0, 0.42, 250.0, 250.0, 1.0), (1.4, 1.8, 0.0, 0.45, 250.0, 200.0, 0.8),
+         (1.15, 2.0, 0.0, 0.42, 250.0, 100.0, 1.1))
+ORDER = {}
 
 SCRATCH = {}
 SHARED = {
-    "bfloat16": "X0 256 LW 144 LV 144 IDM 128 IDB 128 IDC 128 PDH 128 PDL 128 MVB 512 IOM 144 IM 128 CKC 128 CKE 128 IDP 128 NEG 128 "
-                "CM 128 PRE 3072 PRS 3072 YX 256 FS 1024 FR 3072 SELI 256 SEL 2048 XIN 1024 XS 1024",
-    "int32": "PUW 4096 P0 256 I1 8 I2 8 I4 16 I5 16 I6 8 I7 8 I8 8 J3 8 J4 8 J5 8 J6 8 J7 8",
-    "uint16": "RO 16 FIN 16 END 8 REP 8 REP5 8 PICK 4 PIN 1024 PS 1024",
-    "float32": "MVF 512 CL 128 JM 8 COL 24 P0F 256 SW 256 YP 256 YCF 256 GOON 256 ANEW 256 STEP 64",
+    "bfloat16": "X0 256 IO 320 S16 256 S17 144 DD 256 C8 64 G8 32 IDH 256 IDL 256 NIP 128 IDM 128 NID 128 IDB 128 NB 128 IDP 128 "
+                "PEN 128 PDH 128 PDL 128 MVB 512 NEG 128 WA 32 WD 32 CK 256 CE 144 CN 576 IND 144 PC 8 LIM 144 "
+                "PRE 3200 PRS 3200 FS 1024 FR 3072 XS 2048",
+    "int32": "PUW 4096 P0 256 I1 8 I4 16 I5 16 J 64",
+    "uint16": "REPK 8 REPW 8 REPD 8 RT 4 RC 16 RP 8 RG 16 REPA 16 PIN 2048 PS 1024",
+    "float32": "MVF 512 IDF 128 IDD 256 MK1 128 MK2 64 SELN 576 CL 128 COL 32 P0F 256 GOON 256 ANEW 144 I7 8",
 }
 OWN = {
-    "bfloat16": "TX 4224 T0 640 XT 128 D 2048 AB 2048 OA 1024 OB 1024 TA 128 FB 32 CFL 128 LO 128",
+    "bfloat16": "TX 5120 T0 640 D 2048 AB 2048 OA 256 OB 1024 FB 32 OH 128 NE 144 NN 144 XR 128",
     "uint16": "TL 16 CU 128 XL 8",
-    "float32": "NE 136 EL 128 X 384 Y 384 C 128 KS 8 OH 128 PR 256 TO 256 G 256 GT 256 CF 128 ST 64 Z 128 SQ 64 NM 64 TK 8 "
-               "OT 128 UP 128 YC 128 MS 128",
+    "float32": "Y 256 BS 16 C 128 KS 128 PR 256 TO 256 RR 64 G 256 G2 256 GT 256 Z 128 RUN 144 WS 144 TK 8 V1 8 DL 8 VM 128 UP 128 PN 160 "
+               "PT 256 YC 128 YP 256",
 }
 SIDE = {}
 for _t, _k in ((SHARED, 1), (OWN, 2)):
@@ -32,12 +40,11 @@ for _t, _k in ((SHARED, 1), (OWN, 2)):
 for _n in ("pa", "pb", "ma", "mb", "wa0", "wa1", "wb0", "wb1"):
     SCRATCH[_n] = ("psum", [128, 512], "float32")
 
-SEMAPHORES = ["qv", "qs", "qt", "qg", "ls", "dx0", "dp0", "dpu", "dyp", "dyx"]
-SEMAPHORES += [a + e for a in ("dtx", "dt0", "dyc") for e in "ab"]
+SEMAPHORES = ["qv", "qs", "qt", "qg", "ls", "dx0", "dp0", "dpu", "dyx"]
+SEMAPHORES += [a + e for a in ("dtx", "dt0", "dyc", "dyp") for e in "ab"]
 SEMAPHORES += ["%s%s%d" % (a, e, r) for a in ("a1", "a2", "a3", "fl", "dc") for e in "ab" for r in range(R)]
 
-WHO = ("svsv", "svsv")
-HELP = 3
+PARTS = (("s4", "v4", "s4", "v3"), ("s4", "v4", "s4", "v4"))
 
 
 def rank_program(g, core, T, topo):
@@ -52,13 +59,14 @@ def rank_program(g, core, T, topo):
     acc = {}
     total = {}
 
-    def B(name, lo=0, hi=None, step=1):
+    def B(name, lo=0, hi=None, step=1, rows=None):
         if name in SIDE:
             name, at, n = SIDE[name]
             lo, hi = at + lo, at + (n if hi is None else hi)
         if hi is None:
             hi = SCRATCH[name][1][1]
-        ap = T[name][:, lo:hi] if step == 1 else T[name][:, lo:hi:step]
+        p0, p1 = rows or (0, 128)
+        ap = T[name][p0:p1, lo:hi] if step == 1 else T[name][p0:p1, lo:hi:step]
         return (name, lo, hi, ap, (hi - lo + step - 1) // step, step)
 
     def psum(name):
@@ -98,44 +106,45 @@ def rank_program(g, core, T, topo):
             acc[b[0]] = old + [(b, False, pe, tok)]
 
     calls = []
-    second = [0]
+    second = [0, 0]
 
-    def op(e, reads, writes, fn, each=1.0, least=64, fixed=0):
+    def op(e, reads, writes, fn, kind, cycles, group=None):
         def issue():
             need(e, reads, writes)
             fn().then_inc(T.sem["q" + e], 1)
             cnt[e] += 1
             mark(e, ("q" + e, cnt[e]), reads, writes)
-        t = CYCLE * (fixed + max(least, each * writes[0][4])) + (CALL if e == "v" and least else 0.0)
-        calls.append((e, reads, writes, issue, t, t + HOP))
+        calls.append((e, reads, writes, issue, kind, cycles, group))
 
-    def dmas(sem, moves, reads, writes, lands=DMA):
+    def dmas(sem, moves, reads, writes, more=0.0):
         def issue():
             for e, out, in_ in moves:
                 need(e, reads, writes)
                 eng[e].dma_start(out, in_).then_inc(T.sem[sem], 16)
             total[sem] = 16 * len(moves)
             mark("d" + sem, (sem, total[sem]), reads, writes)
-        calls.append((moves[0][0], reads, writes, issue, 60.0, lands))
+        calls.append((moves[0][0], reads, writes, issue, "dma", more, None))
 
-    def remote(transfers, srcs, arrivals, writes):
+    def remote(transfers, srcs, arrivals, more):
         def issue():
             need("g", srcs, [])
             g.remote_dma_fused(transfers, local_sem=T.sem.ls)
             for sem, n, bufs in arrivals:
                 mark("rem", (sem, n), [], bufs)
                 total[sem] = n
-        calls.append(("g", srcs, [b for a in arrivals for b in a[2]], issue, 300.0, REMOTE + 250.0 * (writes - 1)))
+        calls.append(("g", srcs, [b for a in arrivals for b in a[2]], issue, "remote", more, None))
 
-    def issue_all():
-        seen, turn_of, after = {}, {}, [{} for _ in calls]
-        for i, (e, reads, writes, _, _, _) in enumerate(calls):
+    def find_order():
+        n = len(calls)
+        seen, turn_of, after = {}, {}, [set() for _ in calls]
+        for i, (e, reads, writes, _, _, _, group) in enumerate(calls):
             for w, specs in ((False, reads), (True, writes)):
                 for b in specs:
                     for j, a, pw in seen.get(b[0], ()):
                         same = calls[j][0] == e
                         if j != i and (((w or pw) and meet(a, b)) or (psum(b[0]) and (not same or e == "t"))):
-                            after[j][i] = calls[j][4 if same and e == "t" else 5]
+                            if group is None or group is not calls[j][6]:
+                                after[j].add(i)
             for w, specs in ((True, writes), (False, reads)):
                 for b in specs:
                     name = b[0]
@@ -148,93 +157,143 @@ def rank_program(g, core, T, topo):
                     elif w:
                         old = [a for a in old if not covers(b, a[1])]
                     seen[name] = old + [(i, b, w)]
-        way = [0.0] * len(calls)
-        for i in range(len(calls) - 1, -1, -1):
-            way[i] = max([t + way[j] for j, t in after[i].items()] + [calls[i][5]])
-        n = len(calls)
-        before = [{} for _ in calls]
-        for i in range(n):
-            for j, gap in after[i].items():
-                before[j][i] = gap + calls[j][4] - calls[i][4]
 
-        def place(order, nexts, first):
+        def times(slow, gather, call, tensor, same, other, far):
+            hold, done = [], []
+            for e, _, _, _, kind, cycles, _ in calls:
+                if kind in ("dma", "remote", "load"):
+                    hold.append({"dma": 100.0, "remote": 300.0, "load": 1.0}[kind])
+                    done.append(far * (DMA if kind != "remote" else REMOTE) + cycles * (far if kind != "load" else 1.0))
+                else:
+                    hold.append(slow * {"v": call + 0.83 * max(64.0 - call, cycles), "s": 20.0 + 0.83 * cycles, "g": 130.0 + 1.66 * cycles,
+                                        "gather": 60.0 + 0.83 * gather * cycles, "t": 5.0 + tensor * cycles}[kind])
+                    done.append(hold[-1] + (60.0 if e == "t" else 0.0))
+            gaps = [{j: (hold[i] if calls[i][0] == calls[j][0] == "t" else done[i] + (same if calls[i][0] == "v" else other if calls[i][0] == "s" else 100.0))
+                     for j in after[i]} for i in range(n)]
+            return hold, done, gaps
+
+        def place(order, hold, nexts, first, fill_gaps=True):
             there, busy = list(first), {e: ([], []) for e in eng}
             for i in order:
                 t, (starts, stops) = there[i], busy[calls[i][0]]
                 k = len(stops)
-                while k and stops[k - 1] > t:
+                while fill_gaps and k and stops[k - 1] > t:
                     k -= 1
-                while k < len(starts) and starts[k] < t + calls[i][4]:
+                if not fill_gaps and k:
+                    t = max(t, stops[-1])
+                while k < len(starts) and starts[k] < t + hold[i]:
                     t = max(t, stops[k])
                     k += 1
                 starts.insert(k, t)
-                stops.insert(k, t + calls[i][4])
+                stops.insert(k, t + hold[i])
                 there[i] = t
                 for j, gap in nexts[i].items():
                     there[j] = max(there[j], t + gap)
             return there
 
+        sets = [times(*a) for a in TIMES]
+        backwards = []
+        for hold, done, gaps in sets:
+            backwards.append([{} for _ in calls])
+            for i in range(n):
+                for j, gap in gaps[i].items():
+                    backwards[-1][j][i] = gap + hold[j] - hold[i]
+        seed = [12345]
+
+        def chance():
+            seed[0] = (seed[0] * 1103515245 + 12345) % 2147483648
+            return seed[0] / 2147483648.0
+
+        def judge(order):
+            ends = []
+            for hold, done, gaps in sets:
+                there = place(order, hold, gaps, [0.0] * n, False)
+                ends.append(max(there[i] + done[i] for i in range(n)))
+            return sum(t / a[0] for t, a in zip(ends, TIMES)), ends, order
+
         best = None
-        for lead in LEADS:
-            order = sorted(range(n), key=lambda i: (-way[i] - (lead if i < second[0] else 0.0), i))
+        for attempt in range(TRIES):
+            hold, done, gaps = sets[attempt % len(sets)]
+            key = [0.0] * n
+            if attempt < FRESH:
+                lead = LEAD * chance()
+                for i in range(n - 1, -1, -1):
+                    key[i] = -NOISE * chance() + min([key[j] - t for j, t in gaps[i].items()] + [-done[i]])
+                key = [key[i] - (lead if i < second[0] else 0.0) for i in range(n)]
+            else:
+                there, amp = place(best[2], hold, gaps, [0.0] * n, False), SHAKE * chance()
+                for i in best[2]:
+                    key[i] = max(key[i], there[i] + amp * (chance() - 0.5))
+                    for j in gaps[i]:
+                        key[j] = max(key[j], key[i] + 0.001)
+            order = sorted(range(n), key=lambda i: (key[i], i))
             for _ in range(PASSES):
-                there = place(order, after, [0.0] * n)
-                end = max(there[i] + calls[i][5] for i in range(n))
-                if best is None or end < best[0]:
-                    best = (end, there)
-                back = place(sorted(range(n), key=lambda i: (-there[i] - calls[i][4], -i)), before, [c[5] - c[4] for c in calls])
-                order = sorted(range(n), key=lambda i: (-back[i] - calls[i][4], i))
-        for i in sorted(range(n), key=lambda i: (best[1][i], i)):
-            calls[i][3]()
+                there = place(order, hold, gaps, [0.0] * n)
+                found = judge(sorted(range(n), key=lambda i: (there[i], i)))
+                if best is None or found[0] < best[0]:
+                    best = found
+                back = place(sorted(range(n), key=lambda i: (-there[i] - hold[i], -i)), hold, backwards[attempt % len(sets)],
+                             [done[i] - hold[i] for i in range(n)])
+                order = sorted(range(n), key=lambda i: (-back[i] - hold[i], i))
+        return best[1:]
 
     def tt(out, a, b, o):
-        op("v", [a, b], [out], lambda: g.vector.tensor_tensor(out[3], a[3], b[3], o), 1.0 if psum(a[0]) or psum(b[0]) else 2.0)
+        op("v", [a, b], [out], lambda: g.vector.tensor_tensor(out[3], a[3], b[3], o), "v", out[4] * (1.0 if psum(a[0]) or psum(b[0]) else 2.0))
 
     def ts(out, a, s1, o1, s2=None, o2=None):
         reads = [a] + [s for s in (s1, s2) if isinstance(s, tuple)]
         x, y = (s[3] if isinstance(s, tuple) else s for s in (s1, s2))
-        each = 0.5 if short(out, a) else 1.0
+        cycles = out[4] * (0.5 if short(out, a) else 1.0)
         if o2 is None:
-            op("v", reads, [out], lambda: g.vector.tensor_scalar(out[3], a[3], x, None, o1), each)
+            op("v", reads, [out], lambda: g.vector.tensor_scalar(out[3], a[3], x, None, o1), "v", cycles)
         else:
-            op("v", reads, [out], lambda: g.vector.tensor_scalar(out[3], a[3], x, y, o1, o2), each)
+            op("v", reads, [out], lambda: g.vector.tensor_scalar(out[3], a[3], x, y, o1, o2), "v", cycles)
 
     def cp(out, a):
-        op("v", [a], [out], lambda: g.vector.tensor_copy(out[3], a[3]))
+        op("v", [a], [out], lambda: g.vector.tensor_copy(out[3], a[3]), "v", out[4])
 
     def scan(out, a, b, o1, o2):
-        op("v", [a, b], [out], lambda: g.vector.tensor_tensor_scan(out[3], a[3], b[3], 0.0, o1, o2))
+        op("v", [a, b], [out], lambda: g.vector.tensor_tensor_scan(out[3], a[3], b[3], 0.0, o1, o2), "v", out[4] * (0.5 if short(out, a, b) else 1.0))
 
     def gat(out, win, lst, b=None, o=None):
         if b is None:
-            op("v", [win, lst], [out], lambda: g.vector.tensor_copy(out[3], win[3].indirect(lst[3])), GATHER, 0, 60)
+            op("v", [win, lst], [out], lambda: g.vector.tensor_copy(out[3], win[3].indirect(lst[3])), "gather", out[4])
+        elif isinstance(b, tuple):
+            op("v", [win, lst, b], [out], lambda: g.vector.tensor_tensor(out[3], win[3].indirect(lst[3]), b[3], o), "gather", out[4])
         else:
-            op("v", [win, lst, b], [out], lambda: g.vector.tensor_tensor(out[3], win[3].indirect(lst[3]), b[3], o), GATHER, 0, 60)
+            op("v", [win, lst], [out], lambda: g.vector.tensor_scalar(out[3], win[3].indirect(lst[3]), b, None, o), "gather", out[4])
 
     def turn(out, a):
-        op("v", [a], [out], lambda: g.vector.transpose(out[3], a[3]))
+        op("v", [a], [out], lambda: g.vector.transpose(out[3], a[3]), "v", out[4])
 
     def fill(out, value):
-        op("v", [], [out], lambda: g.vector.memset(out[3], value))
+        op("v", [], [out], lambda: g.vector.memset(out[3], value), "v", out[4])
 
     def act(out, a, f, scale=1.0, bias=0.0):
         column = isinstance(bias, tuple)
         x = bias[3] if column else bias
-        op("s", [a, bias] if column else [a], [out], lambda: g.scalar.activation(out[3], a[3], f, bias=x, scale=scale), 1.0, 0, 50)
+        op("s", [a, bias] if column else [a], [out], lambda: g.scalar.activation(out[3], a[3], f, bias=x, scale=scale), "s", out[4])
 
     def sgat(out, win, lst):
-        op("s", [win, lst], [out], lambda: g.scalar.activation(out[3], win[3].indirect(lst[3]), AF.Copy), GATHER, 0, 80)
+        op("s", [win, lst], [out], lambda: g.scalar.activation(out[3], win[3].indirect(lst[3]), AF.Copy), "gather", out[4])
 
-    def mm(out, lhsT, rhs, start, stop):
-        k = PE if short(rhs) else 4.0 * PE
-        op("t", [lhsT, rhs], [out], lambda: g.tensor.matmul(out[3], lhsT[3], rhs[3], start, stop), k, 64 * k, 12)
+    def mm(out, lhsT, rhs, start=False, stop=False, group=None):
+        def fn():
+            if group:
+                group[0] -= 1
+            return g.tensor.matmul(out[3], lhsT[3], rhs[3], start, stop or (group is not None and group[0] == 0))
+        if group:
+            group[0] += 1
+        elif group is not None:
+            group.append(1)
+        op("t", [lhsT, rhs], [out], fn, "t", max(min(64, lhsT[4]), out[4]) * (1.0 if short(rhs) else 4.0), group)
 
-    def iota(name, pattern, base, cm):
-        out = B(name)
+    def iota(name, pattern, base, cm, hi=None):
+        out = B(name, 0, hi)
         if SCRATCH[name][2] == "int32":
-            op("g", [], [out], lambda: g.iota(out[3], pattern, base, cm), 2.0, 0, 160)
+            op("g", [], [out], lambda: g.iota(out[3], pattern, base, cm), "g", out[4])
         else:
-            op("g", [], [out], lambda: g.iota(out[3], pattern, base, cm, allow_small_or_imprecise_dtypes=True), 2.0, 0, 160)
+            op("g", [], [out], lambda: g.iota(out[3], pattern, base, cm, allow_small_or_imprecise_dtypes=True), "g", out[4])
 
     def MV(kind, u, w):
         return B(kind, 128 * (2 * u + w), 128 * (2 * u + w) + 128)
@@ -242,98 +301,92 @@ def rank_program(g, core, T, topo):
     dmas("dp0", [("y", T.P0[:, :], T.p0[:, :])], [], [B("P0")])
     dmas("dx0", [("s", T.X0[:, :], T.x0[:, :])], [], [B("X0")])
     for par, e in enumerate("ab"):
-        dmas("dtx" + e, [("ys"[h], T.TX[32 * a + 16 * h:32 * a + 16 * h + 16, 4224 * par:4224 * par + 4096],
+        dmas("dtx" + e, [("ys"[h], T.TX[32 * a + 16 * h:32 * a + 16 * h + 16, 5120 * par:5120 * par + 4096],
                           T.tx[32 * a + 16 * par:32 * a + 16 * par + 16, :]) for a in range(4) for h in range(2)],
-             [], [B("TX" + e, 0, 4096)], DMA + MIB * (par + 1))
+             [], [B("TX" + e, 0, 4096)], MIB * (par + 1))
     for par, e in enumerate("ab"):
-        dmas("dt0" + e, [("s", B("T0" + e, 0, 128)[3], T.tx[16 * par:128:32, :])], [], [B("T0" + e, 0, 128)], DMA + MIB * 2)
-    dmas("dpu", [("y", T.PUW[:, :], T.pu[:, :])], [], [B("PUW")], DMA + MIB * 4)
+        dmas("dt0" + e, [("s", B("T0" + e, 0, 128)[3], T.tx[16 * par:128:32, :])], [], [B("T0" + e, 0, 128)], MIB * 2)
+    dmas("dpu", [("y", T.PUW[:, :], T.pu[:, :])], [], [B("PUW")], MIB * 4)
     for i, c in enumerate(calls):
         c[3]()
-        calls[i] = c[:3] + (lambda: None,) + c[4:]
+        calls[i] = c[:3] + (lambda: None, "load") + c[5:]
 
     iota("I1", [[0, 8]], 0, 1)
-    iota("IOM", [[1, 144]], 0, 0)
-    iota("I4", [[16, 2], [32, 8]], 0, 0)
-    iota("SELI", [[0, 16], [1, 16]], 0, 0)
-    iota("CKC", [[0, 8], [-128, 16]], 2048, 0)
-    iota("CL", [[0, 8], [-128, 16]], TOP + 2048, 0)
-    iota("CKE", [[0, 8], [128, 16]], 128, 0)
-    iota("I2", [[16, 8]], 0, 0)
-    iota("I5", [[16, 8], [128, 2]], 0, 0)
-    iota("I6", [[16, 8]], 15, 0)
+    iota("IO", [[1, 320]], -192, 0)
+    iota("DD", [[16, 8], [0, 2], [1, 16]], 0, 0)
     iota("I7", [[1, 8]], 0, 0)
-    iota("I8", [[8, 8]], 5, 0)
+    iota("S16", [[0, 16], [1, 16]], 0, 0)
+    iota("G8", [[0, 4], [1, 8]], 0, 0)
+    iota("C8", [[0, 4], [1, 8], [0, 2]], 0, 0)
+    iota("S17", [[0, 8], [1, 17]], 0, 0, 136)
+    iota("I4", [[16, 2], [32, 8]], 0, 0)
+    count = B("IO", 192, 320)
 
     def col(j):
         return B("COL", j, j + 1)
 
-    def ident(out, c, value=None):
-        if value is None:
-            ts(out, B("IOM", 0, 128), c, OP.is_equal)
-        else:
-            ts(out, B("IOM", 0, 128), c, OP.is_equal, value, OP.mult)
+    def J(j):
+        return B("J", 8 * j, 8 * j + 1)
 
-    ts(B("J3"), B("I1"), 16, OP.bitwise_and)
-    ts(B("J4"), B("I1"), 15, OP.bitwise_and)
-    ts(B("J5"), B("I1"), 1, OP.bitwise_and)
+    for j, (value, o) in enumerate(((16, OP.bitwise_and), (15, OP.bitwise_and), (1, OP.bitwise_and), (7, OP.bitwise_and),
+                                    (8, OP.bitwise_and), (4, OP.logical_shift_right), (5, OP.logical_shift_right))):
+        ts(J(j), B("I1", 0, 1), value, o)
     cp(col(0), B("I1", 0, 1))
-    cp(col(1), B("J4", 0, 1))
-    ts(B("RO"), B("I4"), col(1), OP.add)
-    ts(B("FIN"), B("I5"), col(1), OP.add)
-    for name, src in (("END", "I6"), ("REP", "I7"), ("REP5", "I8")):
-        cp(B(name), B(src))
+    cp(col(1), J(1))
+    cp(col(2), J(5))
     for u in range(2):
-        ts(col(3 + u), B("J3", 0, 1), 16.0 * u, OP.not_equal, 1000.0, OP.mult)
+        ts(col(3 + u), J(0), 16.0 * u, OP.not_equal, 1000.0, OP.mult)
         for w in range(2):
             ts(col(5 + 2 * u + w), col(3 + u), col(0), OP.add, 16.0 * (w - u), OP.add)
-            ident(MV("MVB", u, w), col(5 + 2 * u + w))
+            ts(MV("MVB", u, w), count, col(5 + 2 * u + w), OP.is_equal)
             act(MV("MVF", u, w), MV("MVB", u, w), AF.Copy)
-    tt(col(9), col(0), B("J4", 0, 1), OP.subtract)
-    ts(col(10), B("J5", 0, 1), -2.0, OP.mult, 1.0, OP.add)
-    ts(col(11), col(9), 15.0, OP.add)
-    tt(col(12), col(10), col(0), OP.add)
-    tt(col(13), col(9), B("J3", 0, 1), OP.subtract)
-    ts(col(14), col(13), -160.0, OP.add)
-    for c in range(8):
-        ts(B("SEL", 256 * c, 256 * c + 256), B("SELI"), col(0), OP.subtract, -16.0 * c, OP.is_equal)
-    ts(B("LW"), B("IOM"), col(11), OP.is_equal, 4096.0, OP.mult)
-    act(B("LV"), B("LW"), AF.Copy, scale=2.0)
-    ts(B("IM"), B("IOM", 0, 128), col(14), OP.subtract)
-    ident(B("IDM"), col(0))
-    for name, value in (("IDB", BIG), ("IDC", float(TOP)), ("IDP", 128.0)):
+    ts(B("IDM"), count, col(0), OP.is_equal)
+    for name, value in (("IDF", 1.0), ("NID", -1.0), ("IDB", BIG), ("NB", -65536.0), ("IDP", 128.0), ("NIP", -128.0), ("PEN", TOP / DROP)):
         act(B(name), B("IDM"), AF.Copy, scale=value)
-    ident(B("PDH"), col(12))
+    ts(B("IDD"), B("DD"), col(0), OP.is_equal)
+    act(B("IDL"), B("IDD"), AF.Copy)
+    act(B("IDH"), B("IDD"), AF.Copy, scale=128.0)
+    ts(col(9), J(2), -2.0, OP.mult, 1.0, OP.add)
+    ts(B("PDH"), count, col(9), OP.subtract, col(0), OP.is_equal)
     tt(B("PDL"), B("IDM"), B("PDH"), OP.subtract)
     act(B("PDH"), B("PDL"), AF.Copy, scale=128.0)
-    tt(B("JM"), B("I2"), B("J4"), OP.add)
-    act(B("CM"), B("SELI", 0, 128), AF.Identity, scale=0.0, bias=-20480.0)
-    act(B("GOON"), B("SELI"), AF.Sign)
-    act(B("ANEW"), B("SELI"), AF.Relu, scale=-33554432.0, bias=33554432.0)
-    act(B("NEG"), B("SELI", 0, 128), AF.Identity, scale=0.0, bias=-1.0)
-    for j, value in enumerate((0.0, -1.0, -128.0, 1.0, -1.0, -1.0, 0.0, 0.0)):
-        fill(B("STEP", j, None, 8), value)
-    fill(B("ST"), 0.0)
-    ts(B("J6"), B("I1"), 7, OP.bitwise_and)
-    ts(B("J7"), B("I1"), 8, OP.bitwise_and)
-    ts(col(18), B("J6", 0, 1), 0.0, OP.is_equal, 128.0, OP.mult)
-    ts(col(19), B("J6", 0, 1), 3.0, OP.is_equal, 256.0, OP.mult)
-    ts(col(20), B("J7", 0, 1), 2.0, OP.mult, 15.0, OP.add)
-    tt(col(21), col(18), col(19), OP.add)
-    tt(col(22), col(20), col(21), OP.add)
-    ts(B("PICK"), B("I4", 0, 4), col(22), OP.add)
-    fill(B("CKC", 0, None, 16), -1073741824.0)
+    ts(B("WA"), B("G8"), col(2), OP.is_equal, 2.0 * KAP, OP.mult)
+    ts(B("WD"), B("G8"), col(2), OP.is_equal, -KAP, OP.mult)
+    ts(B("MK1"), B("S16", 0, 128), col(1), OP.is_equal)
+    ts(B("MK2"), B("C8"), col(2), OP.is_equal)
+    act(B("GOON"), B("S16"), AF.Sign)
+    act(B("CK"), B("S16"), AF.Identity, scale=-256.0, bias=3840.0)
+    fill(B("CK", 0, 256, 16), -1073741824.0)
+    fill(B("CK", 15, 128, 16), float(TOP))
+    act(B("CL"), B("S16", 0, 128), AF.Identity, scale=-256.0, bias=TOP + 3840.0)
+    ts(B("LIM"), B("S16", 0, 144), 0.0, OP.is_equal, -DROP, OP.mult)
+    ts(B("IND", 0, 136), B("S17", 0, 136), 0.0, OP.is_equal)
+    act(B("ANEW", 0, 136), B("IND", 0, 136), AF.Copy, scale=1073741824.0)
+    act(B("CE", 0, 136), B("S17", 0, 136), AF.Identity, scale=16.0, bias=3776.0)
+    fill(B("CE", 0, 136, 17), 0.0)
+    for r in range(R):
+        act(B("CN", 144 * r, 144 * r + 136), B("IND", 0, 136), AF.Identity, scale=4096.0 + 256.0 * r, bias=OFF + BIG)
+    act(B("NEG"), count, AF.Identity, scale=0.0, bias=-1.0)
+    cp(B("PC"), B("I1"))
+    ts(col(10), J(6), 34.0, OP.mult, col(1), OP.add)
+    for u in range(2):
+        for a in range(2):
+            j = 2 * u + a
+            ts(col(11 + j), col(10), col(3 + u), OP.add, 17.0 * a - 7.0, OP.add)
+            ts(B("SELN", 144 * j, 144 * j + 136), B("IO", 184, 320), col(11 + j), OP.is_equal)
+    ts(B("REPK"), B("I7"), 16.0, OP.mult, 15.0, OP.add)
+    ts(B("REPW"), B("I7"), 17.0, OP.mult, 16.0, OP.add)
+    cp(B("REPD"), B("I7"))
+    ts(col(15), J(2), 16.0, OP.mult, 15.0, OP.add)
+    ts(B("RT"), B("I7", 0, 4), 32.0, OP.mult, col(15), OP.add)
+    ts(col(16), J(4), 0.125, OP.mult)
+    ts(col(17), J(3), 32.0, OP.mult, col(16), OP.add)
+    ts(col(18), col(17), 16.0, OP.add)
+    ts(col(19), J(0), col(17), OP.add)
+    for out, c in ((B("RC", 0, 8), 17), (B("RC", 8, 16), 18), (B("RP"), 19)):
+        ts(out, B("I7"), 2.0, OP.mult, col(c), OP.add)
+    ts(B("RG"), B("I4"), col(1), OP.add)
     cp(B("P0F"), B("P0"))
-    turn(B("SW"), B("P0F"))
-    for par, e in enumerate("ab"):
-        fill(B("PR" + e, 0, 8), 0.0)
-        fill(B("NE" + e, 0, 1), 0.0)
-        sgat(B("MS" + e), B("SW"), B("RO", 8 * par, 8 * par + 8))
-        gat(B("PIN", 128 * par, 128 * par + 128), B("SW"), B("RO", 8 * par, 8 * par + 8))
-        for c in range(8):
-            for h in range(2):
-                mm(B("w%s0" % e, 16 * c, 16 * c + 16), MV("MVB", par, h), B("X0", 32 * c + 16 * h, 32 * c + 16 * h + 16), c + h == 0, c + h == 8)
-        act(B("XIN", 128 * par, 128 * par + 128), B("w%s0" % e, 0, 128), AF.Identity, scale=2.0, bias=256.0)
 
     others = [q for q in range(R) if q != rank]
     nxt, prv = T.cores[(rank + 1) % R], T.cores[(rank - 1) % R]
@@ -344,67 +397,99 @@ def rank_program(g, core, T, topo):
         o = 128 * (2 * r + par)
         p, m, w, w1 = "p" + e, "m" + e, "w%s0" % e, "w%s1" % e
         told, tnew = B("T0" + e, 128 * r, 128 * r + 128), B("T0" + e, 128 * r + 128, 128 * r + 256)
-        fs, xin, xs = B("FS", o, o + 128), B("XIN", o, o + 128), B("XS", o, o + 128)
-        tx, pd = B("TX" + e, 0, 4096), B(p, 0, 128)
+        fs, tx = B("FS", o, o + 128), B("TX" + e, 0, 4096)
+        at = 4096 + 256 * r
+        pre = 400 * (2 * r + par)
+        pn = B("PN" + e, 16, 144)
 
         def S(name, a=0, b=None, step=1):
             return B(name + e, a, b, step)
 
-        def ends(name, j):
-            return S(name, 128 * j + 15, 128 * j + 128, 16)
+        def ends(name, a, b, n=16):
+            return S(name, a + n - 1, b, n)
 
-        def digits(src, high, low):
-            act(high, src, AF.Identity, scale=1.0 / 128.0, bias=159.502)
-            act(B(p, 256, 384), high, AF.Identity, scale=-128.0, bias=20480.0)
-            tt(low, B(p, 256, 384), src, OP.add)
+        def names(out, high, low, start=False, stop=False):
+            mm(out, B("IDP"), high, start)
+            mm(out, B("IDM"), low, False, stop)
 
-        def prepare(src, buf, at):
-            high, low = B(buf, at, at + 128), B(buf, at + 128, at + 256)
-            digits(src, high, low)
-            mm(B(p, 128, 256), B("PDH"), high, True, False)
-            mm(B(p, 128, 256), B("PDL"), low, False, True)
-            act(S("NE", 1, 129), B(p, 128, 256), AF.Abs)
-            scan(B(buf, at + 256, at + 384), S("NE", 0, 128), B("GOON", 0, 128), OP.max, OP.min)
+        def listed(out, parts):
+            for j, (part, ident) in enumerate(parts):
+                mm(B(w, 0, 256), part, B(ident), j == 0, j + 1 == len(parts))
+            turn(S("PT"), B(w, 0, 256))
+            gat(out, S("PT"), B("RP"), -OFF, OP.add)
 
-        def distances(lst, l0, lw, code, banks, whos):
-            for q, who in enumerate(whos):
-                d, bank = S("D", 512 * q, 512 * q + 512), banks[q % 3]
-                (sgat if who == "s" else gat)(d, tx, B(lst, l0 + 32 * q, l0 + 32 * q + 32))
-                mm(B(bank), S("XT"), B("SEL", 512 * q, 512 * q + 512), True, False)
-                mm(B(bank), B("IDM"), d, False, True)
-                act(S("AB", 512 * q, 512 * q + 512), B(bank), AF.Abs)
-            mm(pd, B("IDM"), B(code), True, False)
-            for half in range(2):
-                for s in range(16):
-                    mm(B(p, 64 * half, 64 * half + 64), B(lw, 15 - s, 143 - s), S("AB", 1024 * half + s, 1024 * half + 1024, 16), False,
-                       half + s == 16)
+        def prepare(buf, j):
+            high, low = B(buf, j, j + 128), B(buf, j + 128, j + 256)
+            act(high, pn, AF.Identity, scale=1.0 / 128.0, bias=-0.498)
+            mm(B(w1, 0, 128), B("IDF"), pn, True)
+            mm(B(w1, 0, 128), B("NIP"), high, False, True)
+            act(low, B(w1, 0, 128), AF.Copy)
+            mm(B(w1, 128, 256), B("PDH"), high, True)
+            mm(B(w1, 128, 256), B("PDL"), low, False, True)
+            act(S("NE", 1, 129), B(w1, 128, 256), AF.Abs, scale=DROP)
+            scan(B(buf, j + 256, j + 385), S("NE", 0, 129), B("LIM", 0, 129), OP.add, OP.min)
 
-        mm(B(m, 384, 512), xin, B("IDM"), True, True)
-        ts(S("XT"), B(m, 384, 512), -0.5, OP.mult, 128.0, OP.add)
+        def distances(lst, l0, row, parts, banks, keys, width, group):
+            turns = 0
+            for part in parts:
+                n = int(part[1:])
+                a, b = 128 * row, 128 * (row + n)
+                if part[0] in "vm":
+                    for j in range(0, n, 2):
+                        k = min(2, n - j)
+                        gat(S("D", a + 128 * j, a + 128 * (j + k)), tx, B(lst, l0 + 8 * (row + j), l0 + 8 * (row + j + k)),
+                            S("TX", at, at + 128 * k), OP.subtract)
+                    if part[0] == "v":
+                        ts(S("AB", a, b), S("D", a, b), 0.0, OP.max)
+                    else:
+                        act(S("AB", a, b), S("D", a, b), AF.Abs, scale=0.5)
+                else:
+                    bank = banks[turns % len(banks)]
+                    turns += 1
+                    (sgat if part[0] == "s" else gat)(S("D", a, b), tx, B(lst, l0 + 8 * row, l0 + 8 * (row + n)))
+                    for j in range(0, n, 2):
+                        k = 128 * min(2, n - j)
+                        mm(B(bank, 128 * j, 128 * j + k), B("NID"), S("TX", at, at + k), j == 0)
+                    mm(B(bank, 0, 128 * n), B("IDM"), S("D", a, b), False, True)
+                    act(S("AB", a, b), B(bank, 0, 128 * n), AF.Abs, scale=0.5)
+                for k in range(row, row + n):
+                    if part[0] == "v":
+                        mm(keys(k), S("D", 128 * k, 128 * k + 128), B("WD", 0, width), group=group)
+                    mm(keys(k), S("AB", 128 * k, 128 * k + 128), B("WA", 0, width), group=group)
+                row += n
+
         if r == 0:
-            prepare(S("MS"), "PRE", 3 * o)
-        high, low, goon = (B("PRE", 3 * o + 128 * j, 3 * o + 128 * j + 128) for j in range(3))
-        distances("PIN", o, "LW", "CKC", (w, w1, m), WHO[0])
-        for j, digit in ((1, high), (2, low)):
-            tt(S("X", 128 * j, 128 * j + 128), pd, digit, OP.add)
-        for j in range(3):
-            scan(S("Y", 128 * j, 128 * j + 128), goon, S("X", 128 * j, 128 * j + 128) if j else pd, OP.mult, OP.max)
+            fill(S("NE", 0, 1), 0.0)
+            for a in range(2):
+                mm(B(w, 0, 128), B("P0F", 128 * a, 128 * a + 128), MV("MVF", par, a), a == 0, a == 1)
+            act(pn, B(w, 0, 128), AF.Identity, bias=OFF)
+            fill(S("PN", 144 - 144 * par, 160 - 144 * par), 0.0)
+            for j in range(4):
+                mm(B(m, 128 * (j // 2), 128 * (j // 2) + 128), MV("MVB", par, j % 2), B("X0", 128 * (j % 2), 128 * (j % 2) + 128), j == 0, j == 3)
+            act(S("TX", at, at + 256), B(m, 0, 256), AF.Copy)
+            listed(B("PS", 512 * par, 512 * par + 128), [(pn, "IDD")])
+            prepare("PRE", pre)
+        high, low = B("PRE", pre, pre + 128), B("PRE", pre + 128, pre + 256)
+
+        sums = []
+        mm(B(p, 0, 256), B("IDM"), B("CK"), True)
+        mm(B(p, 0, 256), B("IDM"), B("PRE", pre, pre + 256), group=sums)
+        mm(B(p, 0, 128), B("PEN"), B("PRE", pre + 257, pre + 385), group=sums)
+        mm(B(p, 256, 384), B("IDP"), high, group=sums)
+        mm(B(p, 256, 384), B("IDM"), low, group=sums)
+        lst, l0 = ("PS", 512 * par) if r == 0 else ("PIN", 2 * o + 128)
+        distances(lst, l0, 1, PARTS[0], (w, w1, m), lambda k: B(p, k, 256, 16), 16, sums)
+        for j in range(2):
+            scan(S("Y", 128 * j, 128 * j + 128), B("PRE", pre + 256, pre + 384), B(p, 128 * j, 128 * j + 128), OP.add, OP.max)
+        ts(S("BS"), ends("Y", 0, 256), ROUND, OP.add, -ROUND, OP.add)
+        tt(S("FB", 0, 16), ends("Y", 0, 256), S("BS"), OP.subtract)
         if r > 0:
-            act(S("CFL"), pd, AF.Sign, bias=-16777216.0)
-            ts(S("FB", 16, 24), ends("Y", 0), 16777216.0, OP.is_lt)
-        for j in (1, 2):
-            tt(S("FB", 8 * j - 8, 8 * j), ends("Y", j), ends("Y", 0), OP.subtract)
+            act(S("FB", 16, 24), ends("Y", 0, 128), AF.Relu, scale=-1.0, bias=float(TOP))
         for c in range(8):
-            if c < 8 - HELP:
-                ts(S("OA", 128 * c, 128 * c + 128), B("IM"), S("FB", c, c + 1), OP.is_equal)
-            else:
-                act(S("D", 128 * c, 128 * c + 128), B("IM"), AF.Abs, scale=-1.0, bias=S("FB", c, c + 1))
-            ts(S("OB", 128 * c, 128 * c + 128), B("IOM", 0, 128), S("FB", 8 + c, 9 + c), OP.is_equal,
-               S("FB", 16 + c, 17 + c) if r else 1.0, OP.mult)
-        if HELP:
-            act(S("OA", 1024 - 128 * HELP, 1024), S("D", 1024 - 128 * HELP, 1024), AF.Relu, scale=-1.0, bias=1.0)
-        for c in range(8):
-            mm(B(w, 0, 128), S("OA", 128 * c, 128 * c + 128), S("OB", 128 * c, 128 * c + 128), c == 0, c == 7)
+            ts(S("OA", 32 * c, 32 * c + 32), B("IO", 96, 128), S("FB", c, c + 1), OP.is_equal)
+            ts(S("OB", 128 * c, 128 * c + 128), count, S("FB", 8 + c, 9 + c), OP.is_equal, S("FB", 16 + c, 17 + c) if r else 1.0, OP.mult)
+            mm(B(w, 0, 128, 1, (32 * (c // 2), 32 * (c // 2) + 32)), S("OA", 32 * c, 32 * c + 32), S("OB", 128 * c, 128 * c + 128),
+               c % 2 == 0, c % 2 == 1)
         act(fs, B(w, 0, 128), AF.Sign)
         dsts, ids = [], []
         for q in others:
@@ -415,91 +500,94 @@ def rank_program(g, core, T, topo):
         fl = "fl%s%d" % (e, r)
         remote([RemoteDMATransfer(dst_ids=ids, dma_engine_mask=topo.mask(core, T.cores[others[0]]), remote_sem=T.sem[fl], srcs=[fs[3]],
                                   dsts=dsts)], [fs],
-               [(fl, sum(len(topo.engines(T.cores[q], core)) for q in others), [B("FR", 3 * o, 3 * o + 384)])], 3)
+               [(fl, sum(len(topo.engines(T.cores[q], core)) for q in others), [B("FR", 3 * o, 3 * o + 384)])], 700.0)
         sent[0] += len(topo.engines(core, T.cores[others[0]]))
         for i, mp in enumerate([B("NEG"), fs] + [B("FR", 3 * o + 128 * j, 3 * o + 128 * j + 128) for j in range(3)]):
-            mm(B(w, 128, 256), B("IDB"), mp, i == 0, i == 4)
-        tt(tnew, B(w, 128, 256), told, OP.max)
-        dmas("dc%s%d" % (e, r), [("y", T.TX[16 * h:128:32, 4224 * par:4224 * par + 4096], tnew[3]) for h in range(2)], [tnew], [tx], DMA + 200.0)
-        for j, (lhs, rhs) in enumerate(((B("IDP"), high), (B("IDM"), low), (B("IDM"), B("CM")))):
-            mm(B(p, 384, 512), lhs, rhs, j == 0, j == 2)
+            mm(B(w1, 0, 128), B("IDB"), mp, i == 0, i == 4)
+        tt(tnew, B(w1, 0, 128), told, OP.max)
+        dmas("dc%s%d" % (e, r), [("y", T.TX[16 * h:128:32, 5120 * par:5120 * par + 4096], tnew[3]) for h in range(2)], [tnew], [tx], 350.0)
         if r == 0:
-            dk = ends("Y", 1)
-            gat(S("OH"), S("Y", 128, 256), B("END"), S("X", 128, 256), OP.is_equal)
+            act(S("C"), B(p, 0, 128), AF.Copy)
         else:
-            dk = S("KS")
-            mm(B(m, 128, 256), B("IDC"), S("CFL"), True, False)
-            mm(B(m, 128, 256), B("IDM"), B("CKC"), False, True)
-            scan(S("EL"), B("GOON", 0, 128), B(m, 128, 256), OP.mult, OP.max)
-            tt(S("C"), S("X", 128, 256), B("CL"), OP.min)
-            ts(S("TK"), ends("Y", 1), float(TOP), OP.min)
-            tt(dk, ends("EL", 0), S("TK"), OP.max)
-            gat(S("OH"), dk, B("REP"), S("C"), OP.is_equal)
-        tt(S("PR", 1, 128), S("OH", 1, 128), B(p, 384, 511), OP.mult)
-        tt(S("PR", 128, 256), S("OH"), B(p, 384, 512), OP.mult)
-        scan(S("TO"), B("GOON", 0, 256), S("PR"), OP.mult, OP.add)
-        for h in range(2):
-            mm(B(m, 256 + h, 272, 2), MV("MVF", h, par), ends("TO", 0), h == 0, h == 1)
-        cp(S("TL"), B(m, 256, 272))
-        gat(S("G"), B("PUW"), S("TL"))
+            tt(S("C"), B(p, 0, 128), B("CL"), OP.min)
+        scan(S("KS"), B("GOON", 0, 128), S("C"), OP.mult, OP.max)
+        gat(S("OH"), S("KS"), B("REPK"), S("C"), OP.is_equal)
+        names(B(p, 1, 128), B("PRE", pre, pre + 127), B("PRE", pre + 128, pre + 255), True)
+        names(B(p, 128, 256), high, low)
+        mm(B(p, 1, 128), B("IDB"), S("OH", 1, 128))
+        mm(B(p, 128, 256), B("IDB"), S("OH"), False, True)
+        scan(S("TO"), B("GOON"), B(p, 0, 256), OP.mult, OP.max)
+        gat(S("RR"), S("TO"), B("RT"), B("MK2"), OP.mult)
+        for a in range(4):
+            mm(B(p, 384, 400, 1, (32 * a, 32 * a + 32)), B("MK1", 0, 32), S("RR", 16 * a, 16 * a + 16), True, True)
+        ts(S("TL"), B(p, 384, 400), -OFF - BIG, OP.add)
+        sgat(S("G"), B("PUW"), S("TL"))
         turn(S("GT"), S("G"))
-        gat(S("CU"), S("GT"), B("RO", 8 * par, 8 * par + 8))
-        sgat(S("CF"), S("GT"), B("RO", 8 * par, 8 * par + 8))
-        digits(S("CF"), S("TA"), S("LO"))
-        for at, more in ((0, 192.0), (1, 0.0), (4, 0.0)):
-            act(S("ST", at, 64, 8), dk, AF.Identity, scale=2.0, bias=more - 4352.0)
-        tt(S("ST", 3, 64, 8), S("ST", 1, 64, 8), B("JM"), OP.add)
-        act(S("ST", 5, 64, 8), ends("TO", 1), AF.Identity, scale=-1.0, bias=-20480.0)
-        act(S("Z"), xin, AF.Identity, scale=0.5, bias=127.75)
-        act(S("TX", 4096, 4224), xin, AF.Identity, scale=0.5, bias=-128.0)
-        distances("CU" + e, 0, "LV", "CKE", (w1, m, w), WHO[1])
-        tt(S("X", 128, 256), pd, S("TA"), OP.add)
-        tt(S("X", 256, 384), pd, S("LO"), OP.add)
-        scan(S("Y", 0, 128), B("ANEW", 0, 128), pd, OP.max, OP.min)
-        scan(S("Y", 128, 384), B("ANEW"), S("X", 128, 384), OP.max, OP.min)
-        tt(S("TK"), ends("Y", 0), S("ST", 1, 64, 8), OP.is_lt)
-        gat(S("SQ"), S("Y"), B("PICK"), S("ST"), OP.min)
-        gat(S("OT"), S("TK"), B("REP"), S("OH"), OP.mult)
-        scan(S("NM"), B("STEP"), S("SQ"), OP.mult, OP.add)
-        gat(S("UP"), S("NM"), B("REP5"), S("OT"), OP.mult)
-        ts(S("XL"), S("NM", 4, 64, 8), -1.0, OP.mult, -20480.0, OP.add)
-        tt(S("MS"), S("UP"), B(p, 384, 512), OP.add)
-        gat(xs, S("TX"), S("XL"), S("Z"), OP.add)
+        gat(S("CU"), S("GT"), B("RC", 8 * par, 8 * par + 8))
+        sgat(S("G2"), S("G"), B("RG"))
+        mm(B(p, 0, 136), B("IDM"), B("CN", 144 * r, 144 * r + 136), True)
+        mm(B(p, 0, 136, 17), B("IDM"), B("PC"))
+        for a in range(2):
+            mm(B(p, 0, 136), S("G2", 128 * a, 128 * a + 128), B("SELN", 144 * (2 * par + a), 144 * (2 * par + a) + 136))
+        act(S("Z"), S("TX", at, at + 128), AF.Identity, bias=255.75)
+        sums = []
+        mm(B(m, 0, 136), B("IDM"), B("CE", 0, 136), True)
+        mm(B(m, 0, 136, 17), B("IDF"), ends("KS", 0, 128), group=sums)
+        distances("CU" + e, 0, 0, PARTS[1], (w, w1), lambda k: B(m, 1 + k, 136, 17), 8, sums)
+        scan(S("RUN", 0, 136), B("ANEW", 0, 136), B(m, 0, 136), OP.max, OP.min)
+        tt(S("NN", 0, 136), B(m, 0, 136), S("RUN", 0, 136), OP.not_equal)
+        tt(S("TK"), ends("RUN", 0, 136, 17), ends("KS", 0, 128), OP.is_lt)
+        mm(B(p, 0, 136), B("NB"), S("NN", 0, 136), False, True)
+        scan(S("WS", 0, 136), S("NN", 0, 136), B(p, 0, 136), OP.mult, OP.max)
+        gat(S("VM"), S("WS", 0, 136), B("REPW"), B("MK1"), OP.mult)
+        mm(B(m, 0, 8), S("VM"), B("MK2", 0, 16, 2), True, True)
+        ts(S("XL"), B(m, 0, 8), -OFF - BIG, OP.add)
+        gat(S("XR"), S("TX", 0, at + 128), S("XL"), S("Z"), OP.add)
+        tt(S("V1"), ends("WS", 0, 136, 17), ends("TO", 128, 256), OP.subtract)
+        tt(S("DL"), S("V1"), S("TK"), OP.mult)
+        gat(S("UP"), S("DL"), B("REPD"), S("OH"), OP.mult)
+        tt(pn, B(p, 256, 384), S("UP"), OP.add)
         if r == R - 1:
             ts(S("YC"), tnew, 1000.0, OP.is_ge)
             dmas("dyc" + e, [("y", T.yc[par:8:2, :], S("YC")[3])], [S("YC")], [])
+            for a in range(2):
+                j = 16 + 16 * (a - par)
+                mm(B(w, 128 * a, 128 * a + 128), S("PN", j, j + 128), B("IDF"), a == 0, a == 1)
+            act(S("YP"), B(w, 0, 256), AF.Identity, bias=-OFF)
+            dmas("dyp" + e, [("ys"[c % 2], T.yp[32 * c + 16 * par:32 * c + 16 * par + 16, :],
+                              T.YP[32 * c + 16 * par:32 * c + 16 * par + 16, 256 * par:256 * par + 256]) for c in range(4)], [S("YP")], [])
             return
-        ps = B("PS", o, o + 128)
-        cp(ps, S("MS"))
+        xs = B("XS", 2 * o, 2 * o + 256)
+        ts(B("XS", 2 * o, 2 * o + 128), S("XR"), 0.5, OP.mult, -128.0, OP.add)
+        act(B("XS", 2 * o + 128, 2 * o + 256), S("XR"), AF.Identity, scale=0.5, bias=-128.0)
+        j = 512 * par + 128 * r
+        listed(B("PS", j + 128, j + 256), [(high, "IDH"), (low, "IDL"), (S("UP"), "IDD")])
         rid, pid = topo.addr(nxt)[:2]
         eg, got = topo.engines(core, nxt), len(topo.engines(prv, core)) // 2
         n = len(eg) // 2
-        moves = [("a1%s%d" % (e, r + 1), xs, B("XIN", o + 256, o + 384)), ("a2%s%d" % (e, r + 1), ps, B("PIN", o + 256, o + 384))]
+        moves = [("a1%s%d" % (e, r + 1), xs, S("TX", at + 256, at + 512)),
+                 ("a2%s%d" % (e, r + 1), B("PS", j, j + 256), B("PIN", 2 * o + 512, 2 * o + 768))]
         remote([RemoteDMATransfer(dst_ids=[DstId(rid=rid, pnc=pid)], dma_engine_mask=sum(1 << x for x in eg[n * j:n * j + n]),
                                   remote_sem=T.sem[sem], src=src[3], dst=dst[3]) for j, (sem, src, dst) in enumerate(moves)],
-               [xs, ps], [(sem, got, [dst]) for sem, _, dst in moves], 2)
-        prepare(S("MS"), "PRS", 3 * o)
-        out, land, a3 = B("PRS", 3 * o, 3 * o + 384), B("PRE", 3 * o + 768, 3 * o + 1152), "a3%s%d" % (e, r + 1)
+               [src for _, src, _ in moves], [(sem, got, [dst]) for sem, _, dst in moves], 600.0)
+        prepare("PRS", pre)
+        out, land, a3 = B("PRS", pre, pre + 385), B("PRE", pre + 800, pre + 1185), "a3%s%d" % (e, r + 1)
         remote([RemoteDMATransfer(dst_ids=[DstId(rid=rid, pnc=pid)], dma_engine_mask=topo.mask(core, nxt), remote_sem=T.sem[a3],
-                                  src=out[3], dst=land[3])], [out], [(a3, 2 * got, [land])], 1)
+                                  src=out[3], dst=land[3])], [out], [(a3, 2 * got, [land])], 400.0)
         sent[0] += 2 * len(eg)
 
     for par in range(2):
         second[0] = len(calls)
         for r in range(R):
             stream(par, r)
-    for par in range(2):
-        o = 128 * (2 * (R - 1) + par)
-        for c in range(8):
-            for h in range(2):
-                mm(B("wa0", 32 * c + 16 * h, 32 * c + 16 * h + 16), MV("MVB", h, par), B("XS", o + 16 * c, o + 16 * c + 16),
-                   par + c + h == 0, par + c + h == 9)
-    act(B("YX"), B("wa0", 0, 256), AF.Identity, scale=0.5, bias=-128.0)
-    dmas("dyx", [("s", T.yx[:, :], T.YX[:, :])], [B("YX")], [])
-    gat(B("SW"), B("MS"), B("FIN"))
-    turn(B("YP"), B("SW"))
-    dmas("dyp", [("y", T.yp[:, :], T.YP[:, :])], [B("YP")], [])
-    issue_all()
+    for j in range(4):
+        mm(B("wa1", 128 * (j % 2), 128 * (j % 2) + 128), MV("MVB", j % 2, j // 2), B("XR" + "ab"[j // 2]), j == 0, j == 3)
+    act(B("X0"), B("wa1", 0, 256), AF.Identity, scale=0.5, bias=-128.0)
+    dmas("dyx", [("s", T.yx[:, :], T.X0[:, :])], [B("X0")], [])
+    if "order" not in ORDER:
+        ORDER["order"] = find_order()
+    for i in ORDER["order"][1]:
+        calls[i][3]()
     g.wait_ge(T.sem.ls, sent[0])
     for e in "vstg":
         g.wait_ge(T.sem["q" + e], cnt[e])

from concourse.bass import DstId, RemoteDMATransfer
from concourse.mybir import AluOpType, ActivationFunctionType

R = 4
KAP = 4096.0
BIG = 8192.0
TOP = 2048 * 4096
OFF = 20480.0
DROP = float(2 ** 28)
ROUND = 1.5 * 2 ** 31
DMA, REMOTE, MIB = 1200.0, 1300.0, 3600.0
TRIES, FRESH, PASSES, LEAD, NOISE, SHAKE = 200, 40, 2, 8000.0, 60.0, 2000.0
TIMES = ((1.0, 1.56, 0.0, 0.42, 250.0, 150.0, 0.8), (1.25, 1.3, 0.0, 0.42, 250.0, 250.0, 1.0), (1.4, 1.8, 0.0, 0.45, 250.0, 200.0, 0.8),
         (1.15, 2.0, 0.0, 0.42, 250.0, 100.0, 1.1))
ORDER = {}

SCRATCH = {}
SHARED = {
    "bfloat16": "X0 256 IO 320 S16 256 S17 144 DD 256 C8 64 G8 32 IDH 256 IDL 256 NIP 128 IDM 128 NID 128 IDB 128 NB 128 IDP 128 "
                "PEN 128 PDH 128 PDL 128 MVB 512 NEG 128 WA 32 WD 32 CK 256 CE 144 CN 576 IND 144 PC 8 LIM 144 "
                "PRE 3200 PRS 3200 FS 1024 FR 3072 XS 2048",
    "int32": "PUW 4096 P0 256 I1 8 I4 16 I5 16 J 64",
    "uint16": "REPK 8 REPW 8 REPD 8 RT 4 RC 16 RP 8 RG 16 REPA 16 PIN 2048 PS 1024",
    "float32": "MVF 512 IDF 128 IDD 256 MK1 128 MK2 64 SELN 576 CL 128 COL 32 P0F 256 GOON 256 ANEW 144 I7 8",
}
OWN = {
    "bfloat16": "TX 5120 T0 640 D 2048 AB 2048 OA 256 OB 1024 FB 32 OH 128 NE 144 NN 144 XR 128",
    "uint16": "TL 16 CU 128 XL 8",
    "float32": "Y 256 BS 16 C 128 KS 128 PR 256 TO 256 RR 64 G 256 G2 256 GT 256 Z 128 RUN 144 WS 144 TK 8 V1 8 DL 8 VM 128 UP 128 PN 160 "
               "PT 256 YC 128 YP 256",
}
SIDE = {}
for _t, _k in ((SHARED, 1), (OWN, 2)):
    for _d, _l in _t.items():
        _w = _l.split()
        for _n, _c in zip(_w[::2], _w[1::2]):
            SCRATCH[_n] = ("sbuf", [128, _k * int(_c)], _d)
            if _k == 2:
                SIDE[_n + "a"], SIDE[_n + "b"] = (_n, 0, int(_c)), (_n, int(_c), int(_c))
for _n in ("pa", "pb", "ma", "mb", "wa0", "wa1", "wb0", "wb1"):
    SCRATCH[_n] = ("psum", [128, 512], "float32")

SEMAPHORES = ["qv", "qs", "qt", "qg", "ls", "dx0", "dp0", "dpu", "dyx"]
SEMAPHORES += [a + e for a in ("dtx", "dt0", "dyc", "dyp") for e in "ab"]
SEMAPHORES += ["%s%s%d" % (a, e, r) for a in ("a1", "a2", "a3", "fl", "dc") for e in "ab" for r in range(R)]

PARTS = (("s4", "v4", "s4", "v3"), ("s4", "v4", "s4", "v4"))


def rank_program(g, core, T, topo):
    rank = T.rank_of(core)
    if rank is None:
        return
    OP = AluOpType
    AF = ActivationFunctionType
    eng = {"v": g.vector, "s": g.scalar, "t": g.tensor, "g": g, "y": g.sync}
    cnt = {"v": 0, "s": 0, "t": 0, "g": 0}
    known = {e: {} for e in eng}
    acc = {}
    total = {}

    def B(name, lo=0, hi=None, step=1, rows=None):
        if name in SIDE:
            name, at, n = SIDE[name]
            lo, hi = at + lo, at + (n if hi is None else hi)
        if hi is None:
            hi = SCRATCH[name][1][1]
        p0, p1 = rows or (0, 128)
        ap = T[name][p0:p1, lo:hi] if step == 1 else T[name][p0:p1, lo:hi:step]
        return (name, lo, hi, ap, (hi - lo + step - 1) // step, step)

    def psum(name):
        return SCRATCH[name][0] == "psum"

    def short(*specs):
        return all(SCRATCH[b[0]][2] in ("bfloat16", "uint16") for b in specs)

    def meet(a, b):
        return a[1] < b[2] and b[1] < a[2] and not (a[5] == b[5] and (a[1] - b[1]) % a[5])

    def covers(a, b):
        return a[1] <= b[1] and b[2] <= a[2] and (a[5] == 1 or (a[5] == b[5] and (a[1] - b[1]) % a[5] == 0))

    def need(e, reads, writes):
        deps = {}
        for w, specs in ((False, reads), (True, writes)):
            for b in specs:
                for a, pw, pe, tok in acc.get(b[0], ()):
                    if pe == e == "t":
                        hit = False
                    else:
                        hit = (pe != e and psum(b[0])) or ((pw or w) and meet(a, b))
                    if hit and deps.get(tok[0], 0) < tok[1]:
                        deps[tok[0]] = tok[1]
        for sem in sorted(deps):
            if known[e].get(sem, 0) < deps[sem]:
                eng[e].wait_ge(T.sem[sem], deps[sem])
                known[e][sem] = deps[sem]

    def mark(pe, tok, reads, writes):
        for b in writes:
            old = [a for a in acc.get(b[0], ()) if not (covers(b, a[0]) and (a[2] == pe or not psum(b[0])))]
            acc[b[0]] = old + [(b, True, pe, tok)]
        for b in reads:
            old = [a for a in acc.get(b[0], ()) if not (a[2] == pe and not a[1] and covers(b, a[0]))]
            acc[b[0]] = old + [(b, False, pe, tok)]

    calls = []
    second = [0, 0]

    def op(e, reads, writes, fn, kind, cycles, group=None):
        def issue():
            need(e, reads, writes)
            fn().then_inc(T.sem["q" + e], 1)
            cnt[e] += 1
            mark(e, ("q" + e, cnt[e]), reads, writes)
        calls.append((e, reads, writes, issue, kind, cycles, group))

    def dmas(sem, moves, reads, writes, more=0.0):
        def issue():
            for e, out, in_ in moves:
                need(e, reads, writes)
                eng[e].dma_start(out, in_).then_inc(T.sem[sem], 16)
            total[sem] = 16 * len(moves)
            mark("d" + sem, (sem, total[sem]), reads, writes)
        calls.append((moves[0][0], reads, writes, issue, "dma", more, None))

    def remote(transfers, srcs, arrivals, more):
        def issue():
            need("g", srcs, [])
            g.remote_dma_fused(transfers, local_sem=T.sem.ls)
            for sem, n, bufs in arrivals:
                mark("rem", (sem, n), [], bufs)
                total[sem] = n
        calls.append(("g", srcs, [b for a in arrivals for b in a[2]], issue, "remote", more, None))

    def find_order():
        n = len(calls)
        seen, turn_of, after = {}, {}, [set() for _ in calls]
        for i, (e, reads, writes, _, _, _, group) in enumerate(calls):
            for w, specs in ((False, reads), (True, writes)):
                for b in specs:
                    for j, a, pw in seen.get(b[0], ()):
                        same = calls[j][0] == e
                        if j != i and (((w or pw) and meet(a, b)) or (psum(b[0]) and (not same or e == "t"))):
                            if group is None or group is not calls[j][6]:
                                after[j].add(i)
            for w, specs in ((True, writes), (False, reads)):
                for b in specs:
                    name = b[0]
                    old = seen.get(name, [])
                    if psum(name):
                        if turn_of.get(name, (e,))[0] != e:
                            old = old[turn_of[name][1]:]
                            turn_of[name] = (e, len(old))
                        turn_of.setdefault(name, (e, 0))
                    elif w:
                        old = [a for a in old if not covers(b, a[1])]
                    seen[name] = old + [(i, b, w)]

        def times(slow, gather, call, tensor, same, other, far):
            hold, done = [], []
            for e, _, _, _, kind, cycles, _ in calls:
                if kind in ("dma", "remote", "load"):
                    hold.append({"dma": 100.0, "remote": 300.0, "load": 1.0}[kind])
                    done.append(far * (DMA if kind != "remote" else REMOTE) + cycles * (far if kind != "load" else 1.0))
                else:
                    hold.append(slow * {"v": call + 0.83 * max(64.0 - call, cycles), "s": 20.0 + 0.83 * cycles, "g": 130.0 + 1.66 * cycles,
                                        "gather": 60.0 + 0.83 * gather * cycles, "t": 5.0 + tensor * cycles}[kind])
                    done.append(hold[-1] + (60.0 if e == "t" else 0.0))
            gaps = [{j: (hold[i] if calls[i][0] == calls[j][0] == "t" else done[i] + (same if calls[i][0] == "v" else other if calls[i][0] == "s" else 100.0))
                     for j in after[i]} for i in range(n)]
            return hold, done, gaps

        def place(order, hold, nexts, first, fill_gaps=True):
            there, busy = list(first), {e: ([], []) for e in eng}
            for i in order:
                t, (starts, stops) = there[i], busy[calls[i][0]]
                k = len(stops)
                while fill_gaps and k and stops[k - 1] > t:
                    k -= 1
                if not fill_gaps and k:
                    t = max(t, stops[-1])
                while k < len(starts) and starts[k] < t + hold[i]:
                    t = max(t, stops[k])
                    k += 1
                starts.insert(k, t)
                stops.insert(k, t + hold[i])
                there[i] = t
                for j, gap in nexts[i].items():
                    there[j] = max(there[j], t + gap)
            return there

        sets = [times(*a) for a in TIMES]
        backwards = []
        for hold, done, gaps in sets:
            backwards.append([{} for _ in calls])
            for i in range(n):
                for j, gap in gaps[i].items():
                    backwards[-1][j][i] = gap + hold[j] - hold[i]
        seed = [12345]

        def chance():
            seed[0] = (seed[0] * 1103515245 + 12345) % 2147483648
            return seed[0] / 2147483648.0

        def judge(order):
            ends = []
            for hold, done, gaps in sets:
                there = place(order, hold, gaps, [0.0] * n, False)
                ends.append(max(there[i] + done[i] for i in range(n)))
            return sum(t / a[0] for t, a in zip(ends, TIMES)), ends, order

        best = None
        for attempt in range(TRIES):
            hold, done, gaps = sets[attempt % len(sets)]
            key = [0.0] * n
            if attempt < FRESH:
                lead = LEAD * chance()
                for i in range(n - 1, -1, -1):
                    key[i] = -NOISE * chance() + min([key[j] - t for j, t in gaps[i].items()] + [-done[i]])
                key = [key[i] - (lead if i < second[0] else 0.0) for i in range(n)]
            else:
                there, amp = place(best[2], hold, gaps, [0.0] * n, False), SHAKE * chance()
                for i in best[2]:
                    key[i] = max(key[i], there[i] + amp * (chance() - 0.5))
                    for j in gaps[i]:
                        key[j] = max(key[j], key[i] + 0.001)
            order = sorted(range(n), key=lambda i: (key[i], i))
            for _ in range(PASSES):
                there = place(order, hold, gaps, [0.0] * n)
                found = judge(sorted(range(n), key=lambda i: (there[i], i)))
                if best is None or found[0] < best[0]:
                    best = found
                back = place(sorted(range(n), key=lambda i: (-there[i] - hold[i], -i)), hold, backwards[attempt % len(sets)],
                             [done[i] - hold[i] for i in range(n)])
                order = sorted(range(n), key=lambda i: (-back[i] - hold[i], i))
        return best[1:]

    def tt(out, a, b, o):
        op("v", [a, b], [out], lambda: g.vector.tensor_tensor(out[3], a[3], b[3], o), "v", out[4] * (1.0 if psum(a[0]) or psum(b[0]) else 2.0))

    def ts(out, a, s1, o1, s2=None, o2=None):
        reads = [a] + [s for s in (s1, s2) if isinstance(s, tuple)]
        x, y = (s[3] if isinstance(s, tuple) else s for s in (s1, s2))
        cycles = out[4] * (0.5 if short(out, a) else 1.0)
        if o2 is None:
            op("v", reads, [out], lambda: g.vector.tensor_scalar(out[3], a[3], x, None, o1), "v", cycles)
        else:
            op("v", reads, [out], lambda: g.vector.tensor_scalar(out[3], a[3], x, y, o1, o2), "v", cycles)

    def cp(out, a):
        op("v", [a], [out], lambda: g.vector.tensor_copy(out[3], a[3]), "v", out[4])

    def scan(out, a, b, o1, o2):
        op("v", [a, b], [out], lambda: g.vector.tensor_tensor_scan(out[3], a[3], b[3], 0.0, o1, o2), "v", out[4] * (0.5 if short(out, a, b) else 1.0))

    def gat(out, win, lst, b=None, o=None):
        if b is None:
            op("v", [win, lst], [out], lambda: g.vector.tensor_copy(out[3], win[3].indirect(lst[3])), "gather", out[4])
        elif isinstance(b, tuple):
            op("v", [win, lst, b], [out], lambda: g.vector.tensor_tensor(out[3], win[3].indirect(lst[3]), b[3], o), "gather", out[4])
        else:
            op("v", [win, lst], [out], lambda: g.vector.tensor_scalar(out[3], win[3].indirect(lst[3]), b, None, o), "gather", out[4])

    def turn(out, a):
        op("v", [a], [out], lambda: g.vector.transpose(out[3], a[3]), "v", out[4])

    def fill(out, value):
        op("v", [], [out], lambda: g.vector.memset(out[3], value), "v", out[4])

    def act(out, a, f, scale=1.0, bias=0.0):
        column = isinstance(bias, tuple)
        x = bias[3] if column else bias
        op("s", [a, bias] if column else [a], [out], lambda: g.scalar.activation(out[3], a[3], f, bias=x, scale=scale), "s", out[4])

    def sgat(out, win, lst):
        op("s", [win, lst], [out], lambda: g.scalar.activation(out[3], win[3].indirect(lst[3]), AF.Copy), "gather", out[4])

    def mm(out, lhsT, rhs, start=False, stop=False, group=None):
        def fn():
            if group:
                group[0] -= 1
            return g.tensor.matmul(out[3], lhsT[3], rhs[3], start, stop or (group is not None and group[0] == 0))
        if group:
            group[0] += 1
        elif group is not None:
            group.append(1)
        op("t", [lhsT, rhs], [out], fn, "t", max(min(64, lhsT[4]), out[4]) * (1.0 if short(rhs) else 4.0), group)

    def iota(name, pattern, base, cm, hi=None):
        out = B(name, 0, hi)
        if SCRATCH[name][2] == "int32":
            op("g", [], [out], lambda: g.iota(out[3], pattern, base, cm), "g", out[4])
        else:
            op("g", [], [out], lambda: g.iota(out[3], pattern, base, cm, allow_small_or_imprecise_dtypes=True), "g", out[4])

    def MV(kind, u, w):
        return B(kind, 128 * (2 * u + w), 128 * (2 * u + w) + 128)

    dmas("dp0", [("y", T.P0[:, :], T.p0[:, :])], [], [B("P0")])
    dmas("dx0", [("s", T.X0[:, :], T.x0[:, :])], [], [B("X0")])
    for par, e in enumerate("ab"):
        dmas("dtx" + e, [("ys"[h], T.TX[32 * a + 16 * h:32 * a + 16 * h + 16, 5120 * par:5120 * par + 4096],
                          T.tx[32 * a + 16 * par:32 * a + 16 * par + 16, :]) for a in range(4) for h in range(2)],
             [], [B("TX" + e, 0, 4096)], MIB * (par + 1))
    for par, e in enumerate("ab"):
        dmas("dt0" + e, [("s", B("T0" + e, 0, 128)[3], T.tx[16 * par:128:32, :])], [], [B("T0" + e, 0, 128)], MIB * 2)
    dmas("dpu", [("y", T.PUW[:, :], T.pu[:, :])], [], [B("PUW")], MIB * 4)
    for i, c in enumerate(calls):
        c[3]()
        calls[i] = c[:3] + (lambda: None, "load") + c[5:]

    iota("I1", [[0, 8]], 0, 1)
    iota("IO", [[1, 320]], -192, 0)
    iota("DD", [[16, 8], [0, 2], [1, 16]], 0, 0)
    iota("I7", [[1, 8]], 0, 0)
    iota("S16", [[0, 16], [1, 16]], 0, 0)
    iota("G8", [[0, 4], [1, 8]], 0, 0)
    iota("C8", [[0, 4], [1, 8], [0, 2]], 0, 0)
    iota("S17", [[0, 8], [1, 17]], 0, 0, 136)
    iota("I4", [[16, 2], [32, 8]], 0, 0)
    count = B("IO", 192, 320)

    def col(j):
        return B("COL", j, j + 1)

    def J(j):
        return B("J", 8 * j, 8 * j + 1)

    for j, (value, o) in enumerate(((16, OP.bitwise_and), (15, OP.bitwise_and), (1, OP.bitwise_and), (7, OP.bitwise_and),
                                    (8, OP.bitwise_and), (4, OP.logical_shift_right), (5, OP.logical_shift_right))):
        ts(J(j), B("I1", 0, 1), value, o)
    cp(col(0), B("I1", 0, 1))
    cp(col(1), J(1))
    cp(col(2), J(5))
    for u in range(2):
        ts(col(3 + u), J(0), 16.0 * u, OP.not_equal, 1000.0, OP.mult)
        for w in range(2):
            ts(col(5 + 2 * u + w), col(3 + u), col(0), OP.add, 16.0 * (w - u), OP.add)
            ts(MV("MVB", u, w), count, col(5 + 2 * u + w), OP.is_equal)
            act(MV("MVF", u, w), MV("MVB", u, w), AF.Copy)
    ts(B("IDM"), count, col(0), OP.is_equal)
    for name, value in (("IDF", 1.0), ("NID", -1.0), ("IDB", BIG), ("NB", -65536.0), ("IDP", 128.0), ("NIP", -128.0), ("PEN", TOP / DROP)):
        act(B(name), B("IDM"), AF.Copy, scale=value)
    ts(B("IDD"), B("DD"), col(0), OP.is_equal)
    act(B("IDL"), B("IDD"), AF.Copy)
    act(B("IDH"), B("IDD"), AF.Copy, scale=128.0)
    ts(col(9), J(2), -2.0, OP.mult, 1.0, OP.add)
    ts(B("PDH"), count, col(9), OP.subtract, col(0), OP.is_equal)
    tt(B("PDL"), B("IDM"), B("PDH"), OP.subtract)
    act(B("PDH"), B("PDL"), AF.Copy, scale=128.0)
    ts(B("WA"), B("G8"), col(2), OP.is_equal, 2.0 * KAP, OP.mult)
    ts(B("WD"), B("G8"), col(2), OP.is_equal, -KAP, OP.mult)
    ts(B("MK1"), B("S16", 0, 128), col(1), OP.is_equal)
    ts(B("MK2"), B("C8"), col(2), OP.is_equal)
    act(B("GOON"), B("S16"), AF.Sign)
    act(B("CK"), B("S16"), AF.Identity, scale=-256.0, bias=3840.0)
    fill(B("CK", 0, 256, 16), -1073741824.0)
    fill(B("CK", 15, 128, 16), float(TOP))
    act(B("CL"), B("S16", 0, 128), AF.Identity, scale=-256.0, bias=TOP + 3840.0)
    ts(B("LIM"), B("S16", 0, 144), 0.0, OP.is_equal, -DROP, OP.mult)
    ts(B("IND", 0, 136), B("S17", 0, 136), 0.0, OP.is_equal)
    act(B("ANEW", 0, 136), B("IND", 0, 136), AF.Copy, scale=1073741824.0)
    act(B("CE", 0, 136), B("S17", 0, 136), AF.Identity, scale=16.0, bias=3776.0)
    fill(B("CE", 0, 136, 17), 0.0)
    for r in range(R):
        act(B("CN", 144 * r, 144 * r + 136), B("IND", 0, 136), AF.Identity, scale=4096.0 + 256.0 * r, bias=OFF + BIG)
    act(B("NEG"), count, AF.Identity, scale=0.0, bias=-1.0)
    cp(B("PC"), B("I1"))
    ts(col(10), J(6), 34.0, OP.mult, col(1), OP.add)
    for u in range(2):
        for a in range(2):
            j = 2 * u + a
            ts(col(11 + j), col(10), col(3 + u), OP.add, 17.0 * a - 7.0, OP.add)
            ts(B("SELN", 144 * j, 144 * j + 136), B("IO", 184, 320), col(11 + j), OP.is_equal)
    ts(B("REPK"), B("I7"), 16.0, OP.mult, 15.0, OP.add)
    ts(B("REPW"), B("I7"), 17.0, OP.mult, 16.0, OP.add)
    cp(B("REPD"), B("I7"))
    ts(col(15), J(2), 16.0, OP.mult, 15.0, OP.add)
    ts(B("RT"), B("I7", 0, 4), 32.0, OP.mult, col(15), OP.add)
    ts(col(16), J(4), 0.125, OP.mult)
    ts(col(17), J(3), 32.0, OP.mult, col(16), OP.add)
    ts(col(18), col(17), 16.0, OP.add)
    ts(col(19), J(0), col(17), OP.add)
    for out, c in ((B("RC", 0, 8), 17), (B("RC", 8, 16), 18), (B("RP"), 19)):
        ts(out, B("I7"), 2.0, OP.mult, col(c), OP.add)
    ts(B("RG"), B("I4"), col(1), OP.add)
    cp(B("P0F"), B("P0"))

    others = [q for q in range(R) if q != rank]
    nxt, prv = T.cores[(rank + 1) % R], T.cores[(rank - 1) % R]
    sent = [0]

    def stream(par, r):
        e = "ab"[par]
        o = 128 * (2 * r + par)
        p, m, w, w1 = "p" + e, "m" + e, "w%s0" % e, "w%s1" % e
        told, tnew = B("T0" + e, 128 * r, 128 * r + 128), B("T0" + e, 128 * r + 128, 128 * r + 256)
        fs, tx = B("FS", o, o + 128), B("TX" + e, 0, 4096)
        at = 4096 + 256 * r
        pre = 400 * (2 * r + par)
        pn = B("PN" + e, 16, 144)

        def S(name, a=0, b=None, step=1):
            return B(name + e, a, b, step)

        def ends(name, a, b, n=16):
            return S(name, a + n - 1, b, n)

        def names(out, high, low, start=False, stop=False):
            mm(out, B("IDP"), high, start)
            mm(out, B("IDM"), low, False, stop)

        def listed(out, parts):
            for j, (part, ident) in enumerate(parts):
                mm(B(w, 0, 256), part, B(ident), j == 0, j + 1 == len(parts))
            turn(S("PT"), B(w, 0, 256))
            gat(out, S("PT"), B("RP"), -OFF, OP.add)

        def prepare(buf, j):
            high, low = B(buf, j, j + 128), B(buf, j + 128, j + 256)
            act(high, pn, AF.Identity, scale=1.0 / 128.0, bias=-0.498)
            mm(B(w1, 0, 128), B("IDF"), pn, True)
            mm(B(w1, 0, 128), B("NIP"), high, False, True)
            act(low, B(w1, 0, 128), AF.Copy)
            mm(B(w1, 128, 256), B("PDH"), high, True)
            mm(B(w1, 128, 256), B("PDL"), low, False, True)
            act(S("NE", 1, 129), B(w1, 128, 256), AF.Abs, scale=DROP)
            scan(B(buf, j + 256, j + 385), S("NE", 0, 129), B("LIM", 0, 129), OP.add, OP.min)

        def distances(lst, l0, row, parts, banks, keys, width, group):
            turns = 0
            for part in parts:
                n = int(part[1:])
                a, b = 128 * row, 128 * (row + n)
                if part[0] in "vm":
                    for j in range(0, n, 2):
                        k = min(2, n - j)
                        gat(S("D", a + 128 * j, a + 128 * (j + k)), tx, B(lst, l0 + 8 * (row + j), l0 + 8 * (row + j + k)),
                            S("TX", at, at + 128 * k), OP.subtract)
                    if part[0] == "v":
                        ts(S("AB", a, b), S("D", a, b), 0.0, OP.max)
                    else:
                        act(S("AB", a, b), S("D", a, b), AF.Abs, scale=0.5)
                else:
                    bank = banks[turns % len(banks)]
                    turns += 1
                    (sgat if part[0] == "s" else gat)(S("D", a, b), tx, B(lst, l0 + 8 * row, l0 + 8 * (row + n)))
                    for j in range(0, n, 2):
                        k = 128 * min(2, n - j)
                        mm(B(bank, 128 * j, 128 * j + k), B("NID"), S("TX", at, at + k), j == 0)
                    mm(B(bank, 0, 128 * n), B("IDM"), S("D", a, b), False, True)
                    act(S("AB", a, b), B(bank, 0, 128 * n), AF.Abs, scale=0.5)
                for k in range(row, row + n):
                    if part[0] == "v":
                        mm(keys(k), S("D", 128 * k, 128 * k + 128), B("WD", 0, width), group=group)
                    mm(keys(k), S("AB", 128 * k, 128 * k + 128), B("WA", 0, width), group=group)
                row += n

        if r == 0:
            fill(S("NE", 0, 1), 0.0)
            for a in range(2):
                mm(B(w, 0, 128), B("P0F", 128 * a, 128 * a + 128), MV("MVF", par, a), a == 0, a == 1)
            act(pn, B(w, 0, 128), AF.Identity, bias=OFF)
            fill(S("PN", 144 - 144 * par, 160 - 144 * par), 0.0)
            for j in range(4):
                mm(B(m, 128 * (j // 2), 128 * (j // 2) + 128), MV("MVB", par, j % 2), B("X0", 128 * (j % 2), 128 * (j % 2) + 128), j == 0, j == 3)
            act(S("TX", at, at + 256), B(m, 0, 256), AF.Copy)
            listed(B("PS", 512 * par, 512 * par + 128), [(pn, "IDD")])
            prepare("PRE", pre)
        high, low = B("PRE", pre, pre + 128), B("PRE", pre + 128, pre + 256)

        sums = []
        mm(B(p, 0, 256), B("IDM"), B("CK"), True)
        mm(B(p, 0, 256), B("IDM"), B("PRE", pre, pre + 256), group=sums)
        mm(B(p, 0, 128), B("PEN"), B("PRE", pre + 257, pre + 385), group=sums)
        mm(B(p, 256, 384), B("IDP"), high, group=sums)
        mm(B(p, 256, 384), B("IDM"), low, group=sums)
        lst, l0 = ("PS", 512 * par) if r == 0 else ("PIN", 2 * o + 128)
        distances(lst, l0, 1, PARTS[0], (w, w1, m), lambda k: B(p, k, 256, 16), 16, sums)
        for j in range(2):
            scan(S("Y", 128 * j, 128 * j + 128), B("PRE", pre + 256, pre + 384), B(p, 128 * j, 128 * j + 128), OP.add, OP.max)
        ts(S("BS"), ends("Y", 0, 256), ROUND, OP.add, -ROUND, OP.add)
        tt(S("FB", 0, 16), ends("Y", 0, 256), S("BS"), OP.subtract)
        if r > 0:
            act(S("FB", 16, 24), ends("Y", 0, 128), AF.Relu, scale=-1.0, bias=float(TOP))
        for c in range(8):
            ts(S("OA", 32 * c, 32 * c + 32), B("IO", 96, 128), S("FB", c, c + 1), OP.is_equal)
            ts(S("OB", 128 * c, 128 * c + 128), count, S("FB", 8 + c, 9 + c), OP.is_equal, S("FB", 16 + c, 17 + c) if r else 1.0, OP.mult)
            mm(B(w, 0, 128, 1, (32 * (c // 2), 32 * (c // 2) + 32)), S("OA", 32 * c, 32 * c + 32), S("OB", 128 * c, 128 * c + 128),
               c % 2 == 0, c % 2 == 1)
        act(fs, B(w, 0, 128), AF.Sign)
        dsts, ids = [], []
        for q in others:
            j = 3 * o + 128 * ((rank - q - 1) % R)
            rid, pid = topo.addr(T.cores[q])[:2]
            ids.append(DstId(rid=rid, pnc=pid))
            dsts.append(T.FR[:, j:j + 128])
        fl = "fl%s%d" % (e, r)
        remote([RemoteDMATransfer(dst_ids=ids, dma_engine_mask=topo.mask(core, T.cores[others[0]]), remote_sem=T.sem[fl], srcs=[fs[3]],
                                  dsts=dsts)], [fs],
               [(fl, sum(len(topo.engines(T.cores[q], core)) for q in others), [B("FR", 3 * o, 3 * o + 384)])], 700.0)
        sent[0] += len(topo.engines(core, T.cores[others[0]]))
        for i, mp in enumerate([B("NEG"), fs] + [B("FR", 3 * o + 128 * j, 3 * o + 128 * j + 128) for j in range(3)]):
            mm(B(w1, 0, 128), B("IDB"), mp, i == 0, i == 4)
        tt(tnew, B(w1, 0, 128), told, OP.max)
        dmas("dc%s%d" % (e, r), [("y", T.TX[16 * h:128:32, 5120 * par:5120 * par + 4096], tnew[3]) for h in range(2)], [tnew], [tx], 350.0)
        if r == 0:
            act(S("C"), B(p, 0, 128), AF.Copy)
        else:
            tt(S("C"), B(p, 0, 128), B("CL"), OP.min)
        scan(S("KS"), B("GOON", 0, 128), S("C"), OP.mult, OP.max)
        gat(S("OH"), S("KS"), B("REPK"), S("C"), OP.is_equal)
        names(B(p, 1, 128), B("PRE", pre, pre + 127), B("PRE", pre + 128, pre + 255), True)
        names(B(p, 128, 256), high, low)
        mm(B(p, 1, 128), B("IDB"), S("OH", 1, 128))
        mm(B(p, 128, 256), B("IDB"), S("OH"), False, True)
        scan(S("TO"), B("GOON"), B(p, 0, 256), OP.mult, OP.max)
        gat(S("RR"), S("TO"), B("RT"), B("MK2"), OP.mult)
        for a in range(4):
            mm(B(p, 384, 400, 1, (32 * a, 32 * a + 32)), B("MK1", 0, 32), S("RR", 16 * a, 16 * a + 16), True, True)
        ts(S("TL"), B(p, 384, 400), -OFF - BIG, OP.add)
        sgat(S("G"), B("PUW"), S("TL"))
        turn(S("GT"), S("G"))
        gat(S("CU"), S("GT"), B("RC", 8 * par, 8 * par + 8))
        sgat(S("G2"), S("G"), B("RG"))
        mm(B(p, 0, 136), B("IDM"), B("CN", 144 * r, 144 * r + 136), True)
        mm(B(p, 0, 136, 17), B("IDM"), B("PC"))
        for a in range(2):
            mm(B(p, 0, 136), S("G2", 128 * a, 128 * a + 128), B("SELN", 144 * (2 * par + a), 144 * (2 * par + a) + 136))
        act(S("Z"), S("TX", at, at + 128), AF.Identity, bias=255.75)
        sums = []
        mm(B(m, 0, 136), B("IDM"), B("CE", 0, 136), True)
        mm(B(m, 0, 136, 17), B("IDF"), ends("KS", 0, 128), group=sums)
        distances("CU" + e, 0, 0, PARTS[1], (w, w1), lambda k: B(m, 1 + k, 136, 17), 8, sums)
        scan(S("RUN", 0, 136), B("ANEW", 0, 136), B(m, 0, 136), OP.max, OP.min)
        tt(S("NN", 0, 136), B(m, 0, 136), S("RUN", 0, 136), OP.not_equal)
        tt(S("TK"), ends("RUN", 0, 136, 17), ends("KS", 0, 128), OP.is_lt)
        mm(B(p, 0, 136), B("NB"), S("NN", 0, 136), False, True)
        scan(S("WS", 0, 136), S("NN", 0, 136), B(p, 0, 136), OP.mult, OP.max)
        gat(S("VM"), S("WS", 0, 136), B("REPW"), B("MK1"), OP.mult)
        mm(B(m, 0, 8), S("VM"), B("MK2", 0, 16, 2), True, True)
        ts(S("XL"), B(m, 0, 8), -OFF - BIG, OP.add)
        gat(S("XR"), S("TX", 0, at + 128), S("XL"), S("Z"), OP.add)
        tt(S("V1"), ends("WS", 0, 136, 17), ends("TO", 128, 256), OP.subtract)
        tt(S("DL"), S("V1"), S("TK"), OP.mult)
        gat(S("UP"), S("DL"), B("REPD"), S("OH"), OP.mult)
        tt(pn, B(p, 256, 384), S("UP"), OP.add)
        if r == R - 1:
            ts(S("YC"), tnew, 1000.0, OP.is_ge)
            dmas("dyc" + e, [("y", T.yc[par:8:2, :], S("YC")[3])], [S("YC")], [])
            for a in range(2):
                j = 16 + 16 * (a - par)
                mm(B(w, 128 * a, 128 * a + 128), S("PN", j, j + 128), B("IDF"), a == 0, a == 1)
            act(S("YP"), B(w, 0, 256), AF.Identity, bias=-OFF)
            dmas("dyp" + e, [("ys"[c % 2], T.yp[32 * c + 16 * par:32 * c + 16 * par + 16, :],
                              T.YP[32 * c + 16 * par:32 * c + 16 * par + 16, 256 * par:256 * par + 256]) for c in range(4)], [S("YP")], [])
            return
        xs = B("XS", 2 * o, 2 * o + 256)
        ts(B("XS", 2 * o, 2 * o + 128), S("XR"), 0.5, OP.mult, -128.0, OP.add)
        act(B("XS", 2 * o + 128, 2 * o + 256), S("XR"), AF.Identity, scale=0.5, bias=-128.0)
        j = 512 * par + 128 * r
        listed(B("PS", j + 128, j + 256), [(high, "IDH"), (low, "IDL"), (S("UP"), "IDD")])
        rid, pid = topo.addr(nxt)[:2]
        eg, got = topo.engines(core, nxt), len(topo.engines(prv, core)) // 2
        n = len(eg) // 2
        moves = [("a1%s%d" % (e, r + 1), xs, S("TX", at + 256, at + 512)),
                 ("a2%s%d" % (e, r + 1), B("PS", j, j + 256), B("PIN", 2 * o + 512, 2 * o + 768))]
        remote([RemoteDMATransfer(dst_ids=[DstId(rid=rid, pnc=pid)], dma_engine_mask=sum(1 << x for x in eg[n * j:n * j + n]),
                                  remote_sem=T.sem[sem], src=src[3], dst=dst[3]) for j, (sem, src, dst) in enumerate(moves)],
               [src for _, src, _ in moves], [(sem, got, [dst]) for sem, _, dst in moves], 600.0)
        prepare("PRS", pre)
        out, land, a3 = B("PRS", pre, pre + 385), B("PRE", pre + 800, pre + 1185), "a3%s%d" % (e, r + 1)
        remote([RemoteDMATransfer(dst_ids=[DstId(rid=rid, pnc=pid)], dma_engine_mask=topo.mask(core, nxt), remote_sem=T.sem[a3],
                                  src=out[3], dst=land[3])], [out], [(a3, 2 * got, [land])], 400.0)
        sent[0] += 2 * len(eg)

    for par in range(2):
        second[0] = len(calls)
        for r in range(R):
            stream(par, r)
    for j in range(4):
        mm(B("wa1", 128 * (j % 2), 128 * (j % 2) + 128), MV("MVB", j % 2, j // 2), B("XR" + "ab"[j // 2]), j == 0, j == 3)
    act(B("X0"), B("wa1", 0, 256), AF.Identity, scale=0.5, bias=-128.0)
    dmas("dyx", [("s", T.yx[:, :], T.X0[:, :])], [B("X0")], [])
    if "order" not in ORDER:
        ORDER["order"] = find_order()
    for i in ORDER["order"][1]:
        calls[i][3]()
    g.wait_ge(T.sem.ls, sent[0])
    for e in "vstg":
        g.wait_ge(T.sem["q" + e], cnt[e])
    for s in sorted(total):
        g.wait_ge(T.sem[s], total[s])
